import numpy as np, ml_dtypes
CORES = [2,6,10,14,18,22,26,30]
N = 8
import mx_ref
BF = ml_dtypes.bfloat16
def gcols(t, e):
    v = np.concatenate([t.reshape(8, 16, -1, 4), np.zeros((8, 16, 1, 4), BF)], axis=2)
    return np.ascontiguousarray(np.stack([v[g][:, e[g]] for g in range(8)])).reshape(128, -1)
def gpick(z, e):
    return np.concatenate([z[16 * g:16 * g + 16][:, e[g]] for g in range(8)])
def tile(rs):
    return np.stack(rs, axis=2).reshape(128, -1).astype(BF)
def pick(q, e):
    c = np.concatenate([q[0].reshape(128, -1, 4), np.zeros((128, 1, 4), np.uint8)], axis=1); s = np.concatenate([q[1], np.ones((16, 1), np.uint8)], axis=1)
    return (np.ascontiguousarray(c[:, e].reshape(128, -1)), np.ascontiguousarray(s[:, e]))
def join(*qs):
    return (np.concatenate([q[0] for q in qs], axis=1), np.concatenate([q[1] for q in qs], axis=1))
def put(q, e, v):
    c, s = q[0].reshape(128, -1, 4).copy(), q[1].copy(); c[:, e] = v[0].reshape(128, -1, 4); s[:, e] = v[1]
    return (c.reshape(128, -1), s)
def pk(c, s):
    return (np.ascontiguousarray(c), mx_ref.live(s))
def emit(q):
    return q[0], q[1]
def packed(v, rng):
    q = [mx_ref.quantize(np.ascontiguousarray(v[r])) for r in range(N)]
    return np.stack([a for a, b in q]), np.stack([mx_ref.plane(b, rng) for a, b in q])
def values_of_codes():
    e, c = np.zeros((128, 128, 4), np.float32), np.zeros((128, 2, 4), np.uint8)
    e[np.arange(128), np.arange(128), 0] = 1
    c[:127, :, 0] = np.arange(256).reshape(2, 128).T[:127]
    return mx_ref.matmul(mx_ref.quantize(e.reshape(128, 512).astype(BF)), (c.reshape(128, 8), np.full((16, 2), 127, np.uint8))).T.reshape(-1).astype(np.float64)
CODE_VALUE, SCALE_VALUE = values_of_codes(), 2.0 ** (np.arange(256) - 127.0)
def decode(q):
    return (CODE_VALUE[q[0]].reshape(16, 8, -1, 4) * SCALE_VALUE[q[1]][:, None, :, None] + 0.0).reshape(128, -1).astype(np.float32)
def f(rng, *shape):
    return mx_ref.flush((rng.standard_normal(shape, dtype=np.float32) * np.exp2(rng.integers(-2, 3, shape[:-1] + (1,)))).astype(BF))
def wide(rng, *shape, cols=0):
    v = rng.standard_normal(shape, dtype=np.float32) * np.exp2(rng.integers(-12, 13, shape)).astype(np.float32)
    if cols: v *= np.repeat(np.exp2(rng.integers(-cols, cols + 1, shape[:-2] + (1, shape[-1] // 4))) * (rng.random(shape[:-2] + (1, shape[-1] // 4)) > 0.0625), 4, axis=-1).astype(np.float32)
    return mx_ref.flush(v.astype(BF))
C, R = 256, 3
PARTNER = [1, 2, 4]
def fork(m, p):
    base = m + np.maximum(-p[1::16], np.float32(0.0))
    s = p[::16]
    cost = np.stack([base + np.maximum(-s, np.float32(0.0)), base + np.maximum(s, np.float32(0.0))], axis=2).reshape(8, 2 * C) + np.float32(0.0)
    k = np.sort(np.argsort(cost, axis=1, kind="stable")[:, :C], axis=1)
    return k, np.take_along_axis(cost, k, axis=1)
def big(v, k):
    v = v.astype(np.float32) * np.float32(k)
    v[np.abs(v) < np.float32(2.0 ** -16)] = 0
    return v.astype(BF)
def weights(rng, k, still=slice(0)):
    w = big(f(rng, N, 128, 2048), k).reshape(N, 128, 4, 8, 16, 4)
    w[:, :, :, :, still] = 0
    c, p = packed(w.reshape(N, 128, 2048), rng)
    return {"wc": c, "ws": p}
def numbers_of(rng):
    return {"x": big(f(rng, N, 128, 4 * C), 1), "u": np.array(f(rng, N, 128, 512)), "v": np.array(f(rng, N, 128, 512))}
def planted(rng, unit, d, s):
    o = numbers_of(rng)
    x = o["x"].astype(np.float32).reshape(N, 8, 16, C, 4)
    digits = ((d[..., None] >> np.arange(8)) & 1) * 2.0 ** np.arange(8) * unit
    x[:, :, 0] = 0
    x[:, :, 0, :, 0] = -1
    x[:, :, 8] = digits[..., :4]
    x[:, :, 9] = digits[..., 4:]
    x[:, :, 10] = 0
    x[:, :, 10, :, 0] = s
    x[:, :, 11:] = rng.integers(4, 8, (N, 8, 5, C, 4)) * rng.choice([-1.0, 1.0], (N, 8, 5, C, 4)) * (8 * unit)
    u = o["u"].reshape(N, 128, 128, 4)
    u[:, :, ::16] = 0
    u[:, :, 1::16] = 0
    for h in range(0, 128, 16):
        u[:, h + 10, h, 0] = 1
        u[:, h, h + 1, 0] = 1
        u[:, h + 8:h + 10, h + 1] = -1
    return {"x": x.reshape(N, 128, 4 * C).astype(BF), "u": u.reshape(N, 128, 512), "v": o["v"], **weights(rng, 0.25, [0] + [8 + i for i in range(8)])}
def setup_inputs(rng):
    return {**numbers_of(rng), **weights(rng, 1)}
def setup_inputs_ties(rng):
    d = numbers_of(rng)
    e = rng.permutation(N)
    x = d["x"].reshape(N, 8, 16, C, 4)
    for r in range(N):
        k = np.asarray([0, 0, 1, 1, 1, 1, 2])[rng.permutation(C) % 7]
        a = x[r][:, :8, :3].copy()
        a[:, :, 2] = 0
        if r == e[0]: a[:] = 0
        x[r][:, :8] = a[:, :, k]
    x[e[1]] = 0
    u = d["u"].reshape(N, 8, 16, 128, 4)
    u[:, :, 8:, ::16] = 0
    u[:, :, 8:, 1::16] = 0
    g, j = rng.integers(8), rng.integers(C >> R)
    u[e[0], g, :8, 16 * g] = u[e[0], g, :8, 16 * g + 1]
    x[e[0], g, :8, j] = big(u[e[0], g, :8, 16 * g], 1)
    return {"x": x.reshape(N, 128, 4 * C), "u": u.reshape(N, 128, 512), "v": d["v"], **weights(rng, 1, slice(8))}
def setup_inputs_near(rng):
    d = np.argsort(rng.random((N, 8, C)), axis=2) // 2
    q = np.stack([rng.permutation(8) for r in range(N)])
    d[q % 4 == 0] = (np.arange(C) // 2 + C // 4 + 1) % (C // 2)
    o = planted(rng, 2.0 ** -23, d, rng.choice([-1.0, 1.0], (N, 8, C)) * 2.0 ** -23)
    x = o["x"].reshape(N, 8, 16, C, 4)
    for r in range(N):
        for g in range(8):
            if q[r, g] % 2: x[r, g, 0, np.argmax(d[r, g]), 0] = -2.0 ** 30
            if q[r, g] % 4 == 0:
                j = np.argmin(d[r, g])
                x[r, g, :8, j] = 0
                x[r, g, 0, j, 0] = -2.0 ** -24
    return {**o, "x": x.reshape(N, 128, 4 * C)}
def setup_inputs_ends(rng):
    once = np.stack([rng.permutation(8) % 2 for r in range(N)])[:, :, None] == 1
    d = np.where(once, rng.integers(0, 16, (N, 8, C)), (C - 1 - np.arange(C)) // 2)
    s = np.where(once, 4.0, 2.0 ** -9) * rng.choice([-1.0, 1.0], (N, 8, C))
    return planted(rng, 2.0 ** -6, d, s)
def setup_inputs_huge(rng):
    d = numbers_of(rng)
    low = np.where(rng.permutation(N) < N // 2, 0.25, 0.45)[:, None]
    c = low + (0.7 - low) * rng.random((N, C))
    x = 2.0 ** 30 * c[:, None, :, None] * (0.9 + 0.1 * rng.random((N, 128, C, 4)))
    u = d["u"].reshape(N, 128, 128, 4)
    a = 2.0 ** 30 * (1 - 0.25 * rng.random((2, N, 128, 8, 4)))
    u[:, :, ::16] = (a[0] * rng.choice([-1.0, 1.0], a[0].shape)).astype(np.float32).astype(BF)
    u[:, :, 1::16] = (-a[1]).astype(np.float32).astype(BF)
    return {"x": x.astype(np.float32).reshape(N, 128, 4 * C).astype(BF), "u": u.reshape(N, 128, 512), "v": d["v"], **weights(rng, 2.0 ** -8)}
def setup_inputs_spread(rng):
    d = setup_inputs(rng)
    d["x"] = big(wide(rng, N, 128, 4 * C, cols=6), 1)
    return d
def check_inputs(d):
    b = []
    for k in ("x", "u", "v"):
        a = np.abs(d[k].astype(np.float32))
        if not (np.isfinite(a).all() and ((a == 0) | (a >= 2.0 ** -30) & (a <= 2.0 ** 30)).all()): b.append("a value of " + k)
    return b
def reference(x, u, v, wc, ws):
    qu = [mx_ref.quantize(u[r]) for r in range(N)]
    lay = [[pick(pk(wc[r], ws[r]), np.arange(128 * b, 128 * b + 128)) for b in range(4)] for r in range(N)]
    now = [x[r] for r in range(N)]
    m = np.zeros((N, 8, C), np.float32)
    for t in range(R):
        k, z, sent = [], [], []
        for r in range(N):
            q = mx_ref.quantize(now[r])
            e, m[r] = fork(m[r], mx_ref.matmul(qu[r], q))
            k.append(e)
            z.append(gcols(decode(q).astype(BF), e // 2))
            sent.append(mx_ref.quantize(z[r]))
        for r in range(N):
            sign = np.repeat(1 - 2 * (k[r] % 2), 16, axis=0).astype(np.float32)
            h = [gpick(mx_ref.matmul(lay[r][b], sent[r ^ PARTNER[t]]) * np.float32(0.015625), k[r] // 2) for b in range(4)]
            a = z[r].astype(np.float32).reshape(128, C, 4)
            now[r] = tile([a[:, :, b] + sign * h[b] for b in range(4)])
    y, kl = np.zeros((N, 128, C), np.float32), np.zeros((N, 8, C), np.float32)
    oc, osc = np.zeros((N, 128, 4 * C), np.uint8), np.zeros((N, 16, C), np.uint8)
    for r in range(N):
        q = mx_ref.quantize(now[r])
        y[r] = mx_ref.matmul(mx_ref.quantize(v[r]), q)
        kl[r] = k[r]
        oc[r], osc[r] = emit(q)
    return {"y": y, "kl": kl, "ml": m, "oc": oc, "osc": osc}

@@ -1,0 +1,561 @@
+from concourse.mybir import dt, AluOpType, AxisListType, ActivationFunctionType
+
+A = AluOpType
+F = ActivationFunctionType
+C = 256
+CW = 272
+ROUNDS = 3
+PARTNER = [1, 2, 4]
+XS = [96, 96, 96, 96, 96, 96, 0, 0, 96, 0]
+XM = 96
+BIG = 2.0 ** 76
+B1 = 2.0 ** 74
+B2 = 2.0 ** 84
+SM = [0, 1, 2, 3, 13, 14, 15]
+VM = [4, 5, 6, 7, 8, 9, 10, 11, 12]
+
+X4 = "float8_e4m3fn_x4"
+SCRATCH = {}
+POOL = {}
+
+
+def _buf(name, n, dtype, where="sbuf"):
+    SCRATCH[name] = (where, [128, n], dtype)
+
+
+for _t in range(ROUNDS + 1):
+    _w = CW if _t < ROUNDS else C
+    _buf("tt%d" % _t, 4 * _w, "bfloat16")
+    _buf("qt%d" % _t, _w, X4)
+    _buf("st%d" % _t, _w, "uint8")
+for _t in range(ROUNDS):
+    for _n, _c, _d in [("lq", C, X4), ("ls", C, "uint8"), ("la", 16, "uint16"), ("au", 18, "uint16"),
+                       ("dd", 4 * C, "bfloat16"), ("ds", 4 * C, "bfloat16"), ("zz", 4 * CW, "bfloat16"),
+                       ("zs", 4 * C, "bfloat16"), ("qz", C, X4), ("sz", C, "uint8"), ("rw", 8 * C, "float32")]:
+        _buf(_n + str(_t), _c, _d)
+for _d, _l in [
+    ("bfloat16", [("ub", 512), ("vb", 512), ("diag", 512), ("eb", 2048), ("latch", CW), ("junk", 2048),
+                  ("fl", 2 * XM), ("fsc", XM), ("lt", 512), ("le", 512), ("ysg", 512), ("clt", C), ("cle", C),
+                  ("cap", C), ("sb", 512), ("ifl", 136 * len(VM)), ("lob", 512), ("h2", 512), ("hw", CW), ("hl", CW)]),
+    (X4, [("qu", 128), ("qv", 128), ("qus", 128), ("quz", 128), ("qw", 512), ("qe", 512)]),
+    ("uint8", [("su", 128), ("sv", 128), ("sus", 128), ("suz", 128), ("sw", 512), ("se", 512)]),
+    ("uint16", [("offs", 16), ("pku", 16), ("a2u", 18), ("ku", 18)]),
+    ("int32", [("pki", 16)]),
+    ("float32", [("tab", 256), ("tabt", 256), ("c16", 17), ("cvec", 17), ("chalf", 17), ("r16", CW), ("mbig", 32),
+                 ("mown", 32), ("mb1", 32), ("horn", 8), ("i512", 512), ("ptr", 512), ("nzn", 16), ("asn", 16),
+                 ("lon", 16), ("hin", 24), ("mn", 16), ("mw", CW), ("mtr", 512), ("nz", C), ("r0", C), ("r1", C),
+                 ("base", C), ("xc", 512), ("s1", 32), ("s2", 32), ("s3", 32), ("s4", 32), ("s5", 32), ("s6", 32),
+                 ("s7", 32), ("s8", 32), ("s9", 32), ("piv", 10), ("yy", 10), ("acc", 10), ("w7a", 16), ("w7", 16),
+                 ("v2a", 4), ("v2", 4), ("e1", 8), ("e2", 8), ("e3", 8), ("e4", 8), ("fin", 8), ("prep", 192),
+                 ("prt", 192), ("thr", 4), ("isc", 68 * len(VM)), ("iac", 8), ("a2", 17), ("bitn", 17), ("kn", 17),
+                 ("kw", C), ("yo", C)]),
+]:
+    for _n, _c in _l:
+        if _c <= 96 and _d == "float32":
+            POOL[_n] = (sum(-(-_v[1] // 8) * 8 for _v in POOL.values()), _c)
+        else:
+            _buf(_n, _c, _d)
+_buf("pool", sum(-(-_v[1] // 8) * 8 for _v in POOL.values()), "float32")
+_buf("ps", 4096, "float32", "psum")
+
+SEMAPHORES = ["cv", "cs", "ct", "cg", "loc"] + ["d%d" % _i for _i in range(16)] \
+    + [_n + str(_i) for _n in ("aq", "al", "am") for _i in range(ROUNDS)]
+
+
+def rank_program(g, core, T, topo):
+    rank = T.rank_of(core)
+    if rank is None:
+        return
+    Q = {"v": g.vector, "s": g.scalar, "t": g.tensor, "g": g, "y": g.sync}
+    own = {"v": "cv", "s": "cs", "t": "ct", "g": "cg"}
+    total = {}
+    waited = {}
+    known = {q: {} for q in Q}
+    recs = {}
+    ndma = [0]
+    nj = [0]
+
+    def sl(name, a=None, b=None, step=1):
+        o, n = POOL[name] if name in POOL else (0, SCRATCH[name][1][1])
+        a, b, step = slice(a, b, step).indices(n)
+        if name in POOL:
+            name = "pool"
+        if name == "ps":
+            m = ((1 << 512) - 1) << (512 * (a // 512))
+        else:
+            m = 0
+            for c in range(o + a, o + b, step):
+                m |= 1 << c
+        return (T[name][:, o + a:o + b:step], name, m)
+
+    vw = sl
+
+    def col(name, a):
+        return sl(name, a, a + 1)
+
+    def ind(win, off, cast=None):
+        ap_ = win[0] if cast is None else win[0].bitcast(cast)
+        return (ap_.indirect(off[0]), win[1], win[2], off)
+
+    def need(q, reads, writes):
+        deps = {}
+        for kind, views in (("r", reads), ("w", writes)):
+            for v in views:
+                for (m, k, tok, eng) in recs.get(v[1], []):
+                    if not (m & v[2]):
+                        continue
+                    if kind == "r" and k == "r" and (v[1] != "ps" or eng == q):
+                        continue
+                    if eng == q and q == "t":
+                        continue
+                    if tok[0] not in deps or deps[tok[0]][1] < tok[1]:
+                        deps[tok[0]] = tok
+        for tok in sorted(deps.values(), key=lambda tk: -len(tk[2])):
+            if known[q].get(tok[0], 0) >= tok[1]:
+                continue
+            Q[q].wait_ge(T.sem[tok[0]], tok[1])
+            waited[tok[0]] = max(waited.get(tok[0], 0), tok[1])
+            known[q][tok[0]] = tok[1]
+            for s, n in tok[2].items():
+                if known[q].get(s, 0) < n:
+                    known[q][s] = n
+
+    def note(eng, tok, reads, writes):
+        for v in writes:
+            old = recs.get(v[1], [])
+            recs[v[1]] = [r for r in old if r[0] & ~v[2]] + [(v[2], "w", tok, eng)]
+        for v in reads:
+            recs.setdefault(v[1], []).append((v[2], "r", tok, eng))
+
+    def op(q, fn, writes, reads):
+        rd = []
+        for v in reads:
+            if isinstance(v, tuple):
+                rd.append(v)
+                if len(v) == 4:
+                    rd.append(v[3])
+        need(q, rd, writes)
+        s = own[q]
+        total[s] = total.get(s, 0) + 1
+        fn().then_inc(T.sem[s], 1)
+        note(q, (s, total[s], dict(known[q])), rd, writes)
+
+    def dma(q, out, in_, writes, reads):
+        need(q, reads, writes)
+        s = "d%d" % ndma[0]
+        ndma[0] += 1
+        total[s] = 16
+        Q[q].dma_start(out, in_).then_inc(T.sem[s], 16)
+        note("dma", (s, 16, dict(known[q])), reads, writes)
+
+    def ap(v):
+        return v[0] if isinstance(v, tuple) else v
+
+    def tt(out, a, b, o):
+        op("v", lambda: g.vector.tensor_tensor(out[0], a[0], b[0], o), [out], [a, b])
+
+    def ts(out, a, s1, o0, s2=None, o1=None):
+        if s2 is None:
+            op("v", lambda: g.vector.tensor_scalar(out[0], a[0], ap(s1), None, o0), [out], [a, s1])
+        else:
+            op("v", lambda: g.vector.tensor_scalar(out[0], a[0], ap(s1), ap(s2), o0, o1), [out], [a, s1, s2])
+
+    def cp(out, a):
+        op("v", lambda: g.vector.tensor_copy(out[0], a[0]), [out], [a])
+
+    def scan(out, d0, d1, init, o0, o1):
+        op("v", lambda: g.vector.tensor_tensor_scan(out[0], d0[0], d1[0], init, o0, o1), [out], [d0, d1])
+
+    def red(out, a, o, neg=False):
+        op("v", lambda: g.vector.tensor_reduce(out[0], a[0], AxisListType.X, o, negate=neg), [out], [a])
+
+    def tr(out, a):
+        op("v", lambda: g.vector.transpose(out[0], a[0]), [out], [a])
+
+    def ms(out, c):
+        op("v", lambda: g.vector.memset(out[0], c), [out], [])
+
+    def quant(q, s, a):
+        op("v", lambda: g.vector.quantize_mx(q[0], s[0], a[0]), [q, s], [a])
+
+    def act(out, a, f, bias=None, scale=None, accum=None):
+        kw = {}
+        if scale is not None:
+            kw["scale"] = scale
+        if bias is not None:
+            kw["bias"] = ap(bias)
+        if accum is not None:
+            kw["accum_out"] = accum[0]
+        op("s", lambda: g.scalar.activation(out[0], a[0], f, **kw), [out] + ([accum] if accum else []), [a, bias])
+
+    def pick(q, o, i):
+        if q == "s":
+            act(o, i, F.Copy)
+        else:
+            cp(o, i)
+
+    def mm(bank, n, lq, ls, rq, rs):
+        out = sl("ps", 512 * bank, 512 * bank + n)
+        op("t", lambda: g.tensor.matmul_mx(out[0], lq[0], ls[0], rq[0], rs[0], True, True), [out], [lq, ls, rq, rs])
+
+    def iota(out, pattern, base, mult=0, small=True):
+        if small:
+            op("g", lambda: g.iota(out[0], pattern, base, mult, allow_small_or_imprecise_dtypes=True), [out], [])
+        else:
+            op("g", lambda: g.iota(out[0], pattern, base, mult), [out], [])
+
+    def remote(dst, out_ap, src, src_ap, sem):
+        need("g", [src], [])
+        rid, pid, _ = topo.addr(dst)
+        g.remote_dma(out_ap, src_ap, T.sem[sem], T.sem.loc, pid, rid, topo.mask(core, dst))
+        total["loc"] = total.get("loc", 0) + len(topo.engines(core, dst))
+
+    def junk(n):
+        nj[0] = (nj[0] + 1) % 4
+        return sl("junk", 512 * nj[0], 512 * nj[0] + n)
+
+    def ps(bank, a, b):
+        return sl("ps", 512 * bank + a, 512 * bank + b)
+
+    mates = [T.cores[rank ^ PARTNER[t]] for t in range(ROUNDS)]
+    for t in range(ROUNDS):
+        n = len(topo.engines(mates[t], core))
+        note("far", ("aq%d" % t, 2 * n, {}), [], [vw("lq%d" % t), vw("ls%d" % t)])
+        note("far", ("al%d" % t, n, {}), [], [sl("la%d" % t, 0, 8)])
+        note("far", ("am%d" % t, n, {}), [], [sl("la%d" % t, 8, 16)])
+        total["aq%d" % t] = 2 * n
+        total["al%d" % t] = n
+        total["am%d" % t] = n
+
+    dma("s", T.ub[:], T.u[:], [vw("ub")], [])
+    dma("y", T.tt0[:, 0:4 * C], T.x[:], [sl("tt0", 0, 4 * C)], [])
+    dma("s", T.tt0[:, 4 * C:4 * CW], T.x[:, 0:4 * (CW - C)], [sl("tt0", 4 * C, 4 * CW)], [])
+
+    iota(sl("diag", 0, C), [[1, C]], 0, -4)
+    iota(sl("diag", C, 2 * C), [[1, C]], C, -4)
+    iota(vw("pki"), [[1, 2], [16, 8]], 0, 0, False)
+    tabs = [([[16, 2], [32, 16]], 0), ([[16, 2], [32, 16]], 1), ([[0, 2], [-8, 2], [1, 8]], 8),
+            ([[0, 2], [4, 4], [-1, 4]], 3), ([[-4, 4], [2, 2], [-1, 2]], 13), ([[8, 2], [-4, 2], [1, 4]], 4),
+            ([[0, 2], [1, 16]], 0), ([[1, 2], [0, 16]], 0)]
+    for i, (pat, base) in enumerate(tabs):
+        if i in (4, 5):
+            iota(sl("tab", 32 * i, 32 * i + 16), pat, base)
+            iota(sl("tab", 32 * i + 16, 32 * i + 32), pat, base)
+        else:
+            iota(sl("tab", 32 * i, 32 * i + 32), pat, base)
+    ms(sl("hin", 16, 24), BIG)
+    ms(sl("horn", 1, 8, 2), 1.0)
+    ms(sl("horn", 0, 8, 2), 2.0)
+    ms(sl("lob", 1, 512, 2), -512.0)
+    ms(col("c16", 16), 0.0)
+    for h in (0, C):
+        for b in range(4):
+            ts(sl("eb", 512 * b + h, 512 * b + h + C), sl("diag", h, h + C), float(b), A.is_equal)
+    cp(vw("pku"), vw("pki"))
+    quant(vw("qe"), vw("se"), vw("eb"))
+    quant(vw("qu"), vw("su"), vw("ub"))
+    dma("y", T.qw[:].bitcast(dt.uint8), T.wc[:], [vw("qw")], [vw("ub")])
+    dma("y", T.sw[:], T.ws[:], [vw("sw")], [])
+    dma("y", T.vb[:], T.v[:], [vw("vb")], [])
+    iota(sl("c16", 0, 16), [[16, 16]], 0)
+    icol = col("tabt", 192)
+    hcol = col("tabt", 224)
+    o_s, o_z, o_1, o_3, o_6, o_8 = [col("offs", 2 * i) for i in range(6)]
+
+    def decode(src_q, src_s, dst):
+        for b in range(4):
+            mm(3 + b, C, sl("qe", 128 * b, 128 * b + 128), sl("se", 128 * b, 128 * b + 128), src_q, src_s)
+        for b in range(4):
+            act(sl(dst, C * b, C * b + C), ps(3 + b, 0, C), F.Copy)
+
+    for t in range(ROUNDS):
+        last = t == ROUNDS - 1
+        w = C if last else CW
+        nk = w // 16
+        qt, st, au, la = "qt%d" % t, "st%d" % t, "au%d" % t, "la%d" % t
+        dd, ds, zz, zs, rw = "dd%d" % t, "ds%d" % t, "zz%d" % t, "zs%d" % t, "rw%d" % t
+        if t == 0:
+            cp((T.quz[:].bitcast(dt.uint32),) + vw("quz")[1:], ind(vw("qu"), sl("pku", 8, 16), dt.uint32))
+            act(vw("suz"), ind(vw("su"), sl("pku", 8, 16)), F.Copy)
+            act(vw("sus"), ind(vw("su"), sl("pku", 0, 8)), F.Copy)
+        quant(vw(qt), vw(st), vw("tt%d" % t))
+        mm(0, CW, vw("qu"), vw("su"), vw(qt), vw(st))
+        mm(1, C, vw("quz"), vw("suz"), sl(qt, 0, C), sl(st, 0, C))
+        if t == 0:
+            cp((T.qus[:].bitcast(dt.uint32),) + vw("qus")[1:], ind(vw("qu"), sl("pku", 0, 8), dt.uint32))
+            ms(sl("tab", 72, 75, 2), 16.0)
+            ms(sl("tab", 88, 91, 2), 16.0)
+        mm(2, C, vw("qus"), vw("sus"), sl(qt, 0, C), sl(st, 0, C))
+        remote(mates[t], T["lq%d" % t][:].bitcast(dt.uint8), sl(qt, 0, C), T[qt][:, 0:C].bitcast(dt.uint8), "aq%d" % t)
+        remote(mates[t], T["ls%d" % t][:], sl(st, 0, C), T[st][:, 0:C], "aq%d" % t)
+        if t == 0:
+            iota(vw("r16"), [[0, CW // 16], [1, 16]], 0)
+            iota(vw("i512"), [[1, 512]], 0)
+
+        bs = "nz" if t == 0 else "base"
+        lo = "nzn" if t == 0 else "lon"
+        if t > 0:
+            tr(sl("mtr", C, 2 * C), sl("mw", 16, CW))
+        else:
+            tr(vw("tabt"), vw("tab"))
+        act(vw("nz"), ps(1, 0, C), F.Relu, scale=-1.0)
+        tr(sl("ptr", 0, C), ps(0, 0, C))
+        if t == 0:
+            cp(sl("offs", 0, 12, 2), sl("tabt", 0, 192, 32))
+        tr(sl("ptr", C, 2 * C), ps(0, 16, CW))
+        act(vw("r0"), ps(2, 0, C), F.Relu, scale=-1.0)
+        if t > 0:
+            cp(vw("mn"), ind(vw("mtr"), o_s))
+        ts(vw("nzn"), ind(vw("ptr"), o_z), -1.0, A.mult, 0.0, A.max)
+        act(vw("asn"), ind(vw("ptr"), o_s), F.Abs)
+        act(vw("r1"), ps(2, 0, C), F.Relu)
+        fill = []
+        if t > 0:
+            for h in (0, 128):
+                fill.append(lambda h=h: tt(sl("base", h, h + 128), sl("nz", h, h + 128), sl("mw", h, h + 128), A.add))
+        for j, r in ((0, "r0"), (1, "r1")):
+            for h in (0, 128):
+                fill.append(lambda j=j, r=r, h=h: tt(sl("xc", 2 * h + j, 2 * h + 256, 2), sl(bs, h, h + 128),
+                                                     sl(r, h, h + 128), A.add))
+
+        def filler():
+            if fill:
+                fill.pop(0)()
+
+        if t > 0:
+            filler()
+            tt(vw("lon"), vw("nzn"), vw("mn"), A.add)
+        filler()
+        tt(sl("hin", 0, 16), vw(lo), vw("asn"), A.add)
+        decode(sl(qt, 0, C), sl(st, 0, C), dd)
+
+        def halves(name):
+            return sl(name, 0, 16), sl(name, 16, 32)
+
+        def turns(name):
+            return sl(name, 0, 32, 2), sl(name, 1, 32, 2)
+
+        def step(dst, a, b):
+            tt(dst[0], a, b, A.min)
+            tt(dst[1], a, b, A.max)
+            filler()
+
+        filler()
+        step(turns("s1"), ind(vw("hin"), o_1), vw(lo))
+        step(halves("s2"), *halves("s1"))
+        step(halves("s3"), ind(sl("s2", 16, 32), o_3), sl("s2", 0, 16))
+        while fill:
+            filler()
+
+        def count_s(pv, i):
+            act(junk(512 - XS[i]), sl("xc", XS[i], 512), F.Sign, bias=pv, scale=-1.0, accum=col("acc", i))
+
+        def cmp_v(pv, i):
+            if XS[i]:
+                o = XM * (i % 2)
+                ts(sl("fl", o, o + XS[i]), sl("xc", 0, XS[i]), pv, A.is_le, -B2, A.mult)
+
+        def scan_v(i):
+            if XS[i]:
+                o, hx = XM * (i % 2), XS[i] // 2
+                scan(sl("fsc", o // 2, o // 2 + hx), sl("fl", o, o + hx), sl("fl", o + hx, o + 2 * hx),
+                     (hx - 0.25) * B2, A.add, A.add)
+
+        def why(i):
+            ts(col("yy", i), col("acc", i), -B2 / 2, A.mult,
+               col("fsc", XM * (i % 2) // 2 + XS[i] // 2 - 1) if XS[i] else -0.25 * B2, A.add)
+
+        for i in range(2):
+            count_s(col("hin", 2 * i), 6 + i)
+        fill.append(lambda: cp(sl("piv", 6, 8), sl("hin", 0, 3, 2)))
+        for h in range(0, C, 64):
+            fill.append(lambda h=h: tt(sl("lob", 2 * h, 2 * h + 128, 2), sl("xc", 2 * h, 2 * h + 128, 2),
+                                       sl("xc", 2 * h + 1, 2 * h + 128, 2), A.is_le))
+        step(halves("s4"), *turns("s3"))
+        step(turns("s5"), *turns("s4"))
+        step(turns("s6"), ind(sl("s5", 16, 32), o_6), sl("s5", 0, 16))
+        step(turns("s7"), *halves("s6"))
+        step(turns("s8"), ind(sl("s7", 16, 32), o_8), sl("s7", 0, 16))
+
+        for l in range(2):
+            o = 16 * l
+            tt(sl("s9", o + 1, o + 16, 2), sl("s8", o, o + 8), sl("s8", o + 8, o + 16), A.max)
+            count_s(col("s9", o + 7), l)
+            tt(sl("s9", o, o + 16, 2), sl("s8", o, o + 8), sl("s8", o + 8, o + 16), A.min)
+        for l in range(2):
+            cmp_v(col("s9", 16 * l + 7), l)
+        cp(sl("piv", 0, 2), sl("s9", 7, 32, 16))
+        scan_v(0)
+        if t == 0:
+            ts(vw("mbig"), sl("tab", 224, 256), hcol, A.not_equal, BIG, A.mult)
+            ts(vw("mown"), sl("tab", 224, 256), hcol, A.is_equal, BIG, A.mult)
+            ts(vw("mb1"), sl("tab", 224, 256), hcol, A.is_equal, B1, A.mult)
+        pending = 1
+        for k in range(3):
+            for l in range(2):
+                i = 2 * k + l
+                n = i + 2 if k < 2 else i + 4
+                why(i)
+                filler()
+                scan_v(pending)
+                if k == 0:
+                    lo_c, hi_c = col("s9", 16 * l + 3), col("s9", 16 * l + 11)
+                elif k == 1:
+                    lo_c, hi_c = col("w7", 8 * l + 1), col("w7", 8 * l + 5)
+                else:
+                    lo_c, hi_c = col("v2", 2 * l), col("v2", 2 * l + 1)
+                ts(col("piv", n), col("yy", i), lo_c, A.max, hi_c, A.min)
+                count_s(col("piv", n), n)
+                if k == 0:
+                    ts(sl("w7a", 8 * l, 8 * l + 8), sl("s9", 16 * l, 16 * l + 8), col("yy", i), A.max)
+                    fill.append(lambda l=l: tt(sl("w7", 8 * l, 8 * l + 8), sl("w7a", 8 * l, 8 * l + 8),
+                                               sl("s9", 16 * l + 8, 16 * l + 16), A.min))
+                elif k == 1:
+                    ts(sl("v2a", 2 * l, 2 * l + 2), sl("w7", 8 * l, 8 * l + 3, 2), col("yy", i), A.max)
+                    fill.append(lambda l=l: tt(sl("v2", 2 * l, 2 * l + 2), sl("v2a", 2 * l, 2 * l + 2),
+                                               sl("w7", 8 * l + 4, 8 * l + 7, 2), A.min))
+                elif l == 0:
+                    ts(sl("yy", 6, 8), sl("acc", 6, 8), -B2 / 2, A.mult, -0.25 * B2, A.add)
+                else:
+                    tt(vw("e1"), sl("piv", 0, 8), sl("yy", 0, 8), A.max)
+                cmp_v(col("piv", n), n)
+                pending = n
+        tt(vw("e2"), sl("piv", 0, 8), sl("yy", 0, 8), A.min)
+        ts(vw("e4"), sl("yy", 0, 8), 0.0, A.is_gt)
+        why(8)
+        scan_v(9)
+        red(col("fin", 0), vw("e1"), A.min)
+        red(col("fin", 1), vw("e2"), A.max)
+        scan(vw("e3"), vw("horn"), vw("e4"), -255.5 / 256, A.mult, A.add)
+        ts(col("fin", 3), col("yy", 8), col("piv", 8), A.max, col("fin", 0), A.min)
+        ts(col("fin", 4), col("yy", 8), col("piv", 8), A.min, col("fin", 1), A.max)
+        ts(col("fin", 5), col("yy", 8), 0.0, A.is_gt, col("e3", 7), A.add)
+        decode(vw("lq%d" % t), vw("ls%d" % t), ds)
+        ts(sl("prep", 0, 32), vw("mbig"), col("fin", 3), A.max)
+        ts(sl("prep", 64, 96), vw("mown"), col("fin", 4), A.min)
+        why(9)
+        ts(sl("prep", 128, 160), vw("mb1"), col("fin", 5), A.mult)
+        ts(sl("prep", 32, 64), vw("mbig"), col("piv", 9), A.max, col("yy", 9), A.max)
+        ts(sl("prep", 96, 128), vw("mown"), col("piv", 9), A.min, col("yy", 9), A.min)
+        ts(sl("prep", 160, 192), vw("mb1"), col("yy", 9), A.min, 0.0, A.max)
+        tr(vw("prt"), vw("prep"))
+        if t == 0:
+            ts(vw("cvec"), vw("c16"), icol, A.add)
+        red(col("thr", 0), sl("prt", 0, 64), A.min)
+        red(col("thr", 1), sl("prt", 64, 128), A.max)
+        red(col("thr", 2), sl("prt", 128, 192), A.add, True)
+        if t == 0:
+            ts(vw("chalf"), vw("c16"), icol, A.add, 0.5, A.add)
+        ts(col("thr", 3), col("thr", 2), col("thr", 1), A.max, col("thr", 0), A.min)
+        cut = col("thr", 3)
+
+        act(sl("ysg", 0, C), sl("xc", 0, C), F.Sign, bias=cut, scale=-1.0)
+        act(sl("ysg", C, 2 * C), sl("xc", C, 2 * C), F.Sign, bias=cut, scale=-1.0)
+        ts(sl("lt", C, 2 * C), sl("xc", C, 2 * C), cut, A.is_lt)
+        ts(sl("lt", 0, C), sl("ysg", 0, C), 0.0, A.is_gt)
+        ts(sl("le", 0, C), sl("ysg", 0, C), 0.0, A.is_ge)
+        scan(vw("clt"), sl("lt", 0, 512, 2), sl("lt", 1, 512, 2), 0.0, A.add, A.add)
+        ts(sl("le", C, 2 * C), sl("ysg", C, 2 * C), 0.0, A.is_ge)
+        ts(vw("cap"), vw("clt"), col("clt", C - 1), A.subtract, 256.0, A.add)
+        scan(vw("cle"), sl("le", 0, 512, 2), sl("le", 1, 512, 2), 0.0, A.add, A.add)
+        scan(sl("sb", 1, 512, 2), vw("cle"), vw("cap"), 0.0, A.max, A.min)
+
+        def kept(a, b):
+            return sl("sb", 2 * a + 1, 2 * b, 2)
+
+        for i, m in enumerate(SM):
+            a, b = (0, 160) if m < 8 else (104, 256)
+            act(junk(b - a), kept(a, b), F.Sign, bias=col("chalf", m), scale=-1.0, accum=col("iac", i))
+        nv = len(VM)
+        for i in range(nv + 1):
+            if i < nv:
+                m = VM[i]
+                ts(sl("ifl", 136 * i, 136 * i + 136), kept(8 * m, 8 * m + 136), col("cvec", m), A.is_le)
+            if i > 0:
+                j = i - 1
+                scan(sl("isc", 68 * j, 68 * j + 68), sl("ifl", 136 * j, 136 * j + 68),
+                     sl("ifl", 136 * j + 68, 136 * j + 136), float(8 * VM[j]), A.add, A.add)
+            if i == 5:
+                cp(sl(au, 4, 8), sl("isc", 67, 68 * 4, 68))
+                ts(sl(au, 0, 4), sl("iac", 0, 4), 0.5, A.mult, 80.0, A.add)
+                remote(mates[t], T[la][:, 0:8], sl(au, 0, 8), T[au][:, 0:8], "al%d" % t)
+        ts(sl(au, 13, 16), sl("iac", 4, 7), 0.5, A.mult, 180.0, A.add)
+        cp(sl(au, 8, 13), sl("isc", 68 * 4 + 67, 68 * nv, 68))
+        remote(mates[t], T[la][:, 8:16], sl(au, 8, 16), T[au][:, 8:16], "am%d" % t)
+
+        if not last:
+            ts(col(au, 16), col("iac", 0), 0.5, A.mult, 80.0, A.add)
+        alist = sl(au, 0, nk)
+        klist = sl("ku", 0, nk)
+
+        def zgather(q, b):
+            pick(q, sl(zz, CW * b, CW * b + w), ind(sl(dd, C * b, C * b + C), alist))
+
+        def mosaic(h):
+            for b in range(4):
+                pick("vs"[b % 2], sl(zs, 512 * h + b, 512 * h + 512, 4),
+                     ind(sl(ds, C * b, C * b + C), sl(la, 8 * h, 8 * h + 8)))
+
+        def product(h):
+            q, s = sl("qz%d" % t, 128 * h, 128 * h + 128), sl("sz%d" % t, 128 * h, 128 * h + 128)
+            quant(q, s, sl(zs, 512 * h, 512 * h + 512))
+            for b in range(4):
+                mm((3 + 4 * h + b) % 8, 128, sl("qw", 128 * b, 128 * b + 128), sl("sw", 128 * b, 128 * b + 128), q, s)
+
+        def signed(b, h):
+            for j in range(2):
+                act(sl(rw, 512 * b + 256 * h + j, 512 * b + 256 * h + 256, 2), ps((3 + 4 * h + b) % 8, 0, 128),
+                    F.Copy, scale=(0.015625, -0.015625)[j])
+
+        ts(sl("sb", 0, 512, 2), sl("sb", 1, 512, 2), -1.0, A.add)
+        zgather("s", 0)
+        ts(sl("a2u", 0, nk), alist, 2.0, A.mult)
+        scan(vw("h2"), vw("lob"), vw("sb"), 0.0, A.add, A.max)
+        ts(sl("a2", 0, nk), alist, 2.0, A.mult)
+        act(sl("hw", 0, w), ind(vw("h2"), sl("a2u", 0, nk)), F.Copy)
+        zgather("s", 1)
+        if t == 0:
+            ts(vw("latch"), vw("r16"), icol, A.is_le, 512.0, A.mult)
+        zgather("v", 2)
+        scan(sl("hl", 0, w), sl("latch", 0, w), sl("hw", 0, w), 0.0, A.max, A.min)
+        tt(sl("bitn", 0, nk), sl("hl", 15, w, 16), sl("cvec", 0, nk), A.is_le)
+        if t == 0:
+            quant(vw("qv"), vw("sv"), vw("vb"))
+        tt(sl("kn", 0, nk), sl("bitn", 0, nk), sl("a2", 0, nk), A.add)
+        cp(klist, sl("kn", 0, nk))
+
+        mosaic(0)
+        product(0)
+        pick("s", sl("mw", 0, w), ind(vw("xc"), klist))
+        if last:
+            dma("y", T.ml[:], T.mw[0:128:16, 0:C], [], [vw("mw")])
+        mosaic(1)
+        product(1)
+        for b in range(3):
+            signed(b, 0)
+        zgather("v", 3)
+        if not last:
+            tr(sl("mtr", 0, C), sl("mw", 0, C))
+        for b in range(4):
+            if b > 2:
+                signed(b, 0)
+            signed(b, 1)
+            tt(sl("tt%d" % (t + 1), b, 4 * w, 4), ind(sl(rw, 512 * b, 512 * b + 512), klist),
+               sl(zz, CW * b, CW * b + w), A.add)
+        if last:
+            act(vw("kw"), ind(vw("i512"), klist), F.Copy)
+            dma("y", T.kl[:], T.kw[0:128:16, 0:C], [], [vw("kw")])
+
+    qt, st = "qt%d" % ROUNDS, "st%d" % ROUNDS
+    quant(vw(qt), vw(st), vw("tt%d" % ROUNDS))
+    for h in range(2):
+        mm(h, 128, vw("qv"), vw("sv"), sl(qt, 128 * h, 128 * h + 128), sl(st, 128 * h, 128 * h + 128))
+    dma("y", T.oc[:], T[qt][:].bitcast(dt.uint8), [], [vw(qt)])
+    for k in range(4):
+        dma("s" if k == 3 else "y", T.osc[4 * k:4 * k + 4, :], T[st][32 * k:32 * k + 4, :], [], [vw(st)])
+    act(sl("yo", 0, 128), ps(0, 0, 128), F.Copy)
+    cp(sl("yo", 128, C), ps(1, 0, 128))
+    dma("s", T.y[:], T.yo[:], [], [vw("yo")])
+    for s, n in total.items():
+        if waited.get(s, 0) < n:
+            g.wait_ge(T.sem[s], n)

@@ -6,8 +6,6 @@ C = 256
 CW = 272
 ROUNDS = 3
 PARTNER = [1, 2, 4]
-XS = [96, 96, 96, 96, 96, 96, 0, 0, 96, 0]
-XM = 96
 BIG = 2.0 ** 76
 B1 = 2.0 ** 74
 B2 = 2.0 ** 84
@@ -35,20 +33,20 @@ for _t in range(ROUNDS):
         _buf(_n + str(_t), _c, _d)
 for _d, _l in [
     ("bfloat16", [("ub", 512), ("vb", 512), ("diag", 512), ("eb", 2048), ("latch", CW), ("junk", 2048),
-                  ("fl", 2 * XM), ("fsc", XM), ("lt", 512), ("le", 512), ("ysg", 512), ("clt", C), ("cle", C),
-                  ("cap", C), ("sb", 512), ("ifl", 136 * len(VM)), ("lob", 512), ("h2", 512), ("hw", CW), ("hl", CW)]),
+                  ("lt", 512), ("le", 512), ("ysg", 512), ("clt", 512), ("cap", C), ("sb", 512),
+                  ("ifl", 136 * len(VM)), ("zero", 512), ("hw", CW), ("hl", CW)]),
     (X4, [("qu", 128), ("qv", 128), ("qus", 128), ("quz", 128), ("qw", 512), ("qe", 512)]),
     ("uint8", [("su", 128), ("sv", 128), ("sus", 128), ("suz", 128), ("sw", 512), ("se", 512)]),
     ("uint16", [("offs", 16), ("pku", 16), ("a2u", 18), ("ku", 18)]),
     ("int32", [("pki", 16)]),
     ("float32", [("tab", 256), ("tabt", 256), ("c16", 17), ("cvec", 17), ("chalf", 17), ("r16", CW), ("mbig", 32),
                  ("mown", 32), ("mb1", 32), ("horn", 8), ("i512", 512), ("ptr", 512), ("nzn", 16), ("asn", 16),
-                 ("lon", 16), ("hin", 24), ("mn", 16), ("mw", CW), ("mtr", 512), ("nz", C), ("r0", C), ("r1", C),
+                 ("lon", 16), ("hin", 24), ("mw", CW), ("mtr", 512), ("nz", C), ("r0", C), ("r1", C),
                  ("base", C), ("xc", 512), ("s1", 32), ("s2", 32), ("s3", 32), ("s4", 32), ("s5", 32), ("s6", 32),
-                 ("s7", 32), ("s8", 32), ("s9", 32), ("piv", 10), ("yy", 10), ("acc", 10), ("w7a", 16), ("w7", 16),
-                 ("v2a", 4), ("v2", 4), ("e1", 8), ("e2", 8), ("e3", 8), ("e4", 8), ("fin", 8), ("prep", 192),
-                 ("prt", 192), ("thr", 4), ("isc", 68 * len(VM)), ("iac", 8), ("a2", 17), ("bitn", 17), ("kn", 17),
-                 ("kw", C), ("yo", C)]),
+                 ("s7", 32), ("s8", 32), ("s9", 64), ("mul", 4), ("npv", 20), ("ny", 10), ("cand", 8), ("cs", 17),
+                 ("piv", 10), ("yy", 10), ("acc", 10), ("w7", 8), ("e1", 8), ("e2", 8), ("e3", 8), ("e4", 8),
+                 ("fin", 8), ("prep", 288), ("prt", 288), ("thr", 4), ("isc", 68 * len(VM)), ("iac", 8),
+                 ("a2", 17), ("bitn", 17), ("kn", 17), ("kw", C), ("yo", C)]),
 ]:
     for _n, _c in _l:
         if _c <= 96 and _d == "float32":
@@ -164,7 +162,7 @@ def rank_program(g, core, T, topo):
         op("v", lambda: g.vector.tensor_copy(out[0], a[0]), [out], [a])
 
     def scan(out, d0, d1, init, o0, o1):
-        op("v", lambda: g.vector.tensor_tensor_scan(out[0], d0[0], d1[0], init, o0, o1), [out], [d0, d1])
+        op("v", lambda: g.vector.tensor_tensor_scan(out[0], d0[0], d1[0], ap(init), o0, o1), [out], [d0, d1, init])
 
     def red(out, a, o, neg=False):
         op("v", lambda: g.vector.tensor_reduce(out[0], a[0], AxisListType.X, o, negate=neg), [out], [a])
@@ -246,7 +244,10 @@ def rank_program(g, core, T, topo):
     ms(sl("hin", 16, 24), BIG)
     ms(sl("horn", 1, 8, 2), 1.0)
     ms(sl("horn", 0, 8, 2), 2.0)
-    ms(sl("lob", 1, 512, 2), -512.0)
+    ms(vw("zero"), 0.0)
+    ms(col("mul", 0), -B2)
+    ms(col("mul", 2), B2)
+    ms(sl("mul", 1, 4, 2), -1.0)
     ms(col("c16", 16), 0.0)
     for h in (0, C):
         for b in range(4):
@@ -304,11 +305,6 @@ def rank_program(g, core, T, topo):
             cp(sl("offs", 0, 12, 2), sl("tabt", 0, 192, 32))
         tr(sl("ptr", C, 2 * C), ps(0, 16, CW))
         act(vw("r0"), ps(2, 0, C), F.Relu, scale=-1.0)
-        if t > 0:
-            cp(vw("mn"), ind(vw("mtr"), o_s))
-        ts(vw("nzn"), ind(vw("ptr"), o_z), -1.0, A.mult, 0.0, A.max)
-        act(vw("asn"), ind(vw("ptr"), o_s), F.Abs)
-        act(vw("r1"), ps(2, 0, C), F.Relu)
         fill = []
         if t > 0:
             for h in (0, 128):
@@ -324,7 +320,12 @@ def rank_program(g, core, T, topo):
 
         if t > 0:
             filler()
-            tt(vw("lon"), vw("nzn"), vw("mn"), A.add)
+        ts(vw("nzn"), ind(vw("ptr"), o_z), -1.0, A.mult, 0.0, A.max)
+        act(vw("asn"), ind(vw("ptr"), o_s), F.Abs)
+        act(vw("r1"), ps(2, 0, C), F.Relu)
+        if t > 0:
+            filler()
+            tt(vw("lon"), ind(vw("mtr"), o_s), vw("nzn"), A.add)
         filler()
         tt(sl("hin", 0, 16), vw(lo), vw("asn"), A.add)
         decode(sl(qt, 0, C), sl(st, 0, C), dd)
@@ -344,33 +345,28 @@ def rank_program(g, core, T, topo):
         step(turns("s1"), ind(vw("hin"), o_1), vw(lo))
         step(halves("s2"), *halves("s1"))
         step(halves("s3"), ind(sl("s2", 16, 32), o_3), sl("s2", 0, 16))
-        while fill:
-            filler()
 
-        def count_s(pv, i):
-            act(junk(512 - XS[i]), sl("xc", XS[i], 512), F.Sign, bias=pv, scale=-1.0, accum=col("acc", i))
+        def count(i, pv=None):
+            if pv is None:
+                act(junk(512), vw("xc"), F.Sign, bias=col("npv", 2 * i + 1), accum=col("acc", i))
+            else:
+                act(junk(512), vw("xc"), F.Sign, bias=pv, scale=-1.0, accum=col("acc", i))
 
-        def cmp_v(pv, i):
-            if XS[i]:
-                o = XM * (i % 2)
-                ts(sl("fl", o, o + XS[i]), sl("xc", 0, XS[i]), pv, A.is_le, -B2, A.mult)
+        def why(i, neg=False):
+            sg = (-1.0 if i < 2 else 1.0) * (-1.0 if neg else 1.0)
+            ts(col("ny" if neg else "yy", i), col("acc", i), sg * B2 / 2, A.mult, (0.25 if neg else -0.25) * B2, A.add)
 
-        def scan_v(i):
-            if XS[i]:
-                o, hx = XM * (i % 2), XS[i] // 2
-                scan(sl("fsc", o // 2, o // 2 + hx), sl("fl", o, o + hx), sl("fl", o + hx, o + 2 * hx),
-                     (hx - 0.25) * B2, A.add, A.add)
-
-        def why(i):
-            ts(col("yy", i), col("acc", i), -B2 / 2, A.mult,
-               col("fsc", XM * (i % 2) // 2 + XS[i] // 2 - 1) if XS[i] else -0.25 * B2, A.add)
+        def clamp(out, y, a, b):
+            ts(out, y, a, A.max, b, A.min)
 
         for i in range(2):
-            count_s(col("hin", 2 * i), 6 + i)
+            count(6 + i, col("hin", 2 * i))
         fill.append(lambda: cp(sl("piv", 6, 8), sl("hin", 0, 3, 2)))
-        for h in range(0, C, 64):
-            fill.append(lambda h=h: tt(sl("lob", 2 * h, 2 * h + 128, 2), sl("xc", 2 * h, 2 * h + 128, 2),
-                                       sl("xc", 2 * h + 1, 2 * h + 128, 2), A.is_le))
+        if t == 0:
+            fill.append(lambda: ts(vw("mbig"), sl("tab", 224, 256), hcol, A.not_equal, BIG, A.mult))
+            fill.append(lambda: ts(vw("mown"), sl("tab", 224, 256), hcol, A.is_equal, BIG, A.mult))
+            fill.append(lambda: ts(vw("mb1"), sl("tab", 224, 256), hcol, A.is_equal, B1, A.mult))
+            fill.append(lambda: ts(vw("cvec"), vw("c16"), icol, A.add))
         step(halves("s4"), *turns("s3"))
         step(turns("s5"), *turns("s4"))
         step(turns("s6"), ind(sl("s5", 16, 32), o_6), sl("s5", 0, 16))
@@ -380,85 +376,74 @@ def rank_program(g, core, T, topo):
         for l in range(2):
             o = 16 * l
             tt(sl("s9", o + 1, o + 16, 2), sl("s8", o, o + 8), sl("s8", o + 8, o + 16), A.max)
-            count_s(col("s9", o + 7), l)
+            count(l, col("s9", o + 7))
             tt(sl("s9", o, o + 16, 2), sl("s8", o, o + 8), sl("s8", o + 8, o + 16), A.min)
-        for l in range(2):
-            cmp_v(col("s9", 16 * l + 7), l)
+        ts(sl("yy", 6, 8), sl("acc", 6, 8), -B2 / 2, A.mult, -0.25 * B2, A.add)
+        ts(sl("s9", 32, 64), sl("s9", 0, 32), -1.0, A.mult)
         cp(sl("piv", 0, 2), sl("s9", 7, 32, 16))
-        scan_v(0)
-        if t == 0:
-            ts(vw("mbig"), sl("tab", 224, 256), hcol, A.not_equal, BIG, A.mult)
-            ts(vw("mown"), sl("tab", 224, 256), hcol, A.is_equal, BIG, A.mult)
-            ts(vw("mb1"), sl("tab", 224, 256), hcol, A.is_equal, B1, A.mult)
-        pending = 1
         for k in range(3):
             for l in range(2):
-                i = 2 * k + l
+                i, o = 2 * k + l, 16 * l
                 n = i + 2 if k < 2 else i + 4
+                ends = sl("s9", o + 3, o + 44, 40) if k == 0 else sl("cand", 2 * i - 4, 2 * i - 2)
+                scan(sl("npv", 2 * n, 2 * n + 2), sl("mul", 0, 2) if k == 0 else sl("mul", 2, 4), ends, col("acc", i),
+                     A.mult, A.max)
+                count(n)
                 why(i)
+                if k < 2:
+                    why(i, True)
                 filler()
-                scan_v(pending)
+                filler()
+                y, ny = col("yy", i), col("ny", i)
                 if k == 0:
-                    lo_c, hi_c = col("s9", 16 * l + 3), col("s9", 16 * l + 11)
+                    clamp(col("cand", 2 * l), y, col("s9", o + 1), col("s9", o + 9))
+                    clamp(col("cand", 2 * l + 1), ny, col("s9", 32 + o + 13), col("s9", 32 + o + 5))
+                    clamp(col("w7", 4 * l), y, col("s9", o), col("s9", o + 8))
+                    for j, (yc, a, b) in enumerate(((y, o + 4, o + 12), (ny, 46 + o, 38 + o), (ny, 42 + o, 34 + o))):
+                        fill.append(lambda d=4 * l + 1 + j, yc=yc, a=a, b=b: clamp(col("w7", d), yc, col("s9", a), col("s9", b)))
                 elif k == 1:
-                    lo_c, hi_c = col("w7", 8 * l + 1), col("w7", 8 * l + 5)
-                else:
-                    lo_c, hi_c = col("v2", 2 * l), col("v2", 2 * l + 1)
-                ts(col("piv", n), col("yy", i), lo_c, A.max, hi_c, A.min)
-                count_s(col("piv", n), n)
-                if k == 0:
-                    ts(sl("w7a", 8 * l, 8 * l + 8), sl("s9", 16 * l, 16 * l + 8), col("yy", i), A.max)
-                    fill.append(lambda l=l: tt(sl("w7", 8 * l, 8 * l + 8), sl("w7a", 8 * l, 8 * l + 8),
-                                               sl("s9", 16 * l + 8, 16 * l + 16), A.min))
-                elif k == 1:
-                    ts(sl("v2a", 2 * l, 2 * l + 2), sl("w7", 8 * l, 8 * l + 3, 2), col("yy", i), A.max)
-                    fill.append(lambda l=l: tt(sl("v2", 2 * l, 2 * l + 2), sl("v2a", 2 * l, 2 * l + 2),
-                                               sl("w7", 8 * l + 4, 8 * l + 7, 2), A.min))
+                    filler()
+                    clamp(col("cand", 4 + 2 * l), y, col("w7", 4 * l), col("w7", 4 * l + 1))
+                    clamp(col("cand", 5 + 2 * l), ny, col("w7", 4 * l + 2), col("w7", 4 * l + 3))
                 elif l == 0:
-                    ts(sl("yy", 6, 8), sl("acc", 6, 8), -B2 / 2, A.mult, -0.25 * B2, A.add)
-                else:
-                    tt(vw("e1"), sl("piv", 0, 8), sl("yy", 0, 8), A.max)
-                cmp_v(col("piv", n), n)
-                pending = n
+                    ts(sl("piv", 2, 6), sl("npv", 5, 12, 2), -1.0, A.mult)
+        ts(sl("piv", 8, 10), sl("npv", 17, 20, 2), -1.0, A.mult)
+        tt(vw("e1"), sl("piv", 0, 8), sl("yy", 0, 8), A.max)
         tt(vw("e2"), sl("piv", 0, 8), sl("yy", 0, 8), A.min)
         ts(vw("e4"), sl("yy", 0, 8), 0.0, A.is_gt)
         why(8)
-        scan_v(9)
         red(col("fin", 0), vw("e1"), A.min)
         red(col("fin", 1), vw("e2"), A.max)
         scan(vw("e3"), vw("horn"), vw("e4"), -255.5 / 256, A.mult, A.add)
-        ts(col("fin", 3), col("yy", 8), col("piv", 8), A.max, col("fin", 0), A.min)
-        ts(col("fin", 4), col("yy", 8), col("piv", 8), A.min, col("fin", 1), A.max)
-        ts(col("fin", 5), col("yy", 8), 0.0, A.is_gt, col("e3", 7), A.add)
         decode(vw("lq%d" % t), vw("ls%d" % t), ds)
-        ts(sl("prep", 0, 32), vw("mbig"), col("fin", 3), A.max)
-        ts(sl("prep", 64, 96), vw("mown"), col("fin", 4), A.min)
+        ts(sl("prep", 32, 64), vw("mbig"), col("piv", 8), A.max, col("yy", 8), A.max)
+        ts(sl("prep", 128, 160), vw("mown"), col("piv", 8), A.min, col("yy", 8), A.min)
+        ts(sl("prep", 224, 256), vw("mb1"), col("yy", 8), A.min, 0.0, A.max)
         why(9)
-        ts(sl("prep", 128, 160), vw("mb1"), col("fin", 5), A.mult)
-        ts(sl("prep", 32, 64), vw("mbig"), col("piv", 9), A.max, col("yy", 9), A.max)
-        ts(sl("prep", 96, 128), vw("mown"), col("piv", 9), A.min, col("yy", 9), A.min)
-        ts(sl("prep", 160, 192), vw("mb1"), col("yy", 9), A.min, 0.0, A.max)
-        tr(vw("prt"), vw("prep"))
-        if t == 0:
-            ts(vw("cvec"), vw("c16"), icol, A.add)
-        red(col("thr", 0), sl("prt", 0, 64), A.min)
-        red(col("thr", 1), sl("prt", 64, 128), A.max)
-        red(col("thr", 2), sl("prt", 128, 192), A.add, True)
-        if t == 0:
-            ts(vw("chalf"), vw("c16"), icol, A.add, 0.5, A.add)
+        ts(sl("prep", 0, 32), vw("mbig"), col("fin", 0), A.max)
+        ts(sl("prep", 96, 128), vw("mown"), col("fin", 1), A.min)
+        ts(sl("prep", 192, 224), vw("mb1"), col("e3", 7), A.mult)
+        ts(sl("prep", 64, 96), vw("mbig"), col("piv", 9), A.max, col("yy", 9), A.max)
+        ts(sl("prep", 160, 192), vw("mown"), col("piv", 9), A.min, col("yy", 9), A.min)
+        ts(sl("prep", 256, 288), vw("mb1"), col("yy", 9), A.min, 0.0, A.max)
+        for j in range(3):
+            tr(sl("prt", 96 * j, 96 * j + 96), sl("prep", 96 * j, 96 * j + 96))
+        red(col("thr", 0), sl("prt", 0, 96), A.min)
+        red(col("thr", 1), sl("prt", 96, 192), A.max)
+        red(col("thr", 2), sl("prt", 192, 288), A.add, True)
         ts(col("thr", 3), col("thr", 2), col("thr", 1), A.max, col("thr", 0), A.min)
         cut = col("thr", 3)
 
-        act(sl("ysg", 0, C), sl("xc", 0, C), F.Sign, bias=cut, scale=-1.0)
-        act(sl("ysg", C, 2 * C), sl("xc", C, 2 * C), F.Sign, bias=cut, scale=-1.0)
+        act(vw("ysg"), vw("xc"), F.Sign, bias=cut, scale=-1.0)
+        ts(sl("lt", 0, C), sl("xc", 0, C), cut, A.is_lt)
         ts(sl("lt", C, 2 * C), sl("xc", C, 2 * C), cut, A.is_lt)
-        ts(sl("lt", 0, C), sl("ysg", 0, C), 0.0, A.is_gt)
-        ts(sl("le", 0, C), sl("ysg", 0, C), 0.0, A.is_ge)
-        scan(vw("clt"), sl("lt", 0, 512, 2), sl("lt", 1, 512, 2), 0.0, A.add, A.add)
-        ts(sl("le", C, 2 * C), sl("ysg", C, 2 * C), 0.0, A.is_ge)
-        ts(vw("cap"), vw("clt"), col("clt", C - 1), A.subtract, 256.0, A.add)
-        scan(vw("cle"), sl("le", 0, 512, 2), sl("le", 1, 512, 2), 0.0, A.add, A.add)
-        scan(sl("sb", 1, 512, 2), vw("cle"), vw("cap"), 0.0, A.max, A.min)
+        scan(sl("clt", 0, C), sl("lt", 0, C), sl("zero", 0, C), 0.0, A.add, A.add)
+        scan(vw("cap"), sl("lt", 0, 512, 2), sl("lt", 1, 512, 2), -256.0, A.add, A.add)
+        scan(sl("clt", C, 2 * C), sl("lt", C, 2 * C), sl("zero", 0, C), col("clt", C - 1), A.add, A.add)
+        ts(vw("le"), vw("ysg"), 0.0, A.is_ge)
+        ts(vw("cs"), vw("cvec"), col("cap", C - 1), A.add)
+        ts(vw("chalf"), vw("cvec"), col("cap", C - 1), A.add, 0.5, A.add)
+        scan(vw("sb"), vw("le"), vw("clt"), col("cap", C - 1), A.add, A.min)
 
         def kept(a, b):
             return sl("sb", 2 * a + 1, 2 * b, 2)
@@ -467,24 +452,32 @@ def rank_program(g, core, T, topo):
             a, b = (0, 160) if m < 8 else (104, 256)
             act(junk(b - a), kept(a, b), F.Sign, bias=col("chalf", m), scale=-1.0, accum=col("iac", i))
         nv = len(VM)
-        for i in range(nv + 1):
-            if i < nv:
-                m = VM[i]
-                ts(sl("ifl", 136 * i, 136 * i + 136), kept(8 * m, 8 * m + 136), col("cvec", m), A.is_le)
-            if i > 0:
-                j = i - 1
-                scan(sl("isc", 68 * j, 68 * j + 68), sl("ifl", 136 * j, 136 * j + 68),
-                     sl("ifl", 136 * j + 68, 136 * j + 136), float(8 * VM[j]), A.add, A.add)
-            if i == 5:
-                cp(sl(au, 4, 8), sl("isc", 67, 68 * 4, 68))
-                ts(sl(au, 0, 4), sl("iac", 0, 4), 0.5, A.mult, 80.0, A.add)
-                remote(mates[t], T[la][:, 0:8], sl(au, 0, 8), T[au][:, 0:8], "al%d" % t)
+
+        def below(i):
+            ts(sl("ifl", 136 * i, 136 * i + 136), kept(8 * VM[i], 8 * VM[i] + 136), col("cs", VM[i]), A.is_le)
+
+        def tally(j):
+            scan(sl("isc", 68 * j, 68 * j + 68), sl("ifl", 136 * j, 136 * j + 68),
+                 sl("ifl", 136 * j + 68, 136 * j + 136), float(8 * VM[j]), A.add, A.add)
+
+        for i in range(4):
+            below(i)
+        for i in range(4):
+            tally(i)
+        for i in range(4, 8):
+            below(i)
+        cp(sl(au, 4, 8), sl("isc", 67, 68 * 4, 68))
+        ts(sl(au, 0, 4), sl("iac", 0, 4), 0.5, A.mult, 80.0, A.add)
+        remote(mates[t], T[la][:, 0:8], sl(au, 0, 8), T[au][:, 0:8], "al%d" % t)
+        below(8)
+        for i in range(4, nv):
+            tally(i)
         ts(sl(au, 13, 16), sl("iac", 4, 7), 0.5, A.mult, 180.0, A.add)
+        if not last:
+            ts(col(au, 16), col("iac", 0), 0.5, A.mult, 80.0, A.add)
         cp(sl(au, 8, 13), sl("isc", 68 * 4 + 67, 68 * nv, 68))
         remote(mates[t], T[la][:, 8:16], sl(au, 8, 16), T[au][:, 8:16], "am%d" % t)
 
-        if not last:
-            ts(col(au, 16), col("iac", 0), 0.5, A.mult, 80.0, A.add)
         alist = sl(au, 0, nk)
         klist = sl("ku", 0, nk)
 
@@ -507,20 +500,19 @@ def rank_program(g, core, T, topo):
                 act(sl(rw, 512 * b + 256 * h + j, 512 * b + 256 * h + 256, 2), ps((3 + 4 * h + b) % 8, 0, 128),
                     F.Copy, scale=(0.015625, -0.015625)[j])
 
-        ts(sl("sb", 0, 512, 2), sl("sb", 1, 512, 2), -1.0, A.add)
-        zgather("s", 0)
         ts(sl("a2u", 0, nk), alist, 2.0, A.mult)
-        scan(vw("h2"), vw("lob"), vw("sb"), 0.0, A.add, A.max)
+        zgather("s", 0)
         ts(sl("a2", 0, nk), alist, 2.0, A.mult)
-        act(sl("hw", 0, w), ind(vw("h2"), sl("a2u", 0, nk)), F.Copy)
+        if t == 0:
+            ts(vw("latch"), vw("r16"), icol, A.is_le, 1024.0, A.mult)
+        cp(sl("hw", 0, w), ind(vw("sb"), sl("a2u", 0, nk)))
         zgather("s", 1)
+        zgather("s", 2)
         if t == 0:
-            ts(vw("latch"), vw("r16"), icol, A.is_le, 512.0, A.mult)
-        zgather("v", 2)
-        scan(sl("hl", 0, w), sl("latch", 0, w), sl("hw", 0, w), 0.0, A.max, A.min)
-        tt(sl("bitn", 0, nk), sl("hl", 15, w, 16), sl("cvec", 0, nk), A.is_le)
-        if t == 0:
+            ts(vw("latch"), vw("latch"), -512.0, A.add)
             quant(vw("qv"), vw("sv"), vw("vb"))
+        scan(sl("hl", 0, w), sl("latch", 0, w), sl("hw", 0, w), 0.0, A.max, A.min)
+        tt(sl("bitn", 0, nk), sl("hl", 15, w, 16), sl("cs", 0, nk), A.is_le)
         tt(sl("kn", 0, nk), sl("bitn", 0, nk), sl("a2", 0, nk), A.add)
         cp(klist, sl("kn", 0, nk))
 

@@ -28,20 +28,21 @@ for _t in range(ROUNDS + 1):
     _buf("st%d" % _t, _w, "uint8")
 for _t in range(ROUNDS):
     for _n, _c, _d in [("lq", C, X4), ("ls", C, "uint8"), ("la", 16, "uint16"), ("au", 18, "uint16"),
-                       ("dd", 4 * C, "bfloat16"), ("ds", 4 * C, "bfloat16"), ("zz", 4 * CW, "bfloat16"),
-                       ("zs", 4 * C, "bfloat16"), ("qz", C, X4), ("sz", C, "uint8"), ("rw", 8 * C, "float32")]:
+                       ("dd", 4 * C, "bfloat16"), ("ds", 4 * C, "bfloat16"), ("zz", 2 * CW, "bfloat16"),
+                       ("fw", 4 * C, "bfloat16"), ("zs", 4 * C, "bfloat16"), ("qz", C, X4), ("sz", C, "uint8"),
+                       ("rw", 4 * C, "float32")]:
         _buf(_n + str(_t), _c, _d)
 for _d, _l in [
     ("bfloat16", [("ub", 512), ("vb", 512), ("diag", 512), ("eb", 2048), ("latch", CW), ("junk", 2048),
-                  ("lt", 512), ("le", 512), ("ysg", 512), ("clt", 512), ("cap", C), ("sb", 512),
+                  ("lt", 512), ("le", 528), ("ysg", 512), ("clt", 528), ("sb", 528), ("even", C),
                   ("ifl", 136 * len(VM)), ("zero", 512), ("hw", CW), ("hl", CW)]),
     (X4, [("qu", 128), ("qv", 128), ("qus", 128), ("quz", 128), ("qw", 512), ("qe", 512)]),
     ("uint8", [("su", 128), ("sv", 128), ("sus", 128), ("suz", 128), ("sw", 512), ("se", 512)]),
-    ("uint16", [("offs", 16), ("pku", 16), ("a2u", 18), ("ku", 18)]),
+    ("uint16", [("offs", 16), ("pku", 16), ("ku", 18)]),
     ("int32", [("pki", 16)]),
     ("float32", [("tab", 256), ("tabt", 256), ("c16", 17), ("cvec", 17), ("chalf", 17), ("r16", CW), ("mbig", 32),
-                 ("mown", 32), ("mb1", 32), ("horn", 8), ("i512", 512), ("ptr", 512), ("nzn", 16), ("asn", 16),
-                 ("lon", 16), ("hin", 24), ("mw", CW), ("mtr", 512), ("nz", C), ("r0", C), ("r1", C),
+                 ("mown", 32), ("mb1", 32), ("horn", 8), ("i512", 512), ("ptr", 512), ("tri", 48), ("tmul", 48),
+                 ("lo3", 48), ("hi3", 56), ("mw", CW), ("mtr", 512), ("nz", C), ("r0", C), ("r1", C),
                  ("base", C), ("xc", 512), ("s1", 32), ("s2", 32), ("s3", 32), ("s4", 32), ("s5", 32), ("s6", 32),
                  ("s7", 32), ("s8", 32), ("s9", 64), ("mul", 4), ("npv", 20), ("ny", 10), ("cand", 8), ("cs", 17),
                  ("piv", 10), ("yy", 10), ("acc", 10), ("w7", 8), ("e1", 8), ("e2", 8), ("e3", 8), ("e4", 8),
@@ -229,10 +230,8 @@ def rank_program(g, core, T, topo):
     dma("y", T.tt0[:, 0:4 * C], T.x[:], [sl("tt0", 0, 4 * C)], [])
     dma("s", T.tt0[:, 4 * C:4 * CW], T.x[:, 0:4 * (CW - C)], [sl("tt0", 4 * C, 4 * CW)], [])
 
-    iota(sl("diag", 0, C), [[1, C]], 0, -4)
-    iota(sl("diag", C, 2 * C), [[1, C]], C, -4)
     iota(vw("pki"), [[1, 2], [16, 8]], 0, 0, False)
-    tabs = [([[16, 2], [32, 16]], 0), ([[16, 2], [32, 16]], 1), ([[0, 2], [-8, 2], [1, 8]], 8),
+    tabs = [([[16, 2], [32, 16]], 0), ([[16, 2], [32, 16]], 1), ([[0, 2], [-24, 2], [3, 8]], 26),
             ([[0, 2], [4, 4], [-1, 4]], 3), ([[-4, 4], [2, 2], [-1, 2]], 13), ([[8, 2], [-4, 2], [1, 4]], 4),
             ([[0, 2], [1, 16]], 0), ([[1, 2], [0, 16]], 0)]
     for i, (pat, base) in enumerate(tabs):
@@ -241,7 +240,14 @@ def rank_program(g, core, T, topo):
             iota(sl("tab", 32 * i + 16, 32 * i + 32), pat, base)
         else:
             iota(sl("tab", 32 * i, 32 * i + 32), pat, base)
-    ms(sl("hin", 16, 24), BIG)
+    iota(sl("c16", 0, 16), [[16, 16]], 0)
+    iota(vw("diag"), [[1, 512]], 0, -4)
+    ms(sl("hi3", 48, 56), BIG)
+    ms(sl("tri", 0, 48, 3), 0.0)
+    for j in range(3):
+        ms(sl("tmul", j, 48, 3), 1.0 if j else 0.0)
+    ms(col("le", 15), -256.0)
+    ms(col("clt", 15), 1024.0)
     ms(sl("horn", 1, 8, 2), 1.0)
     ms(sl("horn", 0, 8, 2), 2.0)
     ms(vw("zero"), 0.0)
@@ -249,32 +255,39 @@ def rank_program(g, core, T, topo):
     ms(col("mul", 2), B2)
     ms(sl("mul", 1, 4, 2), -1.0)
     ms(col("c16", 16), 0.0)
-    for h in (0, C):
-        for b in range(4):
-            ts(sl("eb", 512 * b + h, 512 * b + h + C), sl("diag", h, h + C), float(b), A.is_equal)
     cp(vw("pku"), vw("pki"))
-    quant(vw("qe"), vw("se"), vw("eb"))
+    ms(sl("tab", 72, 75, 2), 48.0)
+    ms(sl("tab", 88, 91, 2), 48.0)
     quant(vw("qu"), vw("su"), vw("ub"))
     dma("y", T.qw[:].bitcast(dt.uint8), T.wc[:], [vw("qw")], [vw("ub")])
     dma("y", T.sw[:], T.ws[:], [vw("sw")], [])
     dma("y", T.vb[:], T.v[:], [vw("vb")], [])
-    iota(sl("c16", 0, 16), [[16, 16]], 0)
     icol = col("tabt", 192)
     hcol = col("tabt", 224)
     o_s, o_z, o_1, o_3, o_6, o_8 = [col("offs", 2 * i) for i in range(6)]
+    late = [lambda b=b: ts(sl("eb", 512 * b, 512 * b + 512), vw("diag"), float(b), A.is_equal) for b in range(4)]
+    late.append(lambda: ts(vw("latch"), vw("r16"), icol, A.is_le, 1024.0, A.mult))
+    late += [lambda b=b: quant(sl("qe", 128 * b, 128 * b + 128), sl("se", 128 * b, 128 * b + 128),
+                               sl("eb", 512 * b, 512 * b + 512)) for b in range(4)]
+    late.append(lambda: ts(vw("latch"), vw("latch"), -512.0, A.add))
+    late.append(lambda: quant(vw("qv"), vw("sv"), vw("vb")))
 
-    def decode(src_q, src_s, dst):
+    def later():
+        if late:
+            late.pop(0)()
+
+    def decode(src_q, src_s, dst, up=None):
         for b in range(4):
             mm(3 + b, C, sl("qe", 128 * b, 128 * b + 128), sl("se", 128 * b, 128 * b + 128), src_q, src_s)
         for b in range(4):
-            act(sl(dst, C * b, C * b + C), ps(3 + b, 0, C), F.Copy)
+            act(sl(dst, C * b, C * b + C), ps(3 + b, 0, C), F.Copy, scale=up if b > 1 else None)
 
     for t in range(ROUNDS):
         last = t == ROUNDS - 1
         w = C if last else CW
         nk = w // 16
         qt, st, au, la = "qt%d" % t, "st%d" % t, "au%d" % t, "la%d" % t
-        dd, ds, zz, zs, rw = "dd%d" % t, "ds%d" % t, "zz%d" % t, "zs%d" % t, "rw%d" % t
+        dd, ds, zz, zs, rw, fw = [n + str(t) for n in ("dd", "ds", "zz", "zs", "rw", "fw")]
         if t == 0:
             cp((T.quz[:].bitcast(dt.uint32),) + vw("quz")[1:], ind(vw("qu"), sl("pku", 8, 16), dt.uint32))
             act(vw("suz"), ind(vw("su"), sl("pku", 8, 16)), F.Copy)
@@ -284,8 +297,6 @@ def rank_program(g, core, T, topo):
         mm(1, C, vw("quz"), vw("suz"), sl(qt, 0, C), sl(st, 0, C))
         if t == 0:
             cp((T.qus[:].bitcast(dt.uint32),) + vw("qus")[1:], ind(vw("qu"), sl("pku", 0, 8), dt.uint32))
-            ms(sl("tab", 72, 75, 2), 16.0)
-            ms(sl("tab", 88, 91, 2), 16.0)
         mm(2, C, vw("qus"), vw("sus"), sl(qt, 0, C), sl(st, 0, C))
         remote(mates[t], T["lq%d" % t][:].bitcast(dt.uint8), sl(qt, 0, C), T[qt][:, 0:C].bitcast(dt.uint8), "aq%d" % t)
         remote(mates[t], T["ls%d" % t][:], sl(st, 0, C), T[st][:, 0:C], "aq%d" % t)
@@ -294,8 +305,8 @@ def rank_program(g, core, T, topo):
             iota(vw("i512"), [[1, 512]], 0)
 
         bs = "nz" if t == 0 else "base"
-        lo = "nzn" if t == 0 else "lon"
         if t > 0:
+            tr(sl("mtr", 0, C), sl("mw", 0, C))
             tr(sl("mtr", C, 2 * C), sl("mw", 16, CW))
         else:
             tr(vw("tabt"), vw("tab"))
@@ -319,16 +330,15 @@ def rank_program(g, core, T, topo):
                 fill.pop(0)()
 
         if t > 0:
-            filler()
-        ts(vw("nzn"), ind(vw("ptr"), o_z), -1.0, A.mult, 0.0, A.max)
-        act(vw("asn"), ind(vw("ptr"), o_s), F.Abs)
+            cp(sl("tri", 0, 48, 3), ind(vw("mtr"), o_s))
+        ts(sl("tri", 1, 48, 3), ind(vw("ptr"), o_z), -1.0, A.mult, 0.0, A.max)
+        act(sl("tri", 2, 48, 3), ind(vw("ptr"), o_s), F.Abs)
         act(vw("r1"), ps(2, 0, C), F.Relu)
-        if t > 0:
-            filler()
-            tt(vw("lon"), ind(vw("mtr"), o_s), vw("nzn"), A.add)
         filler()
-        tt(sl("hin", 0, 16), vw(lo), vw("asn"), A.add)
-        decode(sl(qt, 0, C), sl(st, 0, C), dd)
+        scan(sl("hi3", 0, 48), vw("tmul"), vw("tri"), 0.0, A.mult, A.add)
+        scan(vw("lo3"), vw("tmul"), vw("tri"), 0.0, A.mult, A.add)
+        if t > 0:
+            decode(sl(qt, 0, C), sl(st, 0, C), dd, 64.0)
 
         def halves(name):
             return sl(name, 0, 16), sl(name, 16, 32)
@@ -342,9 +352,10 @@ def rank_program(g, core, T, topo):
             filler()
 
         filler()
-        step(turns("s1"), ind(vw("hin"), o_1), vw(lo))
+        step(turns("s1"), ind(vw("hi3"), o_1), sl("lo3", 1, 48, 3))
         step(halves("s2"), *halves("s1"))
         step(halves("s3"), ind(sl("s2", 16, 32), o_3), sl("s2", 0, 16))
+        step(halves("s4"), *turns("s3"))
 
         def count(i, pv=None):
             if pv is None:
@@ -360,18 +371,21 @@ def rank_program(g, core, T, topo):
             ts(out, y, a, A.max, b, A.min)
 
         for i in range(2):
-            count(6 + i, col("hin", 2 * i))
-        fill.append(lambda: cp(sl("piv", 6, 8), sl("hin", 0, 3, 2)))
+            count(6 + i, col("hi3", 2 + 6 * i))
+        cp(sl("piv", 6, 8), sl("hi3", 2, 9, 6))
         if t == 0:
             fill.append(lambda: ts(vw("mbig"), sl("tab", 224, 256), hcol, A.not_equal, BIG, A.mult))
             fill.append(lambda: ts(vw("mown"), sl("tab", 224, 256), hcol, A.is_equal, BIG, A.mult))
             fill.append(lambda: ts(vw("mb1"), sl("tab", 224, 256), hcol, A.is_equal, B1, A.mult))
             fill.append(lambda: ts(vw("cvec"), vw("c16"), icol, A.add))
-        step(halves("s4"), *turns("s3"))
         step(turns("s5"), *turns("s4"))
+        later()
         step(turns("s6"), ind(sl("s5", 16, 32), o_6), sl("s5", 0, 16))
+        later()
         step(turns("s7"), *halves("s6"))
+        later()
         step(turns("s8"), ind(sl("s7", 16, 32), o_8), sl("s7", 0, 16))
+        later()
 
         for l in range(2):
             o = 16 * l
@@ -379,8 +393,11 @@ def rank_program(g, core, T, topo):
             count(l, col("s9", o + 7))
             tt(sl("s9", o, o + 16, 2), sl("s8", o, o + 8), sl("s8", o + 8, o + 16), A.min)
         ts(sl("yy", 6, 8), sl("acc", 6, 8), -B2 / 2, A.mult, -0.25 * B2, A.add)
+        later()
         ts(sl("s9", 32, 64), sl("s9", 0, 32), -1.0, A.mult)
         cp(sl("piv", 0, 2), sl("s9", 7, 32, 16))
+        later()
+        later()
         for k in range(3):
             for l in range(2):
                 i, o = 2 * k + l, 16 * l
@@ -396,6 +413,8 @@ def rank_program(g, core, T, topo):
                 filler()
                 y, ny = col("yy", i), col("ny", i)
                 if k == 0:
+                    if l == 0:
+                        later()
                     clamp(col("cand", 2 * l), y, col("s9", o + 1), col("s9", o + 9))
                     clamp(col("cand", 2 * l + 1), ny, col("s9", 32 + o + 13), col("s9", 32 + o + 5))
                     clamp(col("w7", 4 * l), y, col("s9", o), col("s9", o + 8))
@@ -403,10 +422,14 @@ def rank_program(g, core, T, topo):
                         fill.append(lambda d=4 * l + 1 + j, yc=yc, a=a, b=b: clamp(col("w7", d), yc, col("s9", a), col("s9", b)))
                 elif k == 1:
                     filler()
+                    if l:
+                        later()
                     clamp(col("cand", 4 + 2 * l), y, col("w7", 4 * l), col("w7", 4 * l + 1))
                     clamp(col("cand", 5 + 2 * l), ny, col("w7", 4 * l + 2), col("w7", 4 * l + 3))
                 elif l == 0:
                     ts(sl("piv", 2, 6), sl("npv", 5, 12, 2), -1.0, A.mult)
+                    later()
+                    later()
         ts(sl("piv", 8, 10), sl("npv", 17, 20, 2), -1.0, A.mult)
         tt(vw("e1"), sl("piv", 0, 8), sl("yy", 0, 8), A.max)
         tt(vw("e2"), sl("piv", 0, 8), sl("yy", 0, 8), A.min)
@@ -434,23 +457,25 @@ def rank_program(g, core, T, topo):
         ts(col("thr", 3), col("thr", 2), col("thr", 1), A.max, col("thr", 0), A.min)
         cut = col("thr", 3)
 
-        act(vw("ysg"), vw("xc"), F.Sign, bias=cut, scale=-1.0)
-        ts(sl("lt", 0, C), sl("xc", 0, C), cut, A.is_lt)
-        ts(sl("lt", C, 2 * C), sl("xc", C, 2 * C), cut, A.is_lt)
-        scan(sl("clt", 0, C), sl("lt", 0, C), sl("zero", 0, C), 0.0, A.add, A.add)
-        scan(vw("cap"), sl("lt", 0, 512, 2), sl("lt", 1, 512, 2), -256.0, A.add, A.add)
-        scan(sl("clt", C, 2 * C), sl("lt", C, 2 * C), sl("zero", 0, C), col("clt", C - 1), A.add, A.add)
-        ts(vw("le"), vw("ysg"), 0.0, A.is_ge)
-        ts(vw("cs"), vw("cvec"), col("cap", C - 1), A.add)
-        ts(vw("chalf"), vw("cvec"), col("cap", C - 1), A.add, 0.5, A.add)
-        scan(vw("sb"), vw("le"), vw("clt"), col("cap", C - 1), A.add, A.min)
+        for h in (0, C):
+            act(sl("ysg", h, h + C), sl("xc", h, h + C), F.Sign, bias=cut, scale=-1.0)
+        if t == 0:
+            decode(sl(qt, 0, C), sl(st, 0, C), dd, 64.0)
+        ts(vw("lt"), vw("xc"), cut, A.is_lt)
+        ts(sl("le", 16, 16 + C), sl("ysg", 0, C), 0.0, A.is_ge)
+        ts(sl("le", 16 + C, 528), sl("ysg", C, 2 * C), 0.0, A.is_ge)
+        scan(sl("clt", 16, 528), vw("lt"), vw("zero"), 0.0, A.add, A.add)
+        scan(sl("sb", 15, 528), sl("le", 15, 528), sl("clt", 15, 528), col("clt", 527), A.add, A.min)
+        ts(vw("chalf"), vw("cvec"), col("clt", 527), A.add, -255.5, A.add)
+        ts(vw("cs"), vw("cvec"), col("clt", 527), A.add, -256.0, A.add)
 
         def kept(a, b):
-            return sl("sb", 2 * a + 1, 2 * b, 2)
+            return sl("sb", 17 + 2 * a, 16 + 2 * b, 2)
 
         for i, m in enumerate(SM):
             a, b = (0, 160) if m < 8 else (104, 256)
             act(junk(b - a), kept(a, b), F.Sign, bias=col("chalf", m), scale=-1.0, accum=col("iac", i))
+        act(vw("even"), sl("sb", 16, 528, 2), F.Copy)
         nv = len(VM)
 
         def below(i):
@@ -481,18 +506,14 @@ def rank_program(g, core, T, topo):
         alist = sl(au, 0, nk)
         klist = sl("ku", 0, nk)
 
-        def zgather(q, b):
-            pick(q, sl(zz, CW * b, CW * b + w), ind(sl(dd, C * b, C * b + C), alist))
-
-        def mosaic(h):
-            for b in range(4):
-                pick("vs"[b % 2], sl(zs, 512 * h + b, 512 * h + 512, 4),
-                     ind(sl(ds, C * b, C * b + C), sl(la, 8 * h, 8 * h + 8)))
+        def mosaic(h, b):
+            pick("vs"[b % 2], sl(zs, 512 * h + b, 512 * h + 512, 4),
+                 ind(sl(ds, C * b, C * b + C), sl(la, 8 * h, 8 * h + 8)))
 
         def product(h):
             q, s = sl("qz%d" % t, 128 * h, 128 * h + 128), sl("sz%d" % t, 128 * h, 128 * h + 128)
             quant(q, s, sl(zs, 512 * h, 512 * h + 512))
-            for b in range(4):
+            for b in (0, 2, 1, 3):
                 mm((3 + 4 * h + b) % 8, 128, sl("qw", 128 * b, 128 * b + 128), sl("sw", 128 * b, 128 * b + 128), q, s)
 
         def signed(b, h):
@@ -500,46 +521,44 @@ def rank_program(g, core, T, topo):
                 act(sl(rw, 512 * b + 256 * h + j, 512 * b + 256 * h + 256, 2), ps((3 + 4 * h + b) % 8, 0, 128),
                     F.Copy, scale=(0.015625, -0.015625)[j])
 
-        ts(sl("a2u", 0, nk), alist, 2.0, A.mult)
-        zgather("s", 0)
+        def both(b, h):
+            for j in range(2):
+                tt(sl(fw, 512 * (b - 2) + 256 * h + j, 512 * (b - 2) + 256 * h + 256, 2),
+                   sl(dd, C * b + 128 * h, C * b + 128 * h + 128), ps((3 + 4 * h + b) % 8, 0, 128), (A.add, A.subtract)[j])
+
+        cp(sl("hw", 0, w), ind(vw("even"), alist))
         ts(sl("a2", 0, nk), alist, 2.0, A.mult)
-        if t == 0:
-            ts(vw("latch"), vw("r16"), icol, A.is_le, 1024.0, A.mult)
-        cp(sl("hw", 0, w), ind(vw("sb"), sl("a2u", 0, nk)))
-        zgather("s", 1)
-        zgather("s", 2)
-        if t == 0:
-            ts(vw("latch"), vw("latch"), -512.0, A.add)
-            quant(vw("qv"), vw("sv"), vw("vb"))
+        for b in range(2):
+            act(sl(zz, CW * b, CW * b + w), ind(sl(dd, C * b, C * b + C), alist), F.Copy)
         scan(sl("hl", 0, w), sl("latch", 0, w), sl("hw", 0, w), 0.0, A.max, A.min)
         tt(sl("bitn", 0, nk), sl("hl", 15, w, 16), sl("cs", 0, nk), A.is_le)
-        tt(sl("kn", 0, nk), sl("bitn", 0, nk), sl("a2", 0, nk), A.add)
-        cp(klist, sl("kn", 0, nk))
 
-        mosaic(0)
+        mosaic(0, 0)
+        mosaic(0, 1)
+        tt(sl("kn", 0, nk), sl("bitn", 0, nk), sl("a2", 0, nk), A.add)
+        mosaic(0, 2)
+        mosaic(0, 3)
+        cp(klist, sl("kn", 0, nk))
         product(0)
+        for b in range(4):
+            mosaic(1, b)
+        product(1)
         pick("s", sl("mw", 0, w), ind(vw("xc"), klist))
         if last:
             dma("y", T.ml[:], T.mw[0:128:16, 0:C], [], [vw("mw")])
-        mosaic(1)
-        product(1)
-        for b in range(3):
-            signed(b, 0)
-        zgather("v", 3)
-        if not last:
-            tr(sl("mtr", 0, C), sl("mw", 0, C))
-        for b in range(4):
-            if b > 2:
-                signed(b, 0)
-            signed(b, 1)
+        for h in range(2):
+            for b in range(2):
+                signed(b, h)
+                both(b + 2, h)
+        for b in range(2):
             tt(sl("tt%d" % (t + 1), b, 4 * w, 4), ind(sl(rw, 512 * b, 512 * b + 512), klist),
                sl(zz, CW * b, CW * b + w), A.add)
-        if last:
-            act(vw("kw"), ind(vw("i512"), klist), F.Copy)
-            dma("y", T.kl[:], T.kw[0:128:16, 0:C], [], [vw("kw")])
+            act(sl("tt%d" % (t + 1), b + 2, 4 * w, 4), ind(sl(fw, 512 * b, 512 * b + 512), klist), F.Copy, scale=0.015625)
 
     qt, st = "qt%d" % ROUNDS, "st%d" % ROUNDS
     quant(vw(qt), vw(st), vw("tt%d" % ROUNDS))
+    act(vw("kw"), ind(vw("i512"), sl("ku", 0, 16)), F.Copy)
+    dma("y", T.kl[:], T.kw[0:128:16, 0:C], [], [vw("kw")])
     for h in range(2):
         mm(h, 128, vw("qv"), vw("sv"), sl(qt, 128 * h, 128 * h + 128), sl(st, 128 * h, 128 * h + 128))
     dma("y", T.oc[:], T[qt][:].bitcast(dt.uint8), [], [vw(qt)])

@@ -7,10 +7,13 @@ CW = 272
 ROUNDS = 3
 PARTNER = [1, 2, 4]
 BIG = 2.0 ** 76
-B1 = 2.0 ** 74
+B1 = 2.0 ** 78
 B2 = 2.0 ** 84
 SM = [0, 1, 2, 3, 13, 14, 15]
 VM = [4, 5, 6, 7, 8, 9, 10, 11, 12]
+LW = 17
+YW = 26
+LS = 40
 
 X4 = "float8_e4m3fn_x4"
 SCRATCH = {}
@@ -33,21 +36,21 @@ for _t in range(ROUNDS):
                        ("rw", 4 * C, "float32")]:
         _buf(_n + str(_t), _c, _d)
 for _d, _l in [
-    ("bfloat16", [("ub", 512), ("vb", 512), ("diag", 512), ("eb", 2048), ("latch", CW), ("junk", 2048),
-                  ("lt", 512), ("le", 528), ("ysg", 512), ("clt", 528), ("sb", 528), ("even", C),
-                  ("ifl", 136 * len(VM)), ("zero", 512), ("hw", CW), ("hl", CW)]),
+    ("bfloat16", [("ub", 512), ("vb", 512), ("eb", 516), ("ones", 516), ("latch", CW), ("junk", 2048),
+                  ("lt", 512), ("le", 528), ("ysg", 512), ("clt", 528), ("sb", 528),
+                  ("ifl", 136 * len(VM)), ("isc", 68 * len(VM)), ("cs", 18), ("hw", CW), ("hl", CW)]),
     (X4, [("qu", 128), ("qv", 128), ("qus", 128), ("quz", 128), ("qw", 512), ("qe", 512)]),
     ("uint8", [("su", 128), ("sv", 128), ("sus", 128), ("suz", 128), ("sw", 512), ("se", 512)]),
-    ("uint16", [("offs", 16), ("pku", 16), ("ku", 18)]),
+    ("uint16", [("offs", 16), ("pku", 16), ("ku", 18), ("a2u", 18)]),
     ("int32", [("pki", 16)]),
     ("float32", [("tab", 256), ("tabt", 256), ("c16", 17), ("cvec", 17), ("chalf", 17), ("r16", CW), ("mbig", 32),
-                 ("mown", 32), ("mb1", 32), ("horn", 8), ("i512", 512), ("ptr", 512), ("tri", 48), ("tmul", 48),
-                 ("lo3", 48), ("hi3", 56), ("mw", CW), ("mtr", 512), ("nz", C), ("r0", C), ("r1", C),
+                 ("mown", 32), ("mb1", 32), ("horn", 9), ("i512", 516), ("pcol", 1), ("ptr", 512), ("tri", 48),
+                 ("tmul", 48), ("hi3", 56), ("lo3", 48), ("mw", CW), ("mtr", 512), ("nz", C), ("r0", C), ("r1", C),
                  ("base", C), ("xc", 512), ("s1", 32), ("s2", 32), ("s3", 32), ("s4", 32), ("s5", 32), ("s6", 32),
-                 ("s7", 32), ("s8", 32), ("s9", 64), ("mul", 4), ("npv", 20), ("ny", 10), ("cand", 8), ("cs", 17),
-                 ("piv", 10), ("yy", 10), ("acc", 10), ("w7", 8), ("e1", 8), ("e2", 8), ("e3", 8), ("e4", 8),
-                 ("fin", 8), ("prep", 288), ("prt", 288), ("thr", 4), ("isc", 68 * len(VM)), ("iac", 8),
-                 ("a2", 17), ("bitn", 17), ("kn", 17), ("kw", C), ("yo", C)]),
+                 ("s7", 32), ("s8", 32), ("s9", 2 * LS), ("med", 8), ("tw", 2 * LS), ("w9", 2 * LS), ("w5", 7 * LS),
+                 ("side", 9), ("yv", 10 * YW), ("kvec", YW), ("mul", 4), ("npv", 20), ("madd", 32), ("nsum", 65),
+                 ("nmul", 65), ("piv", 10), ("acc", 10), ("e3", 9), ("e4", 9), ("fin", 2), ("prep", 192),
+                 ("prt", 193), ("cut", 64), ("iac", 8), ("a2", 17), ("bitn", 17), ("kn", 17), ("kw", C), ("yo", C)]),
 ]:
     for _n, _c in _l:
         if _c <= 96 and _d == "float32":
@@ -57,7 +60,7 @@ for _d, _l in [
 _buf("pool", sum(-(-_v[1] // 8) * 8 for _v in POOL.values()), "float32")
 _buf("ps", 4096, "float32", "psum")
 
-SEMAPHORES = ["cv", "cs", "ct", "cg", "loc"] + ["d%d" % _i for _i in range(16)] \
+SEMAPHORES = ["cv", "cs", "ct", "cg", "loc"] + ["d%d" % _i for _i in range(20)] \
     + [_n + str(_i) for _n in ("aq", "al", "am") for _i in range(ROUNDS)]
 
 
@@ -165,8 +168,8 @@ def rank_program(g, core, T, topo):
     def scan(out, d0, d1, init, o0, o1):
         op("v", lambda: g.vector.tensor_tensor_scan(out[0], d0[0], d1[0], ap(init), o0, o1), [out], [d0, d1, init])
 
-    def red(out, a, o, neg=False):
-        op("v", lambda: g.vector.tensor_reduce(out[0], a[0], AxisListType.X, o, negate=neg), [out], [a])
+    def red(out, a, o):
+        op("v", lambda: g.vector.tensor_reduce(out[0], a[0], AxisListType.X, o), [out], [a])
 
     def tr(out, a):
         op("v", lambda: g.vector.transpose(out[0], a[0]), [out], [a])
@@ -230,6 +233,7 @@ def rank_program(g, core, T, topo):
     dma("y", T.tt0[:, 0:4 * C], T.x[:], [sl("tt0", 0, 4 * C)], [])
     dma("s", T.tt0[:, 4 * C:4 * CW], T.x[:, 0:4 * (CW - C)], [sl("tt0", 4 * C, 4 * CW)], [])
 
+    iota(vw("pcol"), [[0, 1]], 3, 4)
     iota(vw("pki"), [[1, 2], [16, 8]], 0, 0, False)
     tabs = [([[16, 2], [32, 16]], 0), ([[16, 2], [32, 16]], 1), ([[0, 2], [-24, 2], [3, 8]], 26),
             ([[0, 2], [4, 4], [-1, 4]], 3), ([[-4, 4], [2, 2], [-1, 2]], 13), ([[8, 2], [-4, 2], [1, 4]], 4),
@@ -241,46 +245,60 @@ def rank_program(g, core, T, topo):
         else:
             iota(sl("tab", 32 * i, 32 * i + 32), pat, base)
     iota(sl("c16", 0, 16), [[16, 16]], 0)
-    iota(vw("diag"), [[1, 512]], 0, -4)
+    ms(vw("ones"), 1.0)
     ms(sl("hi3", 48, 56), BIG)
+    ms(vw("tmul"), 1.0)
     ms(sl("tri", 0, 48, 3), 0.0)
-    for j in range(3):
-        ms(sl("tmul", j, 48, 3), 1.0 if j else 0.0)
-    ms(col("le", 15), -256.0)
-    ms(col("clt", 15), 1024.0)
-    ms(sl("horn", 1, 8, 2), 1.0)
-    ms(sl("horn", 0, 8, 2), 2.0)
-    ms(vw("zero"), 0.0)
-    ms(col("mul", 0), -B2)
-    ms(col("mul", 2), B2)
-    ms(sl("mul", 1, 4, 2), -1.0)
-    ms(col("c16", 16), 0.0)
+    scan(vw("i512"), vw("ones"), vw("ones"), -1.0, A.mult, A.add)
+    ms(sl("tmul", 0, 48, 3), 0.0)
     cp(vw("pku"), vw("pki"))
-    ms(sl("tab", 72, 75, 2), 48.0)
-    ms(sl("tab", 88, 91, 2), 48.0)
+    ts(vw("eb"), vw("i512"), vw("pcol"), A.is_equal)
+    early = [lambda b=b: quant(sl("qe", 128 * b, 128 * b + 128), sl("se", 128 * b, 128 * b + 128),
+                               sl("eb", 3 - b, 515 - b)) for b in range(4)]
+    ms(vw("s9"), 0.0)
+    ms(vw("mul"), -1.0)
+    ms(sl("kvec", 0, LW), B2)
+    early[0]()
     quant(vw("qu"), vw("su"), vw("ub"))
     dma("y", T.qw[:].bitcast(dt.uint8), T.wc[:], [vw("qw")], [vw("ub")])
     dma("y", T.sw[:], T.ws[:], [vw("sw")], [])
     dma("y", T.vb[:], T.v[:], [vw("vb")], [])
+    early[1]()
+    ms(sl("tab", 72, 75, 2), 48.0)
+    cp((T.quz[:].bitcast(dt.uint32),) + vw("quz")[1:], ind(vw("qu"), sl("pku", 8, 16), dt.uint32))
+    act(vw("suz"), ind(vw("su"), sl("pku", 8, 16)), F.Copy)
+    act(vw("sus"), ind(vw("su"), sl("pku", 0, 8)), F.Copy)
+    cp((T.qus[:].bitcast(dt.uint32),) + vw("qus")[1:], ind(vw("qu"), sl("pku", 0, 8), dt.uint32))
+    ms(sl("tab", 88, 91, 2), 48.0)
     icol = col("tabt", 192)
     hcol = col("tabt", 224)
-    o_s, o_z, o_1, o_3, o_6, o_8 = [col("offs", 2 * i) for i in range(6)]
-    late = [lambda b=b: ts(sl("eb", 512 * b, 512 * b + 512), vw("diag"), float(b), A.is_equal) for b in range(4)]
-    late.append(lambda: ts(vw("latch"), vw("r16"), icol, A.is_le, 1024.0, A.mult))
-    late += [lambda b=b: quant(sl("qe", 128 * b, 128 * b + 128), sl("se", 128 * b, 128 * b + 128),
-                               sl("eb", 512 * b, 512 * b + 512)) for b in range(4)]
-    late.append(lambda: ts(vw("latch"), vw("latch"), -512.0, A.add))
-    late.append(lambda: quant(vw("qv"), vw("sv"), vw("vb")))
+    o_s, o_z, o_1, o_3, o_6, o_8, o_r = [col("offs", 2 * i) for i in range(7)]
+    late = [lambda: ts(o_r, icol, -1.0, A.mult, 16.0, A.add), lambda: ms(col("mul", 0), -B2),
+            lambda: ms(col("mul", 2), B2), lambda: ms(sl("kvec", LW, YW), -B2),
+            lambda: ms(vw("nmul"), 1.0), lambda: ms(col("prt", 192), 0.0),
+            lambda: ts(vw("madd"), sl("tab", 224, 256), hcol, A.not_equal, -1024.0, A.mult),
+            lambda: ts(vw("mbig"), sl("tab", 224, 256), hcol, A.not_equal, BIG, A.mult),
+            lambda: ts(vw("mown"), sl("tab", 224, 256), hcol, A.is_equal, BIG, A.mult),
+            lambda: ts(vw("mb1"), sl("tab", 224, 256), hcol, A.is_equal),
+            lambda: ms(vw("horn"), 1.0), lambda: ms(vw("side"), 0.5), lambda: ms(col("c16", 16), 0.0),
+            lambda: ms(col("nmul", 64), -B1), lambda: ms(sl("horn", 2, 7, 4), -2.0),
+            lambda: ms(col("horn", 4), 2.0), lambda: ms(col("horn", 8), -1.0), lambda: ms(sl("side", 0, 2), -0.5),
+            lambda: ms(sl("side", 6, 8), -0.5), lambda: ts(vw("cvec"), vw("c16"), icol, A.add),
+            lambda: ms(col("le", 15), -256.0), lambda: ms(col("clt", 15), 1024.0),
+            lambda: quant(vw("qv"), vw("sv"), vw("vb")),
+            lambda: ts(vw("latch"), vw("r16"), icol, A.is_le, 1024.0, A.mult)]
 
-    def later():
-        if late:
-            late.pop(0)()
+    def later(n=1):
+        for _ in range(n):
+            if late:
+                late.pop(0)()
 
-    def decode(src_q, src_s, dst, up=None):
+    def unpack(src_q, src_s):
         for b in range(4):
             mm(3 + b, C, sl("qe", 128 * b, 128 * b + 128), sl("se", 128 * b, 128 * b + 128), src_q, src_s)
-        for b in range(4):
-            act(sl(dst, C * b, C * b + C), ps(3 + b, 0, C), F.Copy, scale=up if b > 1 else None)
+
+    def fetch(dst, b, up=None):
+        act(sl(dst, C * b, C * b + C), ps(3 + b, 0, C), F.Copy, scale=up if b > 1 else None)
 
     for t in range(ROUNDS):
         last = t == ROUNDS - 1
@@ -288,21 +306,19 @@ def rank_program(g, core, T, topo):
         nk = w // 16
         qt, st, au, la = "qt%d" % t, "st%d" % t, "au%d" % t, "la%d" % t
         dd, ds, zz, zs, rw, fw = [n + str(t) for n in ("dd", "ds", "zz", "zs", "rw", "fw")]
-        if t == 0:
-            cp((T.quz[:].bitcast(dt.uint32),) + vw("quz")[1:], ind(vw("qu"), sl("pku", 8, 16), dt.uint32))
-            act(vw("suz"), ind(vw("su"), sl("pku", 8, 16)), F.Copy)
-            act(vw("sus"), ind(vw("su"), sl("pku", 0, 8)), F.Copy)
-        quant(vw(qt), vw(st), vw("tt%d" % t))
-        mm(0, CW, vw("qu"), vw("su"), vw(qt), vw(st))
+        quant(sl(qt, 0, 144), sl(st, 0, 144), sl("tt%d" % t, 0, 4 * 144))
+        quant(sl(qt, 144, CW), sl(st, 144, CW), sl("tt%d" % t, 4 * 144, 4 * CW))
+        mm(0, 144, vw("qu"), vw("su"), sl(qt, 0, 144), sl(st, 0, 144))
+        mm(7, 144, vw("qu"), vw("su"), sl(qt, 128, CW), sl(st, 128, CW))
         mm(1, C, vw("quz"), vw("suz"), sl(qt, 0, C), sl(st, 0, C))
-        if t == 0:
-            cp((T.qus[:].bitcast(dt.uint32),) + vw("qus")[1:], ind(vw("qu"), sl("pku", 0, 8), dt.uint32))
         mm(2, C, vw("qus"), vw("sus"), sl(qt, 0, C), sl(st, 0, C))
         remote(mates[t], T["lq%d" % t][:].bitcast(dt.uint8), sl(qt, 0, C), T[qt][:, 0:C].bitcast(dt.uint8), "aq%d" % t)
         remote(mates[t], T["ls%d" % t][:], sl(st, 0, C), T[st][:, 0:C], "aq%d" % t)
         if t == 0:
             iota(vw("r16"), [[0, CW // 16], [1, 16]], 0)
-            iota(vw("i512"), [[1, 512]], 0)
+            early[2]()
+            early[3]()
+        unpack(sl(qt, 0, C), sl(st, 0, C))
 
         bs = "nz" if t == 0 else "base"
         if t > 0:
@@ -311,11 +327,12 @@ def rank_program(g, core, T, topo):
         else:
             tr(vw("tabt"), vw("tab"))
         act(vw("nz"), ps(1, 0, C), F.Relu, scale=-1.0)
-        tr(sl("ptr", 0, C), ps(0, 0, C))
+        tr(sl("ptr", 0, 128), ps(0, 0, 128))
+        tr(sl("ptr", C, C + 128), ps(0, 16, 144))
         if t == 0:
             cp(sl("offs", 0, 12, 2), sl("tabt", 0, 192, 32))
-        tr(sl("ptr", C, 2 * C), ps(0, 16, CW))
-        act(vw("r0"), ps(2, 0, C), F.Relu, scale=-1.0)
+        tr(sl("ptr", 128, C), ps(7, 0, 128))
+        tr(sl("ptr", C + 128, 2 * C), ps(7, 16, 144))
         fill = []
         if t > 0:
             for h in (0, 128):
@@ -325,20 +342,30 @@ def rank_program(g, core, T, topo):
                 fill.append(lambda j=j, r=r, h=h: tt(sl("xc", 2 * h + j, 2 * h + 256, 2), sl(bs, h, h + 128),
                                                      sl(r, h, h + 128), A.add))
 
-        def filler():
-            if fill:
-                fill.pop(0)()
+        def filler(n=1):
+            for _ in range(n):
+                if fill:
+                    fill.pop(0)()
 
         if t > 0:
             cp(sl("tri", 0, 48, 3), ind(vw("mtr"), o_s))
+        else:
+            later(3)
         ts(sl("tri", 1, 48, 3), ind(vw("ptr"), o_z), -1.0, A.mult, 0.0, A.max)
         act(sl("tri", 2, 48, 3), ind(vw("ptr"), o_s), F.Abs)
+        act(vw("r0"), ps(2, 0, C), F.Relu, scale=-1.0)
         act(vw("r1"), ps(2, 0, C), F.Relu)
-        filler()
-        scan(sl("hi3", 0, 48), vw("tmul"), vw("tri"), 0.0, A.mult, A.add)
-        scan(vw("lo3"), vw("tmul"), vw("tri"), 0.0, A.mult, A.add)
         if t > 0:
-            decode(sl(qt, 0, C), sl(st, 0, C), dd, 64.0)
+            filler()
+        else:
+            later(3)
+        scan(sl("hi3", 0, 48), vw("tmul"), vw("tri"), 0.0, A.mult, A.add)
+        if t > 0:
+            scan(vw("lo3"), vw("tmul"), vw("tri"), 0.0, A.mult, A.add)
+            filler()
+        for b in range(4):
+            fetch(dd, b, 64.0)
+        unpack(vw("lq%d" % t), vw("ls%d" % t))
 
         def halves(name):
             return sl(name, 0, 16), sl(name, 16, 32)
@@ -349,13 +376,6 @@ def rank_program(g, core, T, topo):
         def step(dst, a, b):
             tt(dst[0], a, b, A.min)
             tt(dst[1], a, b, A.max)
-            filler()
-
-        filler()
-        step(turns("s1"), ind(vw("hi3"), o_1), sl("lo3", 1, 48, 3))
-        step(halves("s2"), *halves("s1"))
-        step(halves("s3"), ind(sl("s2", 16, 32), o_3), sl("s2", 0, 16))
-        step(halves("s4"), *turns("s3"))
 
         def count(i, pv=None):
             if pv is None:
@@ -363,111 +383,101 @@ def rank_program(g, core, T, topo):
             else:
                 act(junk(512), vw("xc"), F.Sign, bias=pv, scale=-1.0, accum=col("acc", i))
 
-        def why(i, neg=False):
-            sg = (-1.0 if i < 2 else 1.0) * (-1.0 if neg else 1.0)
-            ts(col("ny" if neg else "yy", i), col("acc", i), sg * B2 / 2, A.mult, (0.25 if neg else -0.25) * B2, A.add)
+        def why(i, n):
+            ts(sl("yv", YW * i, YW * i + n), sl("kvec", 0, n), col("acc", i), A.mult, -1.0 if i < 2 else 1.0, A.mult)
 
-        def clamp(out, y, a, b):
-            ts(out, y, a, A.max, b, A.min)
-
-        for i in range(2):
-            count(6 + i, col("hi3", 2 + 6 * i))
-        cp(sl("piv", 6, 8), sl("hi3", 2, 9, 6))
-        if t == 0:
-            fill.append(lambda: ts(vw("mbig"), sl("tab", 224, 256), hcol, A.not_equal, BIG, A.mult))
-            fill.append(lambda: ts(vw("mown"), sl("tab", 224, 256), hcol, A.is_equal, BIG, A.mult))
-            fill.append(lambda: ts(vw("mb1"), sl("tab", 224, 256), hcol, A.is_equal, B1, A.mult))
-            fill.append(lambda: ts(vw("cvec"), vw("c16"), icol, A.add))
+        filler()
+        step(turns("s1"), ind(vw("hi3"), o_1), sl("lo3" if t else "tri", 1, 48, 3))
+        filler()
+        step(halves("s2"), *halves("s1"))
+        filler()
+        step(halves("s3"), ind(sl("s2", 16, 32), o_3), sl("s2", 0, 16))
+        filler()
+        count(6, col("hi3", 2))
+        count(7, col("hi3", 8))
+        step(halves("s4"), *turns("s3"))
+        later(3)
         step(turns("s5"), *turns("s4"))
-        later()
+        later(3)
         step(turns("s6"), ind(sl("s5", 16, 32), o_6), sl("s5", 0, 16))
-        later()
-        step(turns("s7"), *halves("s6"))
-        later()
-        step(turns("s8"), ind(sl("s7", 16, 32), o_8), sl("s7", 0, 16))
-        later()
-
+        later(2)
         for l in range(2):
-            o = 16 * l
-            tt(sl("s9", o + 1, o + 16, 2), sl("s8", o, o + 8), sl("s8", o + 8, o + 16), A.max)
-            count(l, col("s9", o + 7))
-            tt(sl("s9", o, o + 16, 2), sl("s8", o, o + 8), sl("s8", o + 8, o + 16), A.min)
-        ts(sl("yy", 6, 8), sl("acc", 6, 8), -B2 / 2, A.mult, -0.25 * B2, A.add)
-        later()
-        ts(sl("s9", 32, 64), sl("s9", 0, 32), -1.0, A.mult)
-        cp(sl("piv", 0, 2), sl("s9", 7, 32, 16))
-        later()
-        later()
-        for k in range(3):
+            scan(sl("med", 4 * l, 4 * l + 4), sl("s6", 4 * l, 32, 8), sl("s6", 4 * l + 2, 32, 8), 0.0, A.max, A.max)
+            count(l, col("med", 4 * l + 3))
+        step(turns("s7"), *halves("s6"))
+        ts(sl("npv", 13, 16, 2), sl("hi3", 2, 9, 6), -1.0, A.mult)
+        later(2)
+        step(turns("s8"), ind(sl("s7", 16, 32), o_8), sl("s7", 0, 16))
+        ts(sl("yv", 6 * YW, 8 * YW, YW), sl("acc", 6, 8), -B2, A.mult)
+        for l in range(2):
+            o = LS * l + 1
+            tt(sl("s9", o + 1, o + 16, 2), sl("s8", 16 * l, 16 * l + 8), sl("s8", 16 * l + 8, 16 * l + 16), A.max)
+            ts(col("s9", o + 37), col("s8", 16 * l + 5), col("s8", 16 * l + 13), A.max, -1.0, A.mult)
+        for l in range(2):
+            o = LS * l + 1
+            tt(sl("s9", o, o + 16, 2), sl("s8", 16 * l, 16 * l + 8), sl("s8", 16 * l + 8, 16 * l + 16), A.min)
+
+        wins = [("s9", "w9", 8), ("w9", "w5", 4), ("w5", None, 2)]
+        due = []
+        for k, (src, dst, h) in enumerate(wins):
             for l in range(2):
-                i, o = 2 * k + l, 16 * l
+                i, o = 2 * k + l, LS * l
                 n = i + 2 if k < 2 else i + 4
-                ends = sl("s9", o + 3, o + 44, 40) if k == 0 else sl("cand", 2 * i - 4, 2 * i - 2)
+                wide = LW + h + 1
+                ends = sl(src, o + h // 2, o + h // 2 + LW + 1, LW) if k else sl("s9", o + 4, o + 39, 34)
                 scan(sl("npv", 2 * n, 2 * n + 2), sl("mul", 0, 2) if k == 0 else sl("mul", 2, 4), ends, col("acc", i),
                      A.mult, A.max)
                 count(n)
-                why(i)
-                if k < 2:
-                    why(i, True)
-                filler()
-                filler()
-                y, ny = col("yy", i), col("ny", i)
-                if k == 0:
-                    if l == 0:
-                        later()
-                    clamp(col("cand", 2 * l), y, col("s9", o + 1), col("s9", o + 9))
-                    clamp(col("cand", 2 * l + 1), ny, col("s9", 32 + o + 13), col("s9", 32 + o + 5))
-                    clamp(col("w7", 4 * l), y, col("s9", o), col("s9", o + 8))
-                    for j, (yc, a, b) in enumerate(((y, o + 4, o + 12), (ny, 46 + o, 38 + o), (ny, 42 + o, 34 + o))):
-                        fill.append(lambda d=4 * l + 1 + j, yc=yc, a=a, b=b: clamp(col("w7", d), yc, col("s9", a), col("s9", b)))
-                elif k == 1:
-                    filler()
-                    if l:
-                        later()
-                    clamp(col("cand", 4 + 2 * l), y, col("w7", 4 * l), col("w7", 4 * l + 1))
-                    clamp(col("cand", 5 + 2 * l), ny, col("w7", 4 * l + 2), col("w7", 4 * l + 3))
-                elif l == 0:
-                    ts(sl("piv", 2, 6), sl("npv", 5, 12, 2), -1.0, A.mult)
-                    later()
-                    later()
-        ts(sl("piv", 8, 10), sl("npv", 17, 20, 2), -1.0, A.mult)
-        tt(vw("e1"), sl("piv", 0, 8), sl("yy", 0, 8), A.max)
-        tt(vw("e2"), sl("piv", 0, 8), sl("yy", 0, 8), A.min)
-        ts(vw("e4"), sl("yy", 0, 8), 0.0, A.is_gt)
-        why(8)
-        red(col("fin", 0), vw("e1"), A.min)
-        red(col("fin", 1), vw("e2"), A.max)
-        scan(vw("e3"), vw("horn"), vw("e4"), -255.5 / 256, A.mult, A.add)
-        decode(vw("lq%d" % t), vw("ls%d" % t), ds)
-        ts(sl("prep", 32, 64), vw("mbig"), col("piv", 8), A.max, col("yy", 8), A.max)
-        ts(sl("prep", 128, 160), vw("mown"), col("piv", 8), A.min, col("yy", 8), A.min)
-        ts(sl("prep", 224, 256), vw("mb1"), col("yy", 8), A.min, 0.0, A.max)
-        why(9)
+                why(i, wide if k < 2 else 1)
+                if due:
+                    due.pop(0)()
+                if k == 2:
+                    later(2)
+                    continue
+                if i == 0:
+                    for e in (0, LS):
+                        ts(sl("s9", e + LW, e + LW + 16), ind(sl("s9", e, e + LW), o_r), -1.0, A.mult)
+                else:
+                    later(1)
+                tt(sl("tw", o, o + wide), sl(src, o, o + wide), sl("yv", YW * i, YW * i + wide), A.max)
+                due.append(lambda o=o, wide=wide, src=src, dst=dst, h=h:
+                           tt(sl(dst, o, o + wide), sl("tw", o, o + wide), sl(src, o + h, o + h + wide), A.min))
+        later(20)
+        ts(sl("piv", 4, 10), sl("npv", 9, 20, 2), -1.0, A.mult)
+        why(8, 1)
+        tt(vw("e4"), sl("acc", 0, 9), vw("side"), A.is_gt)
+        fetch(ds, 0)
+        fetch(ds, 1)
+        tt(sl("w5", 2 * LS + 4, 7 * LS, LS), sl("piv", 4, 9), sl("yv", 4 * YW, 9 * YW, YW), A.max)
+        tt(sl("w5", 2 * LS, 7 * LS, LS), sl("piv", 4, 9), sl("yv", 4 * YW, 9 * YW, YW), A.min)
+        scan(vw("e3"), vw("horn"), vw("e4"), (18 - 255.5 / 16) / -8, A.mult, A.add)
+        y9 = col("yv", 9 * YW)
+        why(9, 1)
+        red(col("fin", 0), sl("w5", 4, 7 * LS, LS), A.min)
+        red(col("fin", 1), sl("w5", 0, 7 * LS, LS), A.max)
+        ts(sl("prep", 128, 160), vw("mb1"), col("e3", 8), A.mult)
+        ts(sl("prep", 160, 192), vw("madd"), col("acc", 9), A.add, 0.0, A.is_gt)
+        ts(sl("prep", 32, 64), vw("mbig"), col("piv", 9), A.max, y9, A.max)
+        ts(sl("prep", 96, 128), vw("mown"), col("piv", 9), A.min, y9, A.min)
         ts(sl("prep", 0, 32), vw("mbig"), col("fin", 0), A.max)
-        ts(sl("prep", 96, 128), vw("mown"), col("fin", 1), A.min)
-        ts(sl("prep", 192, 224), vw("mb1"), col("e3", 7), A.mult)
-        ts(sl("prep", 64, 96), vw("mbig"), col("piv", 9), A.max, col("yy", 9), A.max)
-        ts(sl("prep", 160, 192), vw("mown"), col("piv", 9), A.min, col("yy", 9), A.min)
-        ts(sl("prep", 256, 288), vw("mb1"), col("yy", 9), A.min, 0.0, A.max)
-        for j in range(3):
-            tr(sl("prt", 96 * j, 96 * j + 96), sl("prep", 96 * j, 96 * j + 96))
-        red(col("thr", 0), sl("prt", 0, 96), A.min)
-        red(col("thr", 1), sl("prt", 96, 192), A.max)
-        red(col("thr", 2), sl("prt", 192, 288), A.add, True)
-        ts(col("thr", 3), col("thr", 2), col("thr", 1), A.max, col("thr", 0), A.min)
-        cut = col("thr", 3)
+        ts(sl("prep", 64, 96), vw("mown"), col("fin", 1), A.min)
+        tr(sl("prt", 128, 192), sl("prep", 128, 192))
+        tr(sl("prt", 0, 128), sl("prep", 0, 128))
+        scan(vw("nsum"), vw("nmul"), sl("prt", 128, 193), 0.0, A.mult, A.add)
+        scan(vw("cut"), sl("prt", 64, 128), sl("prt", 0, 64), col("nsum", 64), A.max, A.min)
+        cut = col("cut", 63)
 
         for h in (0, C):
             act(sl("ysg", h, h + C), sl("xc", h, h + C), F.Sign, bias=cut, scale=-1.0)
-        if t == 0:
-            decode(sl(qt, 0, C), sl(st, 0, C), dd, 64.0)
+        fetch(ds, 2)
+        fetch(ds, 3)
         ts(vw("lt"), vw("xc"), cut, A.is_lt)
         ts(sl("le", 16, 16 + C), sl("ysg", 0, C), 0.0, A.is_ge)
+        scan(sl("clt", 16, 528), sl("ones", 0, 512), vw("lt"), 0.0, A.mult, A.add)
         ts(sl("le", 16 + C, 528), sl("ysg", C, 2 * C), 0.0, A.is_ge)
-        scan(sl("clt", 16, 528), vw("lt"), vw("zero"), 0.0, A.add, A.add)
-        scan(sl("sb", 15, 528), sl("le", 15, 528), sl("clt", 15, 528), col("clt", 527), A.add, A.min)
         ts(vw("chalf"), vw("cvec"), col("clt", 527), A.add, -255.5, A.add)
-        ts(vw("cs"), vw("cvec"), col("clt", 527), A.add, -256.0, A.add)
+        ts(sl("cs", 0, 17), vw("cvec"), col("clt", 527), A.add, -256.0, A.add)
+        scan(sl("sb", 15, 528), sl("le", 15, 528), sl("clt", 15, 528), col("clt", 527), A.add, A.min)
 
         def kept(a, b):
             return sl("sb", 17 + 2 * a, 16 + 2 * b, 2)
@@ -475,7 +485,6 @@ def rank_program(g, core, T, topo):
         for i, m in enumerate(SM):
             a, b = (0, 160) if m < 8 else (104, 256)
             act(junk(b - a), kept(a, b), F.Sign, bias=col("chalf", m), scale=-1.0, accum=col("iac", i))
-        act(vw("even"), sl("sb", 16, 528, 2), F.Copy)
         nv = len(VM)
 
         def below(i):
@@ -489,12 +498,13 @@ def rank_program(g, core, T, topo):
             below(i)
         for i in range(4):
             tally(i)
-        for i in range(4, 8):
+        for i in range(4, 7):
             below(i)
         cp(sl(au, 4, 8), sl("isc", 67, 68 * 4, 68))
         ts(sl(au, 0, 4), sl("iac", 0, 4), 0.5, A.mult, 80.0, A.add)
         remote(mates[t], T[la][:, 0:8], sl(au, 0, 8), T[au][:, 0:8], "al%d" % t)
-        below(8)
+        for i in range(7, nv):
+            below(i)
         for i in range(4, nv):
             tally(i)
         ts(sl(au, 13, 16), sl("iac", 4, 7), 0.5, A.mult, 180.0, A.add)
@@ -526,47 +536,60 @@ def rank_program(g, core, T, topo):
                 tt(sl(fw, 512 * (b - 2) + 256 * h + j, 512 * (b - 2) + 256 * h + 256, 2),
                    sl(dd, C * b + 128 * h, C * b + 128 * h + 128), ps((3 + 4 * h + b) % 8, 0, 128), (A.add, A.subtract)[j])
 
-        cp(sl("hw", 0, w), ind(vw("even"), alist))
+        ts(sl("a2u", 0, nk), alist, 2.0, A.mult)
         ts(sl("a2", 0, nk), alist, 2.0, A.mult)
         for b in range(2):
             act(sl(zz, CW * b, CW * b + w), ind(sl(dd, C * b, C * b + C), alist), F.Copy)
-        scan(sl("hl", 0, w), sl("latch", 0, w), sl("hw", 0, w), 0.0, A.max, A.min)
-        tt(sl("bitn", 0, nk), sl("hl", 15, w, 16), sl("cs", 0, nk), A.is_le)
+        cp(sl("hw", 0, w), ind(sl("sb", 16, 528), sl("a2u", 0, nk)))
+        scan(sl("hl", 0, w), sl("latch", 0, w), sl("hw", 0, w), 0.0, A.add, A.min)
 
         mosaic(0, 0)
         mosaic(0, 1)
-        tt(sl("kn", 0, nk), sl("bitn", 0, nk), sl("a2", 0, nk), A.add)
+        tt(sl("bitn", 0, nk), sl("hl", 15, w, 16), sl("cs", 0, nk), A.is_le)
         mosaic(0, 2)
         mosaic(0, 3)
-        cp(klist, sl("kn", 0, nk))
+        tt(sl("kn", 0, nk), sl("bitn", 0, nk), sl("a2", 0, nk), A.add)
         product(0)
         for b in range(4):
             mosaic(1, b)
+        cp(klist, sl("kn", 0, nk))
         product(1)
-        pick("s", sl("mw", 0, w), ind(vw("xc"), klist))
-        if last:
-            dma("y", T.ml[:], T.mw[0:128:16, 0:C], [], [vw("mw")])
+        if not last:
+            pick("s", sl("mw", 0, w), ind(vw("xc"), klist))
         for h in range(2):
             for b in range(2):
                 signed(b, h)
                 both(b + 2, h)
-        for b in range(2):
-            tt(sl("tt%d" % (t + 1), b, 4 * w, 4), ind(sl(rw, 512 * b, 512 * b + 512), klist),
-               sl(zz, CW * b, CW * b + w), A.add)
-            act(sl("tt%d" % (t + 1), b + 2, 4 * w, 4), ind(sl(fw, 512 * b, 512 * b + 512), klist), F.Copy, scale=0.015625)
+        nxt = "tt%d" % (t + 1)
+
+        def state(a, e, which=(0, 1)):
+            kl_ = sl("ku", a // 16, e // 16)
+            for b in which:
+                tt(sl(nxt, 4 * a + b, 4 * e, 4), ind(sl(rw, 512 * b, 512 * b + 512), kl_),
+                   sl(zz, CW * b + a, CW * b + e), A.add)
+                act(sl(nxt, 4 * a + b + 2, 4 * e, 4), ind(sl(fw, 512 * b, 512 * b + 512), kl_), F.Copy, scale=0.015625)
+
+        if not last:
+            state(0, w)
 
     qt, st = "qt%d" % ROUNDS, "st%d" % ROUNDS
-    quant(vw(qt), vw(st), vw("tt%d" % ROUNDS))
-    act(vw("kw"), ind(vw("i512"), sl("ku", 0, 16)), F.Copy)
-    dma("y", T.kl[:], T.kw[0:128:16, 0:C], [], [vw("kw")])
+    state(0, 128)
     for h in range(2):
-        mm(h, 128, vw("qv"), vw("sv"), sl(qt, 128 * h, 128 * h + 128), sl(st, 128 * h, 128 * h + 128))
-    dma("y", T.oc[:], T[qt][:].bitcast(dt.uint8), [], [vw(qt)])
-    for k in range(4):
-        dma("s" if k == 3 else "y", T.osc[4 * k:4 * k + 4, :], T[st][32 * k:32 * k + 4, :], [], [vw(st)])
+        a, e = 128 * h, 128 * h + 128
+        state(128, C, (h,))
+        quant(sl(qt, a, e), sl(st, a, e), sl("tt%d" % ROUNDS, 4 * a, 4 * e))
+        mm(h, 128, vw("qv"), vw("sv"), sl(qt, a, e), sl(st, a, e))
+        dma("y", T.oc[:, 4 * a:4 * e], T[qt][:, a:e].bitcast(dt.uint8), [], [sl(qt, a, e)])
+    act(vw("kw"), ind(sl("i512", 0, 512), sl("ku", 0, 16)), F.Copy)
     act(sl("yo", 0, 128), ps(0, 0, 128), F.Copy)
+    cp(sl("mw", 0, C), ind(vw("xc"), sl("ku", 0, 16)))
     cp(sl("yo", 128, C), ps(1, 0, 128))
-    dma("s", T.y[:], T.yo[:], [], [vw("yo")])
+    dma("s", T.kl[:], T.kw[0:128:16, 0:C], [], [vw("kw")])
+    dma("s", T.y[:, 0:128], T.yo[:, 0:128], [], [sl("yo", 0, 128)])
+    for k in range(4):
+        dma("y", T.osc[4 * k:4 * k + 4, :], T[st][32 * k:32 * k + 4, :], [], [vw(st)])
+    dma("y", T.ml[:], T.mw[0:128:16, 0:C], [], [vw("mw")])
+    dma("s", T.y[:, 128:C], T.yo[:, 128:C], [], [sl("yo", 128, C)])
     for s, n in total.items():
         if waited.get(s, 0) < n:
             g.wait_ge(T.sem[s], n)

@@ -3,14 +3,13 @@ from concourse.mybir import dt, AluOpType, AxisListType, ActivationFunctionType
 A = AluOpType
 F = ActivationFunctionType
 C = 256
-CW = 272
 ROUNDS = 3
 PARTNER = [1, 2, 4]
 BIG = 2.0 ** 76
 B1 = 2.0 ** 78
 B2 = 2.0 ** 84
-SM = [0, 1, 2, 3, 13, 14, 15]
-VM = [4, 5, 6, 7, 8, 9, 10, 11, 12]
+SM = [0, 1, 2, 12, 13, 14, 15]
+VM = [3, 4, 5, 6, 7, 8, 9, 10, 11]
 LW = 17
 YW = 26
 LS = 40
@@ -25,32 +24,31 @@ def _buf(name, n, dtype, where="sbuf"):
 
 
 for _t in range(ROUNDS + 1):
-    _w = CW if _t < ROUNDS else C
-    _buf("tt%d" % _t, 4 * _w, "bfloat16")
-    _buf("qt%d" % _t, _w, X4)
-    _buf("st%d" % _t, _w, "uint8")
+    _buf("tt%d" % _t, 4 * C, "bfloat16")
+    _buf("qt%d" % _t, C, X4)
+    _buf("st%d" % _t, C, "uint8")
 for _t in range(ROUNDS):
-    for _n, _c, _d in [("lq", C, X4), ("ls", C, "uint8"), ("la", 16, "uint16"), ("au", 18, "uint16"),
-                       ("dd", 4 * C, "bfloat16"), ("ds", 4 * C, "bfloat16"), ("zz", 2 * CW, "bfloat16"),
+    for _n, _c, _d in [("lq", C, X4), ("ls", C, "uint8"), ("la", 16, "uint16"), ("au", 16, "uint16"),
+                       ("dd", 4 * C, "bfloat16"), ("ds", 4 * C, "bfloat16"), ("zz", 2 * C, "bfloat16"),
                        ("fw", 4 * C, "bfloat16"), ("zs", 4 * C, "bfloat16"), ("qz", C, X4), ("sz", C, "uint8"),
                        ("rw", 4 * C, "float32")]:
         _buf(_n + str(_t), _c, _d)
 for _d, _l in [
-    ("bfloat16", [("ub", 512), ("vb", 512), ("eb", 516), ("ones", 516), ("latch", CW), ("junk", 2048),
+    ("bfloat16", [("ub", 512), ("vb", 512), ("eb", 516), ("ones", 516), ("latch", C), ("junk", 2048),
                   ("lt", 512), ("le", 528), ("ysg", 512), ("clt", 528), ("sb", 528),
-                  ("ifl", 136 * len(VM)), ("isc", 68 * len(VM)), ("cs", 18), ("hw", CW), ("hl", CW)]),
+                  ("ifl", 136 * len(VM)), ("isc", 68 * len(VM)), ("cs", 16), ("hw", C), ("hl", C)]),
     (X4, [("qu", 128), ("qv", 128), ("qus", 128), ("quz", 128), ("qw", 512), ("qe", 512)]),
     ("uint8", [("su", 128), ("sv", 128), ("sus", 128), ("suz", 128), ("sw", 512), ("se", 512)]),
-    ("uint16", [("offs", 16), ("pku", 16), ("ku", 18), ("a2u", 18)]),
+    ("uint16", [("offs", 16), ("pku", 16), ("ku", 16), ("a2u", 16)]),
     ("int32", [("pki", 16)]),
-    ("float32", [("tab", 256), ("tabt", 256), ("c16", 17), ("cvec", 17), ("chalf", 17), ("r16", CW), ("mbig", 32),
+    ("float32", [("tab", 256), ("tabt", 256), ("c16", 16), ("chalf", 16), ("r16", C), ("mbig", 32),
                  ("mown", 32), ("mb1", 32), ("horn", 9), ("i512", 516), ("pcol", 1), ("ptr", 512), ("tri", 48),
-                 ("tmul", 48), ("hi3", 56), ("lo3", 48), ("mw", CW), ("mtr", 512), ("nz", C), ("r0", C), ("r1", C),
+                 ("tmul", 48), ("hi3", 56), ("lo3", 48), ("mw", C), ("mtr", 512), ("nz", C), ("r0", C), ("r1", C),
                  ("base", C), ("xc", 512), ("s1", 32), ("s2", 32), ("s3", 32), ("s4", 32), ("s5", 32), ("s6", 32),
-                 ("s7", 32), ("s8", 32), ("s9", 2 * LS), ("med", 8), ("tw", 2 * LS), ("w9", 2 * LS), ("w5", 7 * LS),
+                 ("s7", 32), ("s8", 32), ("s9", 2 * LS), ("med", 8), ("tw", 2 * LS), ("w9", 2 * LS), ("w5", 6 * LS),
                  ("side", 9), ("yv", 10 * YW), ("kvec", YW), ("mul", 4), ("npv", 20), ("madd", 32), ("nsum", 65),
-                 ("nmul", 65), ("piv", 10), ("acc", 10), ("e3", 9), ("e4", 9), ("fin", 2), ("prep", 192),
-                 ("prt", 193), ("cut", 64), ("iac", 8), ("a2", 17), ("bitn", 17), ("kn", 17), ("kw", C), ("yo", C)]),
+                 ("nmul", 65), ("piv", 10), ("pin", 4), ("acc", 10), ("e3", 9), ("e4", 9), ("fin", 4), ("prep", 192),
+                 ("prt", 193), ("cut", 64), ("iac", 8), ("a2", 16), ("bitn", 16), ("kn", 16), ("kw", C), ("yo", C)]),
 ]:
     for _n, _c in _l:
         if _c <= 96 and _d == "float32":
@@ -89,6 +87,10 @@ def rank_program(g, core, T, topo):
             for c in range(o + a, o + b, step):
                 m |= 1 << c
         return (T[name][:, o + a:o + b:step], name, m)
+
+    def back(name, a, b):
+        v = sl(name, a, b)
+        return (T[name][:, b - 1:(a - 1 if a else None):-1],) + v[1:]
 
     vw = sl
 
@@ -230,8 +232,8 @@ def rank_program(g, core, T, topo):
         total["am%d" % t] = n
 
     dma("s", T.ub[:], T.u[:], [vw("ub")], [])
-    dma("y", T.tt0[:, 0:4 * C], T.x[:], [sl("tt0", 0, 4 * C)], [])
-    dma("s", T.tt0[:, 4 * C:4 * CW], T.x[:, 0:4 * (CW - C)], [sl("tt0", 4 * C, 4 * CW)], [])
+    for h in (0, 512):
+        dma("y", T.tt0[:, h:h + 512], T.x[:, h:h + 512], [sl("tt0", h, h + 512)], [])
 
     iota(vw("pcol"), [[0, 1]], 3, 4)
     iota(vw("pki"), [[1, 2], [16, 8]], 0, 0, False)
@@ -244,32 +246,28 @@ def rank_program(g, core, T, topo):
             iota(sl("tab", 32 * i + 16, 32 * i + 32), pat, base)
         else:
             iota(sl("tab", 32 * i, 32 * i + 32), pat, base)
-    iota(sl("c16", 0, 16), [[16, 16]], 0)
+    iota(vw("c16"), [[16, 16]], 0)
     ms(vw("ones"), 1.0)
     ms(sl("hi3", 48, 56), BIG)
     ms(vw("tmul"), 1.0)
     ms(sl("tri", 0, 48, 3), 0.0)
+    ms(vw("s9"), 0.0)
     scan(vw("i512"), vw("ones"), vw("ones"), -1.0, A.mult, A.add)
     ms(sl("tmul", 0, 48, 3), 0.0)
     cp(vw("pku"), vw("pki"))
+    ms(vw("mul"), -1.0)
+    ms(sl("kvec", 0, LW), B2)
     ts(vw("eb"), vw("i512"), vw("pcol"), A.is_equal)
     early = [lambda b=b: quant(sl("qe", 128 * b, 128 * b + 128), sl("se", 128 * b, 128 * b + 128),
                                sl("eb", 3 - b, 515 - b)) for b in range(4)]
-    ms(vw("s9"), 0.0)
-    ms(vw("mul"), -1.0)
-    ms(sl("kvec", 0, LW), B2)
-    early[0]()
-    quant(vw("qu"), vw("su"), vw("ub"))
-    dma("y", T.qw[:].bitcast(dt.uint8), T.wc[:], [vw("qw")], [vw("ub")])
-    dma("y", T.sw[:], T.ws[:], [vw("sw")], [])
-    dma("y", T.vb[:], T.v[:], [vw("vb")], [])
-    early[1]()
     ms(sl("tab", 72, 75, 2), 48.0)
+    ms(sl("tab", 88, 91, 2), 48.0)
+    quant(vw("qu"), vw("su"), vw("ub"))
+    early[0]()
+    early[1]()
     cp((T.quz[:].bitcast(dt.uint32),) + vw("quz")[1:], ind(vw("qu"), sl("pku", 8, 16), dt.uint32))
     act(vw("suz"), ind(vw("su"), sl("pku", 8, 16)), F.Copy)
     act(vw("sus"), ind(vw("su"), sl("pku", 0, 8)), F.Copy)
-    cp((T.qus[:].bitcast(dt.uint32),) + vw("qus")[1:], ind(vw("qu"), sl("pku", 0, 8), dt.uint32))
-    ms(sl("tab", 88, 91, 2), 48.0)
     icol = col("tabt", 192)
     hcol = col("tabt", 224)
     o_s, o_z, o_1, o_3, o_6, o_8, o_r = [col("offs", 2 * i) for i in range(7)]
@@ -280,13 +278,11 @@ def rank_program(g, core, T, topo):
             lambda: ts(vw("mbig"), sl("tab", 224, 256), hcol, A.not_equal, BIG, A.mult),
             lambda: ts(vw("mown"), sl("tab", 224, 256), hcol, A.is_equal, BIG, A.mult),
             lambda: ts(vw("mb1"), sl("tab", 224, 256), hcol, A.is_equal),
-            lambda: ms(vw("horn"), 1.0), lambda: ms(vw("side"), 0.5), lambda: ms(col("c16", 16), 0.0),
-            lambda: ms(col("nmul", 64), -B1), lambda: ms(sl("horn", 2, 7, 4), -2.0),
+            lambda: ms(vw("horn"), 1.0), lambda: ms(vw("side"), 0.5),
+            lambda: ms(col("nmul", 64), -B1), lambda: ts(vw("cs"), vw("c16"), icol, A.add),
+            lambda: ts(vw("chalf"), vw("c16"), icol, A.add, 0.5, A.add), lambda: ms(sl("horn", 2, 7, 4), -2.0),
             lambda: ms(col("horn", 4), 2.0), lambda: ms(col("horn", 8), -1.0), lambda: ms(sl("side", 0, 2), -0.5),
-            lambda: ms(sl("side", 6, 8), -0.5), lambda: ts(vw("cvec"), vw("c16"), icol, A.add),
-            lambda: ms(col("le", 15), -256.0), lambda: ms(col("clt", 15), 1024.0),
-            lambda: quant(vw("qv"), vw("sv"), vw("vb")),
-            lambda: ts(vw("latch"), vw("r16"), icol, A.is_le, 1024.0, A.mult)]
+            lambda: ms(sl("side", 6, 8), -0.25), lambda: ms(col("clt", 527), 256.0)]
 
     def later(n=1):
         for _ in range(n):
@@ -302,70 +298,79 @@ def rank_program(g, core, T, topo):
 
     for t in range(ROUNDS):
         last = t == ROUNDS - 1
-        w = C if last else CW
-        nk = w // 16
         qt, st, au, la = "qt%d" % t, "st%d" % t, "au%d" % t, "la%d" % t
         dd, ds, zz, zs, rw, fw = [n + str(t) for n in ("dd", "ds", "zz", "zs", "rw", "fw")]
-        quant(sl(qt, 0, 144), sl(st, 0, 144), sl("tt%d" % t, 0, 4 * 144))
-        quant(sl(qt, 144, CW), sl(st, 144, CW), sl("tt%d" % t, 4 * 144, 4 * CW))
-        mm(0, 144, vw("qu"), vw("su"), sl(qt, 0, 144), sl(st, 0, 144))
-        mm(7, 144, vw("qu"), vw("su"), sl(qt, 128, CW), sl(st, 128, CW))
-        mm(1, C, vw("quz"), vw("suz"), sl(qt, 0, C), sl(st, 0, C))
-        mm(2, C, vw("qus"), vw("sus"), sl(qt, 0, C), sl(st, 0, C))
-        remote(mates[t], T["lq%d" % t][:].bitcast(dt.uint8), sl(qt, 0, C), T[qt][:, 0:C].bitcast(dt.uint8), "aq%d" % t)
-        remote(mates[t], T["ls%d" % t][:], sl(st, 0, C), T[st][:, 0:C], "aq%d" % t)
+
+        def rows(h):
+            q, s = sl(qt, 128 * h, 128 * h + 128), sl(st, 128 * h, 128 * h + 128)
+            mm(1 + 5 * h, 128, vw("quz"), vw("suz"), q, s)
+            mm(2 + 3 * h, 128, vw("qus"), vw("sus"), q, s)
+
+        for h in range(2):
+            quant(sl(qt, 128 * h, 128 * h + 128), sl(st, 128 * h, 128 * h + 128), sl("tt%d" % t, 512 * h, 512 * h + 512))
+            mm(7 * h, 128, vw("qu"), vw("su"), sl(qt, 128 * h, 128 * h + 128), sl(st, 128 * h, 128 * h + 128))
+            if t == 0 and h == 0:
+                cp((T.qus[:].bitcast(dt.uint32),) + vw("qus")[1:], ind(vw("qu"), sl("pku", 0, 8), dt.uint32))
+                rows(0)
         if t == 0:
-            iota(vw("r16"), [[0, CW // 16], [1, 16]], 0)
-            early[2]()
-            early[3]()
-        unpack(sl(qt, 0, C), sl(st, 0, C))
+            dma("y", T.qw[:].bitcast(dt.uint8), T.wc[:], [vw("qw")], [vw("tt0")])
+            dma("y", T.sw[:], T.ws[:], [vw("sw")], [])
+            dma("y", T.vb[:], T.v[:], [vw("vb")], [])
+        else:
+            rows(0)
+        rows(1)
+        remote(mates[t], T["lq%d" % t][:].bitcast(dt.uint8), vw(qt), T[qt][:].bitcast(dt.uint8), "aq%d" % t)
+        remote(mates[t], T["ls%d" % t][:], vw(st), T[st][:], "aq%d" % t)
+        if t == 0:
+            iota(vw("r16"), [[0, C // 16], [1, 16]], 0)
 
         bs = "nz" if t == 0 else "base"
-        if t > 0:
-            tr(sl("mtr", 0, C), sl("mw", 0, C))
-            tr(sl("mtr", C, 2 * C), sl("mw", 16, CW))
-        else:
-            tr(vw("tabt"), vw("tab"))
-        act(vw("nz"), ps(1, 0, C), F.Relu, scale=-1.0)
-        tr(sl("ptr", 0, 128), ps(0, 0, 128))
-        tr(sl("ptr", C, C + 128), ps(0, 16, 144))
-        if t == 0:
-            cp(sl("offs", 0, 12, 2), sl("tabt", 0, 192, 32))
-        tr(sl("ptr", 128, C), ps(7, 0, 128))
-        tr(sl("ptr", C + 128, 2 * C), ps(7, 16, 144))
         fill = []
         if t > 0:
             for h in (0, 128):
                 fill.append(lambda h=h: tt(sl("base", h, h + 128), sl("nz", h, h + 128), sl("mw", h, h + 128), A.add))
-        for j, r in ((0, "r0"), (1, "r1")):
-            for h in (0, 128):
+        for h in (0, 128):
+            for j, r in ((0, "r0"), (1, "r1")):
                 fill.append(lambda j=j, r=r, h=h: tt(sl("xc", 2 * h + j, 2 * h + 256, 2), sl(bs, h, h + 128),
                                                      sl(r, h, h + 128), A.add))
 
-        def filler(n=1):
-            for _ in range(n):
-                if fill:
-                    fill.pop(0)()
+        def filler(other=0):
+            if fill:
+                fill.pop(0)()
+            else:
+                later(other)
 
+        def relus(h):
+            act(sl("r0", 128 * h, 128 * h + 128), ps(2 + 3 * h, 0, 128), F.Relu, scale=-1.0)
+            act(sl("r1", 128 * h, 128 * h + 128), ps(2 + 3 * h, 0, 128), F.Relu)
+
+        if t > 0:
+            tr(sl("mtr", 0, C), vw("mw"))
+            tr(sl("mtr", C, 2 * C), back("mw", 0, C))
+        else:
+            tr(vw("tabt"), vw("tab"))
+        act(sl("nz", 0, 128), ps(1, 0, 128), F.Relu, scale=-1.0)
+        tr(sl("ptr", 0, 128), ps(0, 0, 128))
+        tr(sl("ptr", C + 128, 2 * C), back("ps", 0, 128))
+        if t == 0:
+            relus(0)
+            cp(sl("offs", 0, 12, 2), sl("tabt", 0, 192, 32))
+        tr(sl("ptr", 128, C), ps(7, 0, 128))
+        tr(sl("ptr", C, C + 128), back("ps", 512 * 7, 512 * 7 + 128))
         if t > 0:
             cp(sl("tri", 0, 48, 3), ind(vw("mtr"), o_s))
         else:
-            later(3)
+            filler()
         ts(sl("tri", 1, 48, 3), ind(vw("ptr"), o_z), -1.0, A.mult, 0.0, A.max)
         act(sl("tri", 2, 48, 3), ind(vw("ptr"), o_s), F.Abs)
-        act(vw("r0"), ps(2, 0, C), F.Relu, scale=-1.0)
-        act(vw("r1"), ps(2, 0, C), F.Relu)
+        act(sl("nz", 128, C), ps(6, 0, 128), F.Relu, scale=-1.0)
         if t > 0:
-            filler()
-        else:
-            later(3)
+            relus(0)
+        relus(1)
+        filler()
         scan(sl("hi3", 0, 48), vw("tmul"), vw("tri"), 0.0, A.mult, A.add)
         if t > 0:
             scan(vw("lo3"), vw("tmul"), vw("tri"), 0.0, A.mult, A.add)
-            filler()
-        for b in range(4):
-            fetch(dd, b, 64.0)
-        unpack(vw("lq%d" % t), vw("ls%d" % t))
 
         def halves(name):
             return sl(name, 0, 16), sl(name, 16, 32)
@@ -386,29 +391,55 @@ def rank_program(g, core, T, topo):
         def why(i, n):
             ts(sl("yv", YW * i, YW * i + n), sl("kvec", 0, n), col("acc", i), A.mult, -1.0 if i < 2 else 1.0, A.mult)
 
-        filler()
+        if t > 0:
+            filler()
+        else:
+            later(3)
         step(turns("s1"), ind(vw("hi3"), o_1), sl("lo3" if t else "tri", 1, 48, 3))
         filler()
         step(halves("s2"), *halves("s1"))
         filler()
+        if t == 0:
+            count(6, col("hi3", 2))
+            count(7, col("hi3", 8))
         step(halves("s3"), ind(sl("s2", 16, 32), o_3), sl("s2", 0, 16))
-        filler()
-        count(6, col("hi3", 2))
-        count(7, col("hi3", 8))
+        filler(1)
+        if t == 0:
+            early[2]()
         step(halves("s4"), *turns("s3"))
-        later(3)
+        filler(1)
+        if t == 0:
+            early[3]()
+        else:
+            count(6, col("hi3", 2))
         step(turns("s5"), *turns("s4"))
         later(3)
+        parts = []
+        if t > 0:
+            for j in range(4):
+                parts.append(lambda j=j: ts(sl("lt", 128 * j, 128 * j + 128), sl("xc", 128 * j, 128 * j + 128),
+                                            col("hi3", 8), A.is_lt))
+            parts.append(lambda: scan(sl("ysg", C, 2 * C), sl("lt", 0, C), sl("lt", C, 2 * C), -255.5, A.add, A.add))
+            parts.append(lambda: cp(col("acc", 7), col("ysg", 2 * C - 1)))
+
+        def part(n=1):
+            for _ in range(n):
+                if parts:
+                    parts.pop(0)()
+
+        unpack(vw(qt), vw(st))
         step(turns("s6"), ind(sl("s5", 16, 32), o_6), sl("s5", 0, 16))
+        part()
         later(2)
         for l in range(2):
             scan(sl("med", 4 * l, 4 * l + 4), sl("s6", 4 * l, 32, 8), sl("s6", 4 * l + 2, 32, 8), 0.0, A.max, A.max)
             count(l, col("med", 4 * l + 3))
-        step(turns("s7"), *halves("s6"))
+            if l == 0:
+                step(turns("s7"), *halves("s6"))
         ts(sl("npv", 13, 16, 2), sl("hi3", 2, 9, 6), -1.0, A.mult)
-        later(2)
+        later(1)
         step(turns("s8"), ind(sl("s7", 16, 32), o_8), sl("s7", 0, 16))
-        ts(sl("yv", 6 * YW, 8 * YW, YW), sl("acc", 6, 8), -B2, A.mult)
+        part()
         for l in range(2):
             o = LS * l + 1
             tt(sl("s9", o + 1, o + 16, 2), sl("s8", 16 * l, 16 * l + 8), sl("s8", 16 * l + 8, 16 * l + 16), A.max)
@@ -432,35 +463,45 @@ def rank_program(g, core, T, topo):
                 if due:
                     due.pop(0)()
                 if k == 2:
-                    later(2)
+                    if l == 0:
+                        ts(vw("pin"), sl("npv", 9, 16, 2), -1.0, A.mult)
+                        part(9)
+                        later(3)
+                    else:
+                        ts(sl("yv", 6 * YW, 8 * YW, YW), sl("acc", 6, 8), -B2, A.mult)
                     continue
                 if i == 0:
                     for e in (0, LS):
                         ts(sl("s9", e + LW, e + LW + 16), ind(sl("s9", e, e + LW), o_r), -1.0, A.mult)
                 else:
-                    later(1)
+                    later(2)
+                    part()
                 tt(sl("tw", o, o + wide), sl(src, o, o + wide), sl("yv", YW * i, YW * i + wide), A.max)
                 due.append(lambda o=o, wide=wide, src=src, dst=dst, h=h:
                            tt(sl(dst, o, o + wide), sl("tw", o, o + wide), sl(src, o + h, o + h + wide), A.min))
-        later(20)
-        ts(sl("piv", 4, 10), sl("npv", 9, 20, 2), -1.0, A.mult)
+        later(30)
+        ts(sl("piv", 8, 10), sl("npv", 17, 20, 2), -1.0, A.mult)
+        tt(sl("w5", 2 * LS + 4, 6 * LS, LS), vw("pin"), sl("yv", 4 * YW, 8 * YW, YW), A.max)
+        tt(sl("w5", 2 * LS, 6 * LS, LS), vw("pin"), sl("yv", 4 * YW, 8 * YW, YW), A.min)
         why(8, 1)
         tt(vw("e4"), sl("acc", 0, 9), vw("side"), A.is_gt)
-        fetch(ds, 0)
-        fetch(ds, 1)
-        tt(sl("w5", 2 * LS + 4, 7 * LS, LS), sl("piv", 4, 9), sl("yv", 4 * YW, 9 * YW, YW), A.max)
-        tt(sl("w5", 2 * LS, 7 * LS, LS), sl("piv", 4, 9), sl("yv", 4 * YW, 9 * YW, YW), A.min)
+        for b in (0, 2, 1, 3):
+            fetch(dd, b, 64.0)
+        for b in (0, 2, 1, 3):
+            mm(3 + b, C, sl("qe", 128 * b, 128 * b + 128), sl("se", 128 * b, 128 * b + 128), vw("lq%d" % t), vw("ls%d" % t))
+        red(col("fin", 0), sl("w5", 4, 6 * LS, LS), A.min)
+        red(col("fin", 1), sl("w5", 0, 6 * LS, LS), A.max)
+        y8, y9 = col("yv", 8 * YW), col("yv", 9 * YW)
         scan(vw("e3"), vw("horn"), vw("e4"), (18 - 255.5 / 16) / -8, A.mult, A.add)
-        y9 = col("yv", 9 * YW)
+        ts(col("fin", 2), col("piv", 8), y8, A.max, col("fin", 0), A.min)
+        ts(col("fin", 3), col("piv", 8), y8, A.min, col("fin", 1), A.max)
         why(9, 1)
-        red(col("fin", 0), sl("w5", 4, 7 * LS, LS), A.min)
-        red(col("fin", 1), sl("w5", 0, 7 * LS, LS), A.max)
-        ts(sl("prep", 128, 160), vw("mb1"), col("e3", 8), A.mult)
         ts(sl("prep", 160, 192), vw("madd"), col("acc", 9), A.add, 0.0, A.is_gt)
+        ts(sl("prep", 128, 160), vw("mb1"), col("e3", 8), A.mult)
+        ts(sl("prep", 0, 32), vw("mbig"), col("fin", 2), A.max)
+        ts(sl("prep", 64, 96), vw("mown"), col("fin", 3), A.min)
         ts(sl("prep", 32, 64), vw("mbig"), col("piv", 9), A.max, y9, A.max)
         ts(sl("prep", 96, 128), vw("mown"), col("piv", 9), A.min, y9, A.min)
-        ts(sl("prep", 0, 32), vw("mbig"), col("fin", 0), A.max)
-        ts(sl("prep", 64, 96), vw("mown"), col("fin", 1), A.min)
         tr(sl("prt", 128, 192), sl("prep", 128, 192))
         tr(sl("prt", 0, 128), sl("prep", 0, 128))
         scan(vw("nsum"), vw("nmul"), sl("prt", 128, 193), 0.0, A.mult, A.add)
@@ -469,22 +510,25 @@ def rank_program(g, core, T, topo):
 
         for h in (0, C):
             act(sl("ysg", h, h + C), sl("xc", h, h + C), F.Sign, bias=cut, scale=-1.0)
+        fetch(ds, 0)
         fetch(ds, 2)
-        fetch(ds, 3)
-        ts(vw("lt"), vw("xc"), cut, A.is_lt)
-        ts(sl("le", 16, 16 + C), sl("ysg", 0, C), 0.0, A.is_ge)
-        scan(sl("clt", 16, 528), sl("ones", 0, 512), vw("lt"), 0.0, A.mult, A.add)
-        ts(sl("le", 16 + C, 528), sl("ysg", C, 2 * C), 0.0, A.is_ge)
-        ts(vw("chalf"), vw("cvec"), col("clt", 527), A.add, -255.5, A.add)
-        ts(sl("cs", 0, 17), vw("cvec"), col("clt", 527), A.add, -256.0, A.add)
-        scan(sl("sb", 15, 528), sl("le", 15, 528), sl("clt", 15, 528), col("clt", 527), A.add, A.min)
+        for h in (C, 0):
+            ts(sl("lt", h, h + C), sl("xc", h, h + C), cut, A.is_lt)
+        scan(back("clt", 15 + C, 15 + 2 * C), sl("ones", 0, C), back("lt", C, 2 * C), 256.0, A.mult, A.subtract)
+        for h in (0, C):
+            ts(sl("le", 16 + h, 16 + C + h), sl("ysg", h, h + C), 0.0, A.is_ge)
+        scan(back("clt", 15, 15 + C), sl("ones", 0, C), back("lt", 0, C), col("clt", 15 + C), A.mult, A.subtract)
+        scan(sl("sb", 16, 416), sl("le", 16, 416), sl("clt", 16, 416), 0.0, A.add, A.min)
 
         def kept(a, b):
             return sl("sb", 17 + 2 * a, 16 + 2 * b, 2)
 
-        for i, m in enumerate(SM):
-            a, b = (0, 160) if m < 8 else (104, 256)
-            act(junk(b - a), kept(a, b), F.Sign, bias=col("chalf", m), scale=-1.0, accum=col("iac", i))
+        def signs(first):
+            for i, m in enumerate(SM):
+                a, b = (0, 152) if m < 8 else (96, 256)
+                if (m < 8) == first:
+                    act(junk(b - a), kept(a, b), F.Sign, bias=col("chalf", m), scale=-1.0, accum=col("iac", i))
+
         nv = len(VM)
 
         def below(i):
@@ -494,27 +538,30 @@ def rank_program(g, core, T, topo):
             scan(sl("isc", 68 * j, 68 * j + 68), sl("ifl", 136 * j, 136 * j + 68),
                  sl("ifl", 136 * j + 68, 136 * j + 136), float(8 * VM[j]), A.add, A.add)
 
-        for i in range(4):
+        signs(True)
+        for i in range(2):
             below(i)
-        for i in range(4):
+        scan(sl("sb", 416, 528), sl("le", 416, 528), sl("clt", 416, 528), col("sb", 415), A.add, A.min)
+        signs(False)
+        fetch(ds, 1)
+        fetch(ds, 3)
+        for i in range(2, 5):
+            below(i)
+        for i in range(5):
             tally(i)
-        for i in range(4, 7):
+        for i in range(5, nv):
             below(i)
-        cp(sl(au, 4, 8), sl("isc", 67, 68 * 4, 68))
-        ts(sl(au, 0, 4), sl("iac", 0, 4), 0.5, A.mult, 80.0, A.add)
+        ts(sl(au, 0, 3), sl("iac", 0, 3), 0.5, A.mult, 76.0, A.add)
+        cp(sl(au, 3, 8), sl("isc", 67, 68 * 5, 68))
         remote(mates[t], T[la][:, 0:8], sl(au, 0, 8), T[au][:, 0:8], "al%d" % t)
-        for i in range(7, nv):
-            below(i)
-        for i in range(4, nv):
+        for i in range(5, nv):
             tally(i)
-        ts(sl(au, 13, 16), sl("iac", 4, 7), 0.5, A.mult, 180.0, A.add)
-        if not last:
-            ts(col(au, 16), col("iac", 0), 0.5, A.mult, 80.0, A.add)
-        cp(sl(au, 8, 13), sl("isc", 68 * 4 + 67, 68 * nv, 68))
+        ts(sl(au, 12, 16), sl("iac", 3, 7), 0.5, A.mult, 176.0, A.add)
+        cp(sl(au, 8, 12), sl("isc", 68 * 5 + 67, 68 * nv, 68))
         remote(mates[t], T[la][:, 8:16], sl(au, 8, 16), T[au][:, 8:16], "am%d" % t)
 
-        alist = sl(au, 0, nk)
-        klist = sl("ku", 0, nk)
+        alist = vw(au)
+        klist = vw("ku")
 
         def mosaic(h, b):
             pick("vs"[b % 2], sl(zs, 512 * h + b, 512 * h + 512, 4),
@@ -536,53 +583,56 @@ def rank_program(g, core, T, topo):
                 tt(sl(fw, 512 * (b - 2) + 256 * h + j, 512 * (b - 2) + 256 * h + 256, 2),
                    sl(dd, C * b + 128 * h, C * b + 128 * h + 128), ps((3 + 4 * h + b) % 8, 0, 128), (A.add, A.subtract)[j])
 
-        ts(sl("a2u", 0, nk), alist, 2.0, A.mult)
-        ts(sl("a2", 0, nk), alist, 2.0, A.mult)
-        for b in range(2):
-            act(sl(zz, CW * b, CW * b + w), ind(sl(dd, C * b, C * b + C), alist), F.Copy)
-        cp(sl("hw", 0, w), ind(sl("sb", 16, 528), sl("a2u", 0, nk)))
-        scan(sl("hl", 0, w), sl("latch", 0, w), sl("hw", 0, w), 0.0, A.add, A.min)
+        if t == 0:
+            ts(vw("latch"), vw("r16"), icol, A.is_le, 1024.0, A.mult)
+        ts(vw("a2u"), alist, 2.0, A.mult)
+        ts(vw("a2"), alist, 2.0, A.mult)
+        if t == 0:
+            quant(vw("qv"), vw("sv"), vw("vb"))
+        act(sl(zz, 0, C), ind(sl(dd, 0, C), alist), F.Copy)
+        cp(vw("hw"), ind(sl("sb", 16, 528), vw("a2u")))
 
-        mosaic(0, 0)
-        mosaic(0, 1)
-        tt(sl("bitn", 0, nk), sl("hl", 15, w, 16), sl("cs", 0, nk), A.is_le)
-        mosaic(0, 2)
-        mosaic(0, 3)
-        tt(sl("kn", 0, nk), sl("bitn", 0, nk), sl("a2", 0, nk), A.add)
-        product(0)
         for b in range(4):
-            mosaic(1, b)
-        cp(klist, sl("kn", 0, nk))
+            mosaic(0, b)
+        scan(vw("hl"), vw("latch"), vw("hw"), 0.0, A.add, A.min)
+        product(0)
+        mosaic(1, 0)
+        mosaic(1, 1)
+        tt(vw("bitn"), sl("hl", 15, C, 16), vw("cs"), A.is_le)
+        mosaic(1, 2)
+        mosaic(1, 3)
+        act(sl(zz, C, 2 * C), ind(sl(dd, C, 2 * C), alist), F.Copy)
+        tt(vw("kn"), vw("bitn"), vw("a2"), A.add)
         product(1)
-        if not last:
-            pick("s", sl("mw", 0, w), ind(vw("xc"), klist))
+        cp(klist, vw("kn"))
         for h in range(2):
             for b in range(2):
                 signed(b, h)
                 both(b + 2, h)
+            if h == 0 and not last:
+                pick("s", vw("mw"), ind(vw("xc"), klist))
         nxt = "tt%d" % (t + 1)
 
-        def state(a, e, which=(0, 1)):
+        def state(a, e, which):
             kl_ = sl("ku", a // 16, e // 16)
             for b in which:
                 tt(sl(nxt, 4 * a + b, 4 * e, 4), ind(sl(rw, 512 * b, 512 * b + 512), kl_),
-                   sl(zz, CW * b + a, CW * b + e), A.add)
+                   sl(zz, C * b + a, C * b + e), A.add)
                 act(sl(nxt, 4 * a + b + 2, 4 * e, 4), ind(sl(fw, 512 * b, 512 * b + 512), kl_), F.Copy, scale=0.015625)
 
-        if not last:
-            state(0, w)
+        state(0, C, (0,))
+        state(0, 128, (1,))
+        state(128, C, (1,))
 
     qt, st = "qt%d" % ROUNDS, "st%d" % ROUNDS
-    state(0, 128)
     for h in range(2):
         a, e = 128 * h, 128 * h + 128
-        state(128, C, (h,))
         quant(sl(qt, a, e), sl(st, a, e), sl("tt%d" % ROUNDS, 4 * a, 4 * e))
         mm(h, 128, vw("qv"), vw("sv"), sl(qt, a, e), sl(st, a, e))
         dma("y", T.oc[:, 4 * a:4 * e], T[qt][:, a:e].bitcast(dt.uint8), [], [sl(qt, a, e)])
-    act(vw("kw"), ind(sl("i512", 0, 512), sl("ku", 0, 16)), F.Copy)
+    act(vw("kw"), ind(sl("i512", 0, 512), vw("ku")), F.Copy)
     act(sl("yo", 0, 128), ps(0, 0, 128), F.Copy)
-    cp(sl("mw", 0, C), ind(vw("xc"), sl("ku", 0, 16)))
+    cp(vw("mw"), ind(vw("xc"), vw("ku")))
     cp(sl("yo", 128, C), ps(1, 0, 128))
     dma("s", T.kl[:], T.kw[0:128:16, 0:C], [], [vw("kw")])
     dma("s", T.y[:, 0:128], T.yo[:, 0:128], [], [sl("yo", 0, 128)])

@@ -1,3 +1,4 @@
+import numpy as np
 from concourse.mybir import dt, AluOpType, AxisListType, ActivationFunctionType
 
 A = AluOpType
@@ -8,11 +9,14 @@ PARTNER = [1, 2, 4]
 BIG = 2.0 ** 76
 B1 = 2.0 ** 78
 B2 = 2.0 ** 84
-SM = [0, 1, 2, 12, 13, 14, 15]
+HUGE = 2.0 ** 95
+SM = {0: (0, 152), 1: (8, 144), 2: (0, 152), 12: (96, 256), 13: (104, 248), 14: (104, 248), 15: (96, 256)}
 VM = [3, 4, 5, 6, 7, 8, 9, 10, 11]
-LW = 17
-YW = 26
-LS = 40
+MID = (76.0, 176.0)
+WL = 80
+D4 = 144
+OWN = [3, 4, 0, 1]
+FAR = [2, 5, 6, 7]
 
 X4 = "float8_e4m3fn_x4"
 SCRATCH = {}
@@ -20,7 +24,7 @@ POOL = {}
 
 
 def _buf(name, n, dtype, where="sbuf"):
-    SCRATCH[name] = (where, [128, n], dtype)
+    SCRATCH[name] = (where, [128] + (n if isinstance(n, list) else [n]), dtype)
 
 
 for _t in range(ROUNDS + 1):
@@ -34,31 +38,32 @@ for _t in range(ROUNDS):
                        ("rw", 4 * C, "float32")]:
         _buf(_n + str(_t), _c, _d)
 for _d, _l in [
-    ("bfloat16", [("ub", 512), ("vb", 512), ("eb", 516), ("ones", 516), ("latch", C), ("junk", 2048),
-                  ("lt", 512), ("le", 528), ("ysg", 512), ("clt", 528), ("sb", 528),
-                  ("ifl", 136 * len(VM)), ("isc", 68 * len(VM)), ("cs", 16), ("hw", C), ("hl", C)]),
+    ("bfloat16", [("ub", 512), ("vb", 512), ("eb", 516), ("ones", C), ("latch", C), ("junk", 2048),
+                  ("lt", 512), ("le", 528), ("ysg", 512), ("clt", 528), ("sb", 528), ("odd", C),
+                  ("c16w", C), ("ifl", 136 * len(VM)), ("cs", 16), ("gw", C), ("hw", C), ("hl", C)]),
     (X4, [("qu", 128), ("qv", 128), ("qus", 128), ("quz", 128), ("qw", 512), ("qe", 512)]),
     ("uint8", [("su", 128), ("sv", 128), ("sus", 128), ("suz", 128), ("sw", 512), ("se", 512)]),
-    ("uint16", [("offs", 16), ("pku", 16), ("ku", 16), ("a2u", 16)]),
-    ("int32", [("pki", 16)]),
-    ("float32", [("tab", 256), ("tabt", 256), ("c16", 16), ("chalf", 16), ("r16", C), ("mbig", 32),
-                 ("mown", 32), ("mb1", 32), ("horn", 9), ("i512", 516), ("pcol", 1), ("ptr", 512), ("tri", 48),
-                 ("tmul", 48), ("hi3", 56), ("lo3", 48), ("mw", C), ("mtr", 512), ("nz", C), ("r0", C), ("r1", C),
-                 ("base", C), ("xc", 512), ("s1", 32), ("s2", 32), ("s3", 32), ("s4", 32), ("s5", 32), ("s6", 32),
-                 ("s7", 32), ("s8", 32), ("s9", 2 * LS), ("med", 8), ("tw", 2 * LS), ("w9", 2 * LS), ("w5", 6 * LS),
-                 ("side", 9), ("yv", 10 * YW), ("kvec", YW), ("mul", 4), ("npv", 20), ("madd", 32), ("nsum", 65),
-                 ("nmul", 65), ("piv", 10), ("pin", 4), ("acc", 10), ("e3", 9), ("e4", 9), ("fin", 4), ("prep", 192),
-                 ("prt", 193), ("cut", 64), ("iac", 8), ("a2", 16), ("bitn", 16), ("kn", 16), ("kw", C), ("yo", C)]),
+    ("uint16", [("offs", 16), ("pku", 16), ("ku", 16)]),
+    ("float32", [("tab", 128), ("tabt", 128), ("tab2", [3, 2, 16]), ("tabu", 96), ("c16", 16), ("chalf", 16),
+                 ("r16", C), ("mbig", 32), ("mown", 32), ("mpm", 32), ("mb1", 32), ("madd", 32),
+                 ("horn", 8), ("i512", 512), ("i256", 1), ("ptr", 512), ("tri", 96), ("tmul", 96), ("x6", 96),
+                 ("mw", C), ("mtr", 512), ("r0", C), ("r1", C), ("nz", C), ("ab", C), ("bh", 512), ("xc", 512),
+                 ("y1", [16, 4]), ("y2", [8, 2, 4]), ("y3", [8, 2, 4]), ("y4", [16, 2, 2]), ("y5", [8, 8]),
+                 ("y6", [4, 2, 8]), ("y7", [8, 2, 4]), ("y8", [16, 2, 2]),
+                 ("med", 16), ("w2", 2 * WL), ("d2", 160), ("w3", 176), ("s4", 112), ("kk", 56), ("lat", 1),
+                 ("u3", 16), ("fin", 2), ("yy", 2), ("side", 8), ("nsum", 97), ("nmul", 97),
+                 ("acc", 10), ("e3", 8), ("e4", 8), ("prep", 320), ("prt", 320), ("cut", 96),
+                 ("isc", 68 * 16), ("kw", C), ("yo", C)]),
 ]:
     for _n, _c in _l:
-        if _c <= 96 and _d == "float32":
+        if _d == "float32" and not isinstance(_c, list) and _c <= 176:
             POOL[_n] = (sum(-(-_v[1] // 8) * 8 for _v in POOL.values()), _c)
         else:
             _buf(_n, _c, _d)
 _buf("pool", sum(-(-_v[1] // 8) * 8 for _v in POOL.values()), "float32")
 _buf("ps", 4096, "float32", "psum")
 
-SEMAPHORES = ["cv", "cs", "ct", "cg", "loc"] + ["d%d" % _i for _i in range(20)] \
+SEMAPHORES = ["cv", "cs", "ct", "cg", "loc", "loq"] + ["d%d" % _i for _i in range(20)] \
     + [_n + str(_i) for _n in ("aq", "al", "am") for _i in range(ROUNDS)]
 
 
@@ -86,13 +91,22 @@ def rank_program(g, core, T, topo):
             m = 0
             for c in range(o + a, o + b, step):
                 m |= 1 << c
-        return (T[name][:, o + a:o + b:step], name, m)
+        return (T[name][:, o + a:(o + b if o + b >= 0 else None):step], name, m)
 
     def back(name, a, b):
         v = sl(name, a, b)
         return (T[name][:, b - 1:(a - 1 if a else None):-1],) + v[1:]
 
+    def nd(name, *idx):
+        shape = SCRATCH[name][1][1:]
+        m = 0
+        for c in np.arange(int(np.prod(shape))).reshape(shape)[idx].reshape(-1).tolist():
+            m |= 1 << c
+        return (T[name][(slice(None),) + idx], name, m)
+
     vw = sl
+    al = slice(None)
+    rv = slice(None, None, -1)
 
     def col(name, a):
         return sl(name, a, a + 1)
@@ -202,17 +216,14 @@ def rank_program(g, core, T, topo):
         out = sl("ps", 512 * bank, 512 * bank + n)
         op("t", lambda: g.tensor.matmul_mx(out[0], lq[0], ls[0], rq[0], rs[0], True, True), [out], [lq, ls, rq, rs])
 
-    def iota(out, pattern, base, mult=0, small=True):
-        if small:
-            op("g", lambda: g.iota(out[0], pattern, base, mult, allow_small_or_imprecise_dtypes=True), [out], [])
-        else:
-            op("g", lambda: g.iota(out[0], pattern, base, mult), [out], [])
+    def iota(out, pattern, base, mult=0):
+        op("g", lambda: g.iota(out[0], pattern, base, mult, allow_small_or_imprecise_dtypes=True), [out], [])
 
-    def remote(dst, out_ap, src, src_ap, sem):
+    def remote(dst, out_ap, src, src_ap, sem, left="loc"):
         need("g", [src], [])
         rid, pid, _ = topo.addr(dst)
-        g.remote_dma(out_ap, src_ap, T.sem[sem], T.sem.loc, pid, rid, topo.mask(core, dst))
-        total["loc"] = total.get("loc", 0) + len(topo.engines(core, dst))
+        g.remote_dma(out_ap, src_ap, T.sem[sem], T.sem[left], pid, rid, topo.mask(core, dst))
+        total[left] = total.get(left, 0) + len(topo.engines(core, dst))
 
     def junk(n):
         nj[0] = (nj[0] + 1) % 4
@@ -220,6 +231,11 @@ def rank_program(g, core, T, topo):
 
     def ps(bank, a, b):
         return sl("ps", 512 * bank + a, 512 * bank + b)
+
+    def some(todo, n=1):
+        for _ in range(n):
+            if todo:
+                todo.pop(0)()
 
     mates = [T.cores[rank ^ PARTNER[t]] for t in range(ROUNDS)]
     for t in range(ROUNDS):
@@ -235,332 +251,370 @@ def rank_program(g, core, T, topo):
     for h in (0, 512):
         dma("y", T.tt0[:, h:h + 512], T.x[:, h:h + 512], [sl("tt0", h, h + 512)], [])
 
-    iota(vw("pcol"), [[0, 1]], 3, 4)
-    iota(vw("pki"), [[1, 2], [16, 8]], 0, 0, False)
-    tabs = [([[16, 2], [32, 16]], 0), ([[16, 2], [32, 16]], 1), ([[0, 2], [-24, 2], [3, 8]], 26),
-            ([[0, 2], [4, 4], [-1, 4]], 3), ([[-4, 4], [2, 2], [-1, 2]], 13), ([[8, 2], [-4, 2], [1, 4]], 4),
-            ([[0, 2], [1, 16]], 0), ([[1, 2], [0, 16]], 0)]
-    for i, (pat, base) in enumerate(tabs):
-        if i in (4, 5):
-            iota(sl("tab", 32 * i, 32 * i + 16), pat, base)
-            iota(sl("tab", 32 * i + 16, 32 * i + 32), pat, base)
-        else:
-            iota(sl("tab", 32 * i, 32 * i + 32), pat, base)
-    iota(vw("c16"), [[16, 16]], 0)
     ms(vw("ones"), 1.0)
-    ms(sl("hi3", 48, 56), BIG)
-    ms(vw("tmul"), 1.0)
-    ms(sl("tri", 0, 48, 3), 0.0)
-    ms(vw("s9"), 0.0)
-    scan(vw("i512"), vw("ones"), vw("ones"), -1.0, A.mult, A.add)
-    ms(sl("tmul", 0, 48, 3), 0.0)
-    cp(vw("pku"), vw("pki"))
-    ms(vw("mul"), -1.0)
-    ms(sl("kvec", 0, LW), B2)
-    ts(vw("eb"), vw("i512"), vw("pcol"), A.is_equal)
+    ms(vw("eb"), 0.0)
+    op("g", lambda: g.affine_select(T.eb[:, 3:515:4], T.ones[:, 0:128], [[-1, 128]], A.is_equal, 0.0, 0, 1),
+       [sl("eb", 3, 515, 4)], [vw("ones")])
     early = [lambda b=b: quant(sl("qe", 128 * b, 128 * b + 128), sl("se", 128 * b, 128 * b + 128),
                                sl("eb", 3 - b, 515 - b)) for b in range(4)]
-    ms(sl("tab", 72, 75, 2), 48.0)
-    ms(sl("tab", 88, 91, 2), 48.0)
+    for d in range(2):
+        iota(nd("tab2", 0, d, al), [[-1, 4], [17, 2], [-8, 2]], 9)
+    for i, a, b, step, pat, base in [
+            (1, 1, 16, 4, [[2, 4]], 66), (1, 3, 16, 4, [[57, 2], [17, 2]], 0), (2, 0, 4, 1, [[32, 4]], 24),
+            (2, 4, 8, 1, [[1, 4]], D4 + 24), (2, 8, 12, 1, [[32, 4]], 22), (2, 12, 16, 1, [[1, 4]], D4 + 28)]:
+        iota(nd("tab2", i, al, slice(a, b, step)), [[0, 2]] + pat, base)
+    for a in (64, 80):
+        scan(sl("tab", a, a + 16), sl("ones", 0, 16), sl("ones", 0, 16), -1.0, A.mult, A.add)
+    for name, a, b, v in [("tab", 96, 112, 0.0), ("tab", 112, 128, 1.0), ("tmul", 0, 96, -1.0), ("kk", 0, 48, -1.0)]:
+        ms(sl(name, a, b), v)
+    for a, v in ((0, 0.0), (16, 16.0), (32, 1.0), (48, 17.0)):
+        ts(sl("tab", a, a + 16), sl("tab", 64, 80), 32.0, A.mult, v, A.add)
+    for e in range(2):
+        ts(sl("pku", 8 * e, 8 * e + 8), sl("tab", 64, 72), 16.0, A.mult, float(e), A.add)
+    ms(vw("tri"), 0.0)
+    tr(vw("tabt"), vw("tab"))
+    for name, a, b, step, v in [("tmul", 0, 96, 6, 0.0), ("tmul", 1, 96, 6, 1.0)]:
+        ms(sl(name, a, b, step), v)
+    some(early, 1)
+    cp(sl("offs", 0, 4, 2), sl("tabt", 0, 64, 32))
+    some(early, 2)
+
+    rest = []
+    for name, a, b, step, v in [
+            ("d2", 128, 160, 1, -HUGE), ("kk", 49, 50, 1, B2), ("w3", 0, 128, 1, BIG), ("w3", 128, D4, 1, -HUGE),
+            ("w2", 32, 56, 1, BIG), ("w2", WL + 32, WL + 56, 1, BIG), ("w2", 56, 64, 1, -HUGE),
+            ("w2", WL + 56, WL + 64, 1, -HUGE), ("s4", 0, 16, 1, BIG), ("horn", 0, 8, 1, 1), ("side", 0, 7, 1, 0),
+            ("nmul", 96, 97, 1, -B1), ("nmul", 0, 96, 1, 1), ("prt", 96, 97, 1, 0), ("d2", 138, 160, 16, 0),
+            ("kk", 0, 49, 48, -B2), ("kk", 16, 33, 16, B2), ("kk", 35, 40, 1, 1), ("kk", 41, 45, 1, 1),
+            ("kk", 25, 28, 2, 1), ("horn", 2, 7, 4, -2), ("horn", 4, 5, 1, 2), ("side", 2, 6, 1, 1),
+            ("clt", 527, 528, 1, C), (1, 2, 9, 6, 56), (1, 0, 1, 1, 4), (1, 6, 7, 1, 21), (1, 4, 5, 1, 76),
+            (1, 10, 11, 1, 78), (1, 12, 13, 1, 52), (1, 14, 15, 1, 50), (0, 12, 13, 1, 12), (0, 14, 15, 1, 29)]:
+        n = len(range(a, b, step))
+        if isinstance(name, str):
+            out = sl(name, a, b, step)
+        else:
+            out, n = nd("tab2", name, al, slice(a, b, step)), 2 * n
+        rest.append(lambda out=out, n=n, v=v: act(out, sl("ones", 0, n), F.Copy, scale=float(v)))
+    some(rest, 20)
     quant(vw("qu"), vw("su"), vw("ub"))
-    early[0]()
-    early[1]()
-    cp((T.quz[:].bitcast(dt.uint32),) + vw("quz")[1:], ind(vw("qu"), sl("pku", 8, 16), dt.uint32))
-    act(vw("suz"), ind(vw("su"), sl("pku", 8, 16)), F.Copy)
-    act(vw("sus"), ind(vw("su"), sl("pku", 0, 8)), F.Copy)
-    icol = col("tabt", 192)
-    hcol = col("tabt", 224)
-    o_s, o_z, o_1, o_3, o_6, o_8, o_r = [col("offs", 2 * i) for i in range(7)]
-    late = [lambda: ts(o_r, icol, -1.0, A.mult, 16.0, A.add), lambda: ms(col("mul", 0), -B2),
-            lambda: ms(col("mul", 2), B2), lambda: ms(sl("kvec", LW, YW), -B2),
-            lambda: ms(vw("nmul"), 1.0), lambda: ms(col("prt", 192), 0.0),
-            lambda: ts(vw("madd"), sl("tab", 224, 256), hcol, A.not_equal, -1024.0, A.mult),
-            lambda: ts(vw("mbig"), sl("tab", 224, 256), hcol, A.not_equal, BIG, A.mult),
-            lambda: ts(vw("mown"), sl("tab", 224, 256), hcol, A.is_equal, BIG, A.mult),
-            lambda: ts(vw("mb1"), sl("tab", 224, 256), hcol, A.is_equal),
-            lambda: ms(vw("horn"), 1.0), lambda: ms(vw("side"), 0.5),
-            lambda: ms(col("nmul", 64), -B1), lambda: ts(vw("cs"), vw("c16"), icol, A.add),
-            lambda: ts(vw("chalf"), vw("c16"), icol, A.add, 0.5, A.add), lambda: ms(sl("horn", 2, 7, 4), -2.0),
-            lambda: ms(col("horn", 4), 2.0), lambda: ms(col("horn", 8), -1.0), lambda: ms(sl("side", 0, 2), -0.5),
-            lambda: ms(sl("side", 6, 8), -0.25), lambda: ms(col("clt", 527), 256.0)]
+    icol = col("tabt", 64)
+    hcol = col("tabt", 96)
+    half = sl("tab", 96, 128)
+    o_s, o_z, o_1, o_2, o_3 = [col("offs", 2 * i) for i in range(5)]
+    masks = [lambda: ts(vw("mbig"), half, hcol, A.not_equal, BIG, A.mult),
+             lambda: ts(vw("mown"), half, hcol, A.is_equal, BIG, A.mult),
+             lambda: ts(vw("madd"), half, hcol, A.not_equal, -1024.0, A.mult),
+             lambda: ts(vw("mb1"), half, hcol, A.is_equal, -1.0, A.mult),
+             lambda: tt(vw("mpm"), vw("mown"), vw("mbig"), A.subtract)]
+    late = [lambda: tr(vw("tabu"), nd("tab2", al, al, al)),
+            lambda: cp(sl("offs", 4, 10, 2), sl("tabu", 0, 96, 32)),
+            lambda: ts(vw("cs"), vw("c16"), icol, A.add),
+            lambda: ts(vw("chalf"), vw("c16"), icol, A.add, 0.5, A.add),
+            lambda: ts(vw("lat"), icol, 1.0, A.add, 1024.0, A.mult), lambda: ts(vw("i256"), icol, 256.0, A.add)]
 
-    def later(n=1):
-        for _ in range(n):
-            if late:
-                late.pop(0)()
+    def unpack(banks, src_q, src_s):
+        for b in (0, 2, 1, 3):
+            mm(banks[b], C, sl("qe", 128 * b, 128 * b + 128), sl("se", 128 * b, 128 * b + 128), src_q, src_s)
 
-    def unpack(src_q, src_s):
-        for b in range(4):
-            mm(3 + b, C, sl("qe", 128 * b, 128 * b + 128), sl("se", 128 * b, 128 * b + 128), src_q, src_s)
-
-    def fetch(dst, b, up=None):
-        act(sl(dst, C * b, C * b + C), ps(3 + b, 0, C), F.Copy, scale=up if b > 1 else None)
+    def fetch(dst, banks, b, up=None):
+        act(sl(dst, C * b, C * b + C), ps(banks[b], 0, C), F.Copy, scale=up if b > 1 else None)
 
     for t in range(ROUNDS):
         last = t == ROUNDS - 1
         qt, st, au, la = "qt%d" % t, "st%d" % t, "au%d" % t, "la%d" % t
         dd, ds, zz, zs, rw, fw = [n + str(t) for n in ("dd", "ds", "zz", "zs", "rw", "fw")]
 
-        def rows(h):
-            q, s = sl(qt, 128 * h, 128 * h + 128), sl(st, 128 * h, 128 * h + 128)
-            mm(1 + 5 * h, 128, vw("quz"), vw("suz"), q, s)
-            mm(2 + 3 * h, 128, vw("qus"), vw("sus"), q, s)
+        def turn(h):
+            for c, n in (((0, 64),), ((64, 192), (C, C)))[h]:
+                tr(sl("mtr", c, c + n), sl("mw", c, c + n) if c < C else back("mw", 0, C))
+
+        def z(h):
+            mm(1 + 5 * h, 128, vw("quz"), vw("suz"), sl(qt, 128 * h, 128 * h + 128), sl(st, 128 * h, 128 * h + 128))
+
+        def s_(h):
+            mm(2 + 3 * h, 128, vw("qus"), vw("sus"), sl(qt, 128 * h, 128 * h + 128), sl(st, 128 * h, 128 * h + 128))
 
         for h in range(2):
             quant(sl(qt, 128 * h, 128 * h + 128), sl(st, 128 * h, 128 * h + 128), sl("tt%d" % t, 512 * h, 512 * h + 512))
             mm(7 * h, 128, vw("qu"), vw("su"), sl(qt, 128 * h, 128 * h + 128), sl(st, 128 * h, 128 * h + 128))
-            if t == 0 and h == 0:
-                cp((T.qus[:].bitcast(dt.uint32),) + vw("qus")[1:], ind(vw("qu"), sl("pku", 0, 8), dt.uint32))
-                rows(0)
+            if t > 0:
+                turn(h)
         if t == 0:
-            dma("y", T.qw[:].bitcast(dt.uint8), T.wc[:], [vw("qw")], [vw("tt0")])
+            act(vw("suz"), ind(vw("su"), sl("pku", 8, 16)), F.Copy)
+            act(vw("sus"), ind(vw("su"), sl("pku", 0, 8)), F.Copy)
+            some(rest, 4)
+            cp((T.quz[:].bitcast(dt.uint32),) + vw("quz")[1:], ind(vw("qu"), sl("pku", 8, 16), dt.uint32))
+        left = "loc" if t else "loq"
+        remote(mates[t], T["lq%d" % t][:].bitcast(dt.uint8), vw(qt), T[qt][:].bitcast(dt.uint8), "aq%d" % t, left)
+        remote(mates[t], T["ls%d" % t][:], vw(st), T[st][:], "aq%d" % t, left)
+        if t == 0:
+            g.sync.wait_ge(T.sem.loq, total["loq"])
+            waited["loq"] = total["loq"]
+            dma("y", T.qw[:].bitcast(dt.uint8), T.wc[:], [vw("qw")], [])
             dma("y", T.sw[:], T.ws[:], [vw("sw")], [])
             dma("y", T.vb[:], T.v[:], [vw("vb")], [])
-        else:
-            rows(0)
-        rows(1)
-        remote(mates[t], T["lq%d" % t][:].bitcast(dt.uint8), vw(qt), T[qt][:].bitcast(dt.uint8), "aq%d" % t)
-        remote(mates[t], T["ls%d" % t][:], vw(st), T[st][:], "aq%d" % t)
-        if t == 0:
-            iota(vw("r16"), [[0, C // 16], [1, 16]], 0)
+            for name, pat, base in [("c16", [[16, 16]], 0), ("r16", [[0, C // 16], [1024, 16]], 0),
+                                    ("c16w", [[16, C // 16], [0, 16]], 0), ("odd", [[2, C]], 1 - C),
+                                    ("i512", [[1, 512]], 0)]:
+                iota(vw(name), pat, base)
 
-        bs = "nz" if t == 0 else "base"
-        fill = []
-        if t > 0:
-            for h in (0, 128):
-                fill.append(lambda h=h: tt(sl("base", h, h + 128), sl("nz", h, h + 128), sl("mw", h, h + 128), A.add))
+        fill, forks = [], []
         for h in (0, 128):
-            for j, r in ((0, "r0"), (1, "r1")):
-                fill.append(lambda j=j, r=r, h=h: tt(sl("xc", 2 * h + j, 2 * h + 256, 2), sl(bs, h, h + 128),
-                                                     sl(r, h, h + 128), A.add))
+            for a in (h, h + 64):
+                if t > 0:
+                    fill.append(lambda a=a: tt(sl("bh", a, a + 64), sl("nz", a, a + 64), sl("mw", a, a + 64), A.add))
+            for a in (h, h + 64):
+                fill.append(lambda a=a: tt(sl("bh", C + a, C + a + 64), sl("bh", a, a + 64), sl("ab", a, a + 64), A.add))
+        for j, a, e in ((0, 0, 64), (1, 0, 96), (0, 64, 160), (0, 160, C), (1, 96, C)):
+            forks.append(lambda j=j, a=a, e=e: tt(sl("xc", 2 * a + j, 2 * e, 2), sl("bh", a, e), sl("r%d" % j, a, e), A.add))
 
-        def filler(other=0):
-            if fill:
-                fill.pop(0)()
-            else:
-                later(other)
+        def size(h):
+            act(sl("ab", 128 * h, 128 * h + 128), ps(2 + 3 * h, 0, 128), F.Abs)
 
         def relus(h):
             act(sl("r0", 128 * h, 128 * h + 128), ps(2 + 3 * h, 0, 128), F.Relu, scale=-1.0)
             act(sl("r1", 128 * h, 128 * h + 128), ps(2 + 3 * h, 0, 128), F.Relu)
 
-        if t > 0:
-            tr(sl("mtr", 0, C), vw("mw"))
-            tr(sl("mtr", C, 2 * C), back("mw", 0, C))
+        def nz(h):
+            act(sl("nz" if t else "bh", 128 * h, 128 * h + 128), ps(1 + 5 * h, 0, 128), F.Relu, scale=-1.0)
+
+        if t == 0:
+            z(0)
+            z(1)
         else:
-            tr(vw("tabt"), vw("tab"))
-        act(sl("nz", 0, 128), ps(1, 0, 128), F.Relu, scale=-1.0)
+            z(0)
+            s_(0)
+            z(1)
+            s_(1)
         tr(sl("ptr", 0, 128), ps(0, 0, 128))
         tr(sl("ptr", C + 128, 2 * C), back("ps", 0, 128))
-        if t == 0:
-            relus(0)
-            cp(sl("offs", 0, 12, 2), sl("tabt", 0, 192, 32))
         tr(sl("ptr", 128, C), ps(7, 0, 128))
         tr(sl("ptr", C, C + 128), back("ps", 512 * 7, 512 * 7 + 128))
+        nz(0)
         if t > 0:
-            cp(sl("tri", 0, 48, 3), ind(vw("mtr"), o_s))
+            size(0)
+            cp(sl("tri", 0, 96, 6), ind(vw("mtr"), o_s))
         else:
-            filler()
-        ts(sl("tri", 1, 48, 3), ind(vw("ptr"), o_z), -1.0, A.mult, 0.0, A.max)
-        act(sl("tri", 2, 48, 3), ind(vw("ptr"), o_s), F.Abs)
-        act(sl("nz", 128, C), ps(6, 0, 128), F.Relu, scale=-1.0)
+            cp((T.qus[:].bitcast(dt.uint32),) + vw("qus")[1:], ind(vw("qu"), sl("pku", 0, 8), dt.uint32))
+            s_(0)
+            s_(1)
+            nz(1)
+        ts(sl("tri", 1, 96, 6), ind(vw("ptr"), o_z), -1.0, A.mult, 0.0, A.max)
+        act(sl("tri", 3, 96, 6), ind(vw("ptr"), o_s), F.Abs)
         if t > 0:
-            relus(0)
+            nz(1)
+            size(1)
+            some(fill, 2)
+        else:
+            some(rest, 6)
+            size(0)
+            size(1)
+            some(masks, 3)
+        scan(vw("x6"), vw("tmul"), vw("tri"), 0.0, A.mult, A.add)
+        relus(0)
         relus(1)
-        filler()
-        scan(sl("hi3", 0, 48), vw("tmul"), vw("tri"), 0.0, A.mult, A.add)
-        if t > 0:
-            scan(vw("lo3"), vw("tmul"), vw("tri"), 0.0, A.mult, A.add)
-
-        def halves(name):
-            return sl(name, 0, 16), sl(name, 16, 32)
-
-        def turns(name):
-            return sl(name, 0, 32, 2), sl(name, 1, 32, 2)
-
-        def step(dst, a, b):
-            tt(dst[0], a, b, A.min)
-            tt(dst[1], a, b, A.max)
-
-        def count(i, pv=None):
-            if pv is None:
-                act(junk(512), vw("xc"), F.Sign, bias=col("npv", 2 * i + 1), accum=col("acc", i))
-            else:
-                act(junk(512), vw("xc"), F.Sign, bias=pv, scale=-1.0, accum=col("acc", i))
-
-        def why(i, n):
-            ts(sl("yv", YW * i, YW * i + n), sl("kvec", 0, n), col("acc", i), A.mult, -1.0 if i < 2 else 1.0, A.mult)
-
-        if t > 0:
-            filler()
-        else:
-            later(3)
-        step(turns("s1"), ind(vw("hi3"), o_1), sl("lo3" if t else "tri", 1, 48, 3))
-        filler()
-        step(halves("s2"), *halves("s1"))
-        filler()
         if t == 0:
-            count(6, col("hi3", 2))
-            count(7, col("hi3", 8))
-        step(halves("s3"), ind(sl("s2", 16, 32), o_3), sl("s2", 0, 16))
-        filler(1)
-        if t == 0:
-            early[2]()
-        step(halves("s4"), *turns("s3"))
-        filler(1)
-        if t == 0:
-            early[3]()
-        else:
-            count(6, col("hi3", 2))
-        step(turns("s5"), *turns("s4"))
-        later(3)
-        parts = []
-        if t > 0:
-            for j in range(4):
-                parts.append(lambda j=j: ts(sl("lt", 128 * j, 128 * j + 128), sl("xc", 128 * j, 128 * j + 128),
-                                            col("hi3", 8), A.is_lt))
-            parts.append(lambda: scan(sl("ysg", C, 2 * C), sl("lt", 0, C), sl("lt", C, 2 * C), -255.5, A.add, A.add))
-            parts.append(lambda: cp(col("acc", 7), col("ysg", 2 * C - 1)))
+            some(rest, 9)
+            some(masks, 1)
+            some(early, 1)
+        unpack(OWN, vw(qt), vw(st))
 
-        def part(n=1):
-            for _ in range(n):
-                if parts:
-                    parts.pop(0)()
+        def step(lo, hi, a, b):
+            tt(lo, a, b, A.min)
+            tt(hi, a, b, A.max)
 
-        unpack(vw(qt), vw(st))
-        step(turns("s6"), ind(sl("s5", 16, 32), o_6), sl("s5", 0, 16))
-        part()
-        later(2)
-        for l in range(2):
-            scan(sl("med", 4 * l, 4 * l + 4), sl("s6", 4 * l, 32, 8), sl("s6", 4 * l + 2, 32, 8), 0.0, A.max, A.max)
-            count(l, col("med", 4 * l + 3))
-            if l == 0:
-                step(turns("s7"), *halves("s6"))
-        ts(sl("npv", 13, 16, 2), sl("hi3", 2, 9, 6), -1.0, A.mult)
-        later(1)
-        step(turns("s8"), ind(sl("s7", 16, 32), o_8), sl("s7", 0, 16))
-        part()
-        for l in range(2):
-            o = LS * l + 1
-            tt(sl("s9", o + 1, o + 16, 2), sl("s8", 16 * l, 16 * l + 8), sl("s8", 16 * l + 8, 16 * l + 16), A.max)
-            ts(col("s9", o + 37), col("s8", 16 * l + 5), col("s8", 16 * l + 13), A.max, -1.0, A.mult)
-        for l in range(2):
-            o = LS * l + 1
-            tt(sl("s9", o, o + 16, 2), sl("s8", 16 * l, 16 * l + 8), sl("s8", 16 * l + 8, 16 * l + 16), A.min)
+        def count(i, pv, scale):
+            act(junk(512), vw("bh"), F.Sign, bias=pv, scale=scale, accum=col("acc", i))
 
-        wins = [("s9", "w9", 8), ("w9", "w5", 4), ("w5", None, 2)]
-        due = []
-        for k, (src, dst, h) in enumerate(wins):
-            for l in range(2):
-                i, o = 2 * k + l, LS * l
-                n = i + 2 if k < 2 else i + 4
-                wide = LW + h + 1
-                ends = sl(src, o + h // 2, o + h // 2 + LW + 1, LW) if k else sl("s9", o + 4, o + 39, 34)
-                scan(sl("npv", 2 * n, 2 * n + 2), sl("mul", 0, 2) if k == 0 else sl("mul", 2, 4), ends, col("acc", i),
-                     A.mult, A.max)
-                count(n)
-                why(i, wide if k < 2 else 1)
-                if due:
-                    due.pop(0)()
-                if k == 2:
-                    if l == 0:
-                        ts(vw("pin"), sl("npv", 9, 16, 2), -1.0, A.mult)
-                        part(9)
-                        later(3)
-                    else:
-                        ts(sl("yv", 6 * YW, 8 * YW, YW), sl("acc", 6, 8), -B2, A.mult)
-                    continue
-                if i == 0:
-                    for e in (0, LS):
-                        ts(sl("s9", e + LW, e + LW + 16), ind(sl("s9", e, e + LW), o_r), -1.0, A.mult)
-                else:
-                    later(2)
-                    part()
-                tt(sl("tw", o, o + wide), sl(src, o, o + wide), sl("yv", YW * i, YW * i + wide), A.max)
-                due.append(lambda o=o, wide=wide, src=src, dst=dst, h=h:
-                           tt(sl(dst, o, o + wide), sl("tw", o, o + wide), sl(src, o + h, o + h + wide), A.min))
-        later(30)
-        ts(sl("piv", 8, 10), sl("npv", 17, 20, 2), -1.0, A.mult)
-        tt(sl("w5", 2 * LS + 4, 6 * LS, LS), vw("pin"), sl("yv", 4 * YW, 8 * YW, YW), A.max)
-        tt(sl("w5", 2 * LS, 6 * LS, LS), vw("pin"), sl("yv", 4 * YW, 8 * YW, YW), A.min)
-        why(8, 1)
-        tt(vw("e4"), sl("acc", 0, 9), vw("side"), A.is_gt)
-        for b in (0, 2, 1, 3):
-            fetch(dd, b, 64.0)
-        for b in (0, 2, 1, 3):
-            mm(3 + b, C, sl("qe", 128 * b, 128 * b + 128), sl("se", 128 * b, 128 * b + 128), vw("lq%d" % t), vw("ls%d" % t))
-        red(col("fin", 0), sl("w5", 4, 6 * LS, LS), A.min)
-        red(col("fin", 1), sl("w5", 0, 6 * LS, LS), A.max)
-        y8, y9 = col("yv", 8 * YW), col("yv", 9 * YW)
+        some(fill, 2 if t else 0)
+        step(nd("y1", al, slice(0, 4, 2)), nd("y1", al, slice(1, 4, 2)), sl("x6", 1, 96, 3), sl("x6", 95, 1, -3))
+        some(fill, 2)
+        step(nd("y2", al, al, slice(0, 4, 2)), nd("y2", al, al, slice(1, 4, 2)), nd("y1", slice(0, 8), al),
+             nd("y1", slice(15, 7, -1), al))
+        some(fill, 2)
+        step(nd("y3", al, 0, al), nd("y3", al, 1, al), nd("y2", slice(0, 4), al, al), nd("y2", slice(4, 8), al, rv))
+        red(col("w3", 88), nd("y2", slice(0, 8, 2), 0, 3), A.max)
+        fetch(dd, OWN, 0)
+        count(6, col("w3", 88), -1.0)
+        some(forks, 1)
+        step(nd("y4", al, 0, al), nd("y4", al, 1, al), nd("y3", al, al, slice(0, 2)), nd("y3", al, al, slice(2, 4)))
+        some(forks, 1)
+        step(nd("y5", al, slice(0, 8, 2)), nd("y5", al, slice(1, 8, 2)), nd("y4", al, al, 0), nd("y4", al, al, 1))
+        some(forks, 1)
+
+        def kth(out, l, s, k, init):
+            scan(out, nd("y5", 4 + 2 * l + s, slice(k - 1, None, -1)), nd("y5", 2 * l + s, slice(0, k)), init,
+                 A.max, A.min)
+
+        for l in range(2):
+            kth(sl("med", 8 * l, 8 * l + 8), l, 0, 8, 0.0)
+            count(l, col("med", 8 * l + 7), -1.0)
+        tt(col("w3", 120), nd("y5", 2, slice(7, 8)), nd("y5", 6, slice(7, 8)), A.max)
+        step(nd("y6", al, 0, al), nd("y6", al, 1, al), nd("y5", slice(0, 4), al), nd("y5", slice(4, 8), rv))
+        for l in range(2):
+            kth(sl("d2", 40 + 16 * l, 160, 32), l, 0, 4, 0.0)
+            kth(sl("d2", 9 + 16 * l, 160, 32), l, 1, 5, -BIG)
+        step(nd("y7", al, 0, al), nd("y7", al, 1, al), nd("y6", al, al, slice(0, 4)), nd("y6", al, al, slice(4, 8)))
+        ts(sl("w3", 86, 128, 32), sl("w3", 88, 128, 32), -1.0, A.mult)
+        some(late, 1)
+        step(nd("y8", al, 0, al), nd("y8", al, 1, al), nd("y7", al, al, slice(0, 2)), nd("y7", al, al, slice(2, 4)))
+
+        def level2(l):
+            o = WL * l + 32
+            scan(sl("w2", o, o + 22, 2), sl("kk", 0, 11), sl("d2", 128 + 16 * l, 139 + 16 * l), col("acc", l),
+                 A.mult, A.max)
+            count(2 + l, col("w2", o + 18), 1.0)
+
+        def sort_end(l):
+            o = WL * l
+            step(sl("w2", o, o + 32, 2), sl("w2", o + 1, o + 32, 2), nd("y8", slice(8 * l, 8 * l + 8), al, 0),
+                 nd("y8", slice(8 * l, 8 * l + 8), al, 1))
+
+        def clamp1(l):
+            o = WL * l
+            tt(sl("w2", o + 64, o + 80), ind(sl("w2", o, o + 32), o_1), sl("w2", o + 32, o + 48), A.min)
+
+        def level3(l):
+            o = WL * l
+            scan(sl("w3", 32 * l, 32 * l + 26, 2), sl("kk", 16, 29), sl("w2", o + 56, o + 69), col("acc", 2 + l),
+                 A.mult, A.max)
+            count(4 + l, col("w3", 32 * l + 22), 1.0)
+
+        def clamp2(l):
+            o = WL * l
+            tt(sl("w3", D4 + l, D4 + 32, 2), ind(sl("w2", o, o + WL), o_2), sl("w3", 32 * l, 32 * l + 16), A.min)
+
+        def level4(l):
+            scan(sl("s4", l, 112, 8), sl("kk", 32, 46), sl("w3", D4 - 4 + l, D4 + 24, 2), col("acc", 4 + l),
+                 A.mult, A.max)
+            count(8 + l, col("s4", 96 + l), 1.0)
+
+        def alone(l):
+            ts(sl("s4", 2 + l, 16, 8), sl("kk", 48, 50), col("ysg", C - 1) if l else col("acc", 6), A.mult)
+
+        def under(a):
+            ts(sl("lt", a, a + C), sl("bh", a, a + C), col("w3", 120), A.is_lt)
+
+        level2(0)
+        some(late, 1)
+        sort_end(0)
+        sort_end(1)
+        level2(1)
+        clamp1(0)
+        under(0)
+        clamp1(1)
+        level3(0)
+        under(C)
+        clamp2(0)
+        some(masks, 1)
+        level3(1)
+        some(forks, 1)
+        scan(sl("ysg", 0, C), sl("lt", 0, C), sl("lt", C, 2 * C), -255.5, A.add, A.add)
+        clamp2(1)
+        level4(0)
+        some(forks, 1)
+        alone(0)
+        alone(1)
+        level4(1)
+        for b in (2, 1, 3):
+            fetch(dd, OWN, b, 64.0)
+
+        def bounds(l, hi, lo):
+            ts(sl("prep", hi, hi + 32), vw("mbig"), col("s4", 104 + l), A.max, col("yy", l), A.max)
+            ts(sl("prep", lo, lo + 32), vw("mown"), col("s4", 104 + l), A.min, col("yy", l), A.min)
+
+        def verdict(l):
+            ts(sl("prep", 32 + 32 * l, 64 + 32 * l), vw("madd"), col("acc", 8 + l), A.add, 0.0, A.is_gt)
+            ts(col("yy", l), col("acc", 8 + l), B2, A.mult)
+
+        ts(col("e4", 7), col("ysg", C - 1), 0.0, A.is_ge)
+        tt(sl("e4", 0, 7), sl("acc", 0, 7), sl("side", 0, 7), A.is_ge)
+        tt(vw("u3"), ind(vw("w3"), o_3), sl("s4", 0, 16), A.min)
         scan(vw("e3"), vw("horn"), vw("e4"), (18 - 255.5 / 16) / -8, A.mult, A.add)
-        ts(col("fin", 2), col("piv", 8), y8, A.max, col("fin", 0), A.min)
-        ts(col("fin", 3), col("piv", 8), y8, A.min, col("fin", 1), A.max)
-        why(9, 1)
-        ts(sl("prep", 160, 192), vw("madd"), col("acc", 9), A.add, 0.0, A.is_gt)
-        ts(sl("prep", 128, 160), vw("mb1"), col("e3", 8), A.mult)
-        ts(sl("prep", 0, 32), vw("mbig"), col("fin", 2), A.max)
-        ts(sl("prep", 64, 96), vw("mown"), col("fin", 3), A.min)
-        ts(sl("prep", 32, 64), vw("mbig"), col("piv", 9), A.max, y9, A.max)
-        ts(sl("prep", 96, 128), vw("mown"), col("piv", 9), A.min, y9, A.min)
+        verdict(0)
+        red(col("fin", 0), sl("u3", 0, 8), A.max)
+        red(col("fin", 1), sl("u3", 8, 16), A.max)
+        ts(sl("prep", 0, 32), vw("mb1"), col("e3", 7), A.mult)
+        bounds(0, 160, 256)
+        verdict(1)
+        ts(sl("prep", 128, 160), vw("mpm"), col("fin", 1), A.min, -1.0, A.mult)
+        ts(sl("prep", 288, 320), vw("mown"), col("fin", 0), A.min)
+        tr(sl("prt", 0, 96), sl("prep", 0, 96))
+        bounds(1, 192, 224)
         tr(sl("prt", 128, 192), sl("prep", 128, 192))
-        tr(sl("prt", 0, 128), sl("prep", 0, 128))
-        scan(vw("nsum"), vw("nmul"), sl("prt", 128, 193), 0.0, A.mult, A.add)
-        scan(vw("cut"), sl("prt", 64, 128), sl("prt", 0, 64), col("nsum", 64), A.max, A.min)
-        cut = col("cut", 63)
+        tr(sl("prt", 256, 320), sl("prep", 256, 320))
+        scan(vw("nsum"), vw("nmul"), sl("prt", 0, 97), 0.0, A.mult, A.add)
+        tr(sl("prt", 192, 256), sl("prep", 192, 256))
+        scan(vw("cut"), sl("prt", 224, 320), sl("prt", 128, 224), col("nsum", 96), A.max, A.min)
+        cut = col("cut", 95)
+        unpack(FAR, vw("lq%d" % t), vw("ls%d" % t))
 
-        for h in (0, C):
-            act(sl("ysg", h, h + C), sl("xc", h, h + C), F.Sign, bias=cut, scale=-1.0)
-        fetch(ds, 0)
-        fetch(ds, 2)
+        for a, e in ((0, 400), (400, 2 * C)):
+            act(sl("ysg", a, e), sl("xc", a, e), F.Sign, bias=cut, scale=-1.0)
+        for b in (0, 2, 1, 3):
+            fetch(ds, FAR, b)
         for h in (C, 0):
             ts(sl("lt", h, h + C), sl("xc", h, h + C), cut, A.is_lt)
         scan(back("clt", 15 + C, 15 + 2 * C), sl("ones", 0, C), back("lt", C, 2 * C), 256.0, A.mult, A.subtract)
-        for h in (0, C):
-            ts(sl("le", 16 + h, 16 + C + h), sl("ysg", h, h + C), 0.0, A.is_ge)
+        ts(sl("le", 16, 416), sl("ysg", 0, 400), 0.0, A.is_ge)
         scan(back("clt", 15, 15 + C), sl("ones", 0, C), back("lt", 0, C), col("clt", 15 + C), A.mult, A.subtract)
+        ts(sl("le", 416, 528), sl("ysg", 400, 2 * C), 0.0, A.is_ge)
+        some(late, 2)
         scan(sl("sb", 16, 416), sl("le", 16, 416), sl("clt", 16, 416), 0.0, A.add, A.min)
+        some(late, 2)
 
         def kept(a, b):
             return sl("sb", 17 + 2 * a, 16 + 2 * b, 2)
 
         def signs(first):
-            for i, m in enumerate(SM):
-                a, b = (0, 152) if m < 8 else (96, 256)
+            for m, (a, b) in SM.items():
                 if (m < 8) == first:
-                    act(junk(b - a), kept(a, b), F.Sign, bias=col("chalf", m), scale=-1.0, accum=col("iac", i))
+                    act(junk(b - a), kept(a, b), F.Sign, bias=col("chalf", m), scale=-1.0, accum=col("isc", 68 * m + 67))
 
         nv = len(VM)
 
         def below(i):
-            ts(sl("ifl", 136 * i, 136 * i + 136), kept(8 * VM[i], 8 * VM[i] + 136), col("cs", VM[i]), A.is_le)
+            ts(sl("ifl", 136 * i, 136 * i + 136), kept(8 * VM[i], 8 * VM[i] + 136), col("cs", VM[i]), A.is_le,
+               2.0, A.mult)
 
         def tally(j):
-            scan(sl("isc", 68 * j, 68 * j + 68), sl("ifl", 136 * j, 136 * j + 68),
-                 sl("ifl", 136 * j + 68, 136 * j + 136), float(8 * VM[j]), A.add, A.add)
+            m = VM[j]
+            scan(sl("isc", 68 * m, 68 * m + 68), sl("ifl", 136 * j, 136 * j + 68),
+                 sl("ifl", 136 * j + 68, 136 * j + 136), 16.0 * m - 2 * MID[m // 8], A.add, A.add)
 
+        def send(h):
+            ts(sl(au, 8 * h, 8 * h + 8), sl("isc", 544 * h + 67, 544 * h + 544, 68), 0.5, A.mult, MID[h], A.add)
+            remote(mates[t], T[la][:, 8 * h:8 * h + 8], sl(au, 8 * h, 8 * h + 8), T[au][:, 8 * h:8 * h + 8],
+                   ("al%d", "am%d")[h] % t)
+
+        def mine(h):
+            for b in range(2):
+                act(sl(zz, C * b + 128 * h, C * b + 128 * h + 128), ind(sl(dd, C * b, C * b + C), sl(au, 8 * h, 8 * h + 8)),
+                    F.Copy)
+
+        if t == 1:
+            quant(vw("qv"), vw("sv"), vw("vb"))
         signs(True)
         for i in range(2):
             below(i)
         scan(sl("sb", 416, 528), sl("le", 416, 528), sl("clt", 416, 528), col("sb", 415), A.add, A.min)
         signs(False)
-        fetch(ds, 1)
-        fetch(ds, 3)
+        if t == 0:
+            act(vw("latch"), vw("r16"), F.Relu, bias=vw("lat"), scale=-1.0)
         for i in range(2, 5):
             below(i)
         for i in range(5):
             tally(i)
         for i in range(5, nv):
             below(i)
-        ts(sl(au, 0, 3), sl("iac", 0, 3), 0.5, A.mult, 76.0, A.add)
-        cp(sl(au, 3, 8), sl("isc", 67, 68 * 5, 68))
-        remote(mates[t], T[la][:, 0:8], sl(au, 0, 8), T[au][:, 0:8], "al%d" % t)
+        send(0)
+        mine(0)
         for i in range(5, nv):
             tally(i)
-        ts(sl(au, 12, 16), sl("iac", 3, 7), 0.5, A.mult, 176.0, A.add)
-        cp(sl(au, 8, 12), sl("isc", 68 * 5 + 67, 68 * nv, 68))
-        remote(mates[t], T[la][:, 8:16], sl(au, 8, 16), T[au][:, 8:16], "am%d" % t)
+        scan(vw("gw"), vw("odd"), sl("sb", 16, 528, 2), -256.0, A.max, A.subtract)
+        send(1)
+        mine(1)
 
-        alist = vw(au)
         klist = vw("ku")
 
         def mosaic(h, b):
@@ -571,46 +625,40 @@ def rank_program(g, core, T, topo):
             q, s = sl("qz%d" % t, 128 * h, 128 * h + 128), sl("sz%d" % t, 128 * h, 128 * h + 128)
             quant(q, s, sl(zs, 512 * h, 512 * h + 512))
             for b in (0, 2, 1, 3):
-                mm((3 + 4 * h + b) % 8, 128, sl("qw", 128 * b, 128 * b + 128), sl("sw", 128 * b, 128 * b + 128), q, s)
+                mm((OWN, FAR)[h][b], 128, sl("qw", 128 * b, 128 * b + 128), sl("sw", 128 * b, 128 * b + 128), q, s)
 
         def signed(b, h):
             for j in range(2):
-                act(sl(rw, 512 * b + 256 * h + j, 512 * b + 256 * h + 256, 2), ps((3 + 4 * h + b) % 8, 0, 128),
+                act(sl(rw, 512 * b + 256 * h + j, 512 * b + 256 * h + 256, 2), ps((OWN, FAR)[h][b], 0, 128),
                     F.Copy, scale=(0.015625, -0.015625)[j])
 
         def both(b, h):
             for j in range(2):
                 tt(sl(fw, 512 * (b - 2) + 256 * h + j, 512 * (b - 2) + 256 * h + 256, 2),
-                   sl(dd, C * b + 128 * h, C * b + 128 * h + 128), ps((3 + 4 * h + b) % 8, 0, 128), (A.add, A.subtract)[j])
+                   sl(dd, C * b + 128 * h, C * b + 128 * h + 128), ps((OWN, FAR)[h][b], 0, 128), (A.add, A.subtract)[j])
 
-        if t == 0:
-            ts(vw("latch"), vw("r16"), icol, A.is_le, 1024.0, A.mult)
-        ts(vw("a2u"), alist, 2.0, A.mult)
-        ts(vw("a2"), alist, 2.0, A.mult)
-        if t == 0:
-            quant(vw("qv"), vw("sv"), vw("vb"))
-        act(sl(zz, 0, C), ind(sl(dd, 0, C), alist), F.Copy)
-        cp(vw("hw"), ind(sl("sb", 16, 528), vw("a2u")))
+        for h in (0, 128):
+            tt(sl("hw", h, h + 128), ind(vw("gw"), sl(au, h // 16, h // 16 + 8)), sl("c16w", h, h + 128), A.add)
+        for h in (0, 128):
+            scan(sl("hl", h, h + 128), sl("latch", h, h + 128), sl("hw", h, h + 128), 0.0, A.add, A.min)
 
-        for b in range(4):
+        mosaic(0, 0)
+        ts(klist, sl("hl", 15, C, 16), vw("i256"), A.add)
+        for b in range(1, 4):
             mosaic(0, b)
-        scan(vw("hl"), vw("latch"), vw("hw"), 0.0, A.add, A.min)
-        product(0)
         mosaic(1, 0)
         mosaic(1, 1)
-        tt(vw("bitn"), sl("hl", 15, C, 16), vw("cs"), A.is_le)
+        product(0)
         mosaic(1, 2)
         mosaic(1, 3)
-        act(sl(zz, C, 2 * C), ind(sl(dd, C, 2 * C), alist), F.Copy)
-        tt(vw("kn"), vw("bitn"), vw("a2"), A.add)
         product(1)
-        cp(klist, vw("kn"))
+        pick("s", vw("mw"), ind(vw("xc"), klist))
+        if last:
+            dma("y", T.ml[:], T.mw[0:128:16, 0:C], [], [vw("mw")])
         for h in range(2):
             for b in range(2):
                 signed(b, h)
                 both(b + 2, h)
-            if h == 0 and not last:
-                pick("s", vw("mw"), ind(vw("xc"), klist))
         nxt = "tt%d" % (t + 1)
 
         def state(a, e, which):
@@ -628,17 +676,15 @@ def rank_program(g, core, T, topo):
     for h in range(2):
         a, e = 128 * h, 128 * h + 128
         quant(sl(qt, a, e), sl(st, a, e), sl("tt%d" % ROUNDS, 4 * a, 4 * e))
-        mm(h, 128, vw("qv"), vw("sv"), sl(qt, a, e), sl(st, a, e))
+        mm(3 + h, 128, vw("qv"), vw("sv"), sl(qt, a, e), sl(st, a, e))
         dma("y", T.oc[:, 4 * a:4 * e], T[qt][:, a:e].bitcast(dt.uint8), [], [sl(qt, a, e)])
     act(vw("kw"), ind(sl("i512", 0, 512), vw("ku")), F.Copy)
-    act(sl("yo", 0, 128), ps(0, 0, 128), F.Copy)
-    cp(vw("mw"), ind(vw("xc"), vw("ku")))
-    cp(sl("yo", 128, C), ps(1, 0, 128))
+    cp(sl("yo", 0, 128), ps(3, 0, 128))
+    cp(sl("yo", 128, C), ps(4, 0, 128))
     dma("s", T.kl[:], T.kw[0:128:16, 0:C], [], [vw("kw")])
     dma("s", T.y[:, 0:128], T.yo[:, 0:128], [], [sl("yo", 0, 128)])
     for k in range(4):
         dma("y", T.osc[4 * k:4 * k + 4, :], T[st][32 * k:32 * k + 4, :], [], [vw(st)])
-    dma("y", T.ml[:], T.mw[0:128:16, 0:C], [], [vw("mw")])
     dma("s", T.y[:, 128:C], T.yo[:, 128:C], [], [sl("yo", 128, C)])
     for s, n in total.items():
         if waited.get(s, 0) < n:

import numpy as np
from concourse.mybir import dt, AluOpType, AxisListType, ActivationFunctionType

A = AluOpType
F = ActivationFunctionType
C = 256
ROUNDS = 3
PARTNER = [1, 2, 4]
BIG = 2.0 ** 76
B1 = 2.0 ** 78
B2 = 2.0 ** 84
HUGE = 2.0 ** 95
SM = {0: (0, 152), 1: (8, 144), 2: (0, 152), 12: (96, 256), 13: (104, 248), 14: (104, 248), 15: (96, 256)}
VM = [3, 4, 5, 6, 7, 8, 9, 10, 11]
MID = (76.0, 176.0)
WL = 80
D4 = 144
OWN = [3, 4, 0, 1]
FAR = [2, 5, 6, 7]

X4 = "float8_e4m3fn_x4"
SCRATCH = {}
POOL = {}


def _buf(name, n, dtype, where="sbuf"):
    SCRATCH[name] = (where, [128] + (n if isinstance(n, list) else [n]), dtype)


for _t in range(ROUNDS + 1):
    _buf("tt%d" % _t, 4 * C, "bfloat16")
    _buf("qt%d" % _t, C, X4)
    _buf("st%d" % _t, C, "uint8")
for _t in range(ROUNDS):
    for _n, _c, _d in [("lq", C, X4), ("ls", C, "uint8"), ("la", 16, "uint16"), ("au", 16, "uint16"),
                       ("dd", 4 * C, "bfloat16"), ("ds", 4 * C, "bfloat16"), ("zz", 2 * C, "bfloat16"),
                       ("fw", 4 * C, "bfloat16"), ("zs", 4 * C, "bfloat16"), ("qz", C, X4), ("sz", C, "uint8"),
                       ("rw", 4 * C, "float32")]:
        _buf(_n + str(_t), _c, _d)
for _d, _l in [
    ("bfloat16", [("ub", 512), ("vb", 512), ("eb", 516), ("ones", C), ("latch", C), ("junk", 2048),
                  ("lt", 512), ("le", 528), ("ysg", 512), ("clt", 528), ("sb", 528), ("odd", C),
                  ("c16w", C), ("ifl", 136 * len(VM)), ("cs", 16), ("gw", C), ("hw", C), ("hl", C)]),
    (X4, [("qu", 128), ("qv", 128), ("qus", 128), ("quz", 128), ("qw", 512), ("qe", 512)]),
    ("uint8", [("su", 128), ("sv", 128), ("sus", 128), ("suz", 128), ("sw", 512), ("se", 512)]),
    ("uint16", [("offs", 16), ("pku", 16), ("ku", 16)]),
    ("float32", [("tab", 128), ("tabt", 128), ("tab2", [3, 2, 16]), ("tabu", 96), ("c16", 16), ("chalf", 16),
                 ("r16", C), ("mbig", 32), ("mown", 32), ("mpm", 32), ("mb1", 32), ("madd", 32),
                 ("horn", 8), ("i512", 512), ("i256", 1), ("ptr", 512), ("tri", 96), ("tmul", 96), ("x6", 96),
                 ("mw", C), ("mtr", 512), ("r0", C), ("r1", C), ("nz", C), ("ab", C), ("bh", 512), ("xc", 512),
                 ("y1", [16, 4]), ("y2", [8, 2, 4]), ("y3", [8, 2, 4]), ("y4", [16, 2, 2]), ("y5", [8, 8]),
                 ("y6", [4, 2, 8]), ("y7", [8, 2, 4]), ("y8", [16, 2, 2]),
                 ("med", 16), ("w2", 2 * WL), ("d2", 160), ("w3", 176), ("s4", 112), ("kk", 56), ("lat", 1),
                 ("u3", 16), ("fin", 2), ("yy", 2), ("side", 8), ("nsum", 97), ("nmul", 97),
                 ("acc", 10), ("e3", 8), ("e4", 8), ("prep", 320), ("prt", 320), ("cut", 96),
                 ("isc", 68 * 16), ("kw", C), ("yo", C)]),
]:
    for _n, _c in _l:
        if _d == "float32" and not isinstance(_c, list) and _c <= 176:
            POOL[_n] = (sum(-(-_v[1] // 8) * 8 for _v in POOL.values()), _c)
        else:
            _buf(_n, _c, _d)
_buf("pool", sum(-(-_v[1] // 8) * 8 for _v in POOL.values()), "float32")
_buf("ps", 4096, "float32", "psum")

SEMAPHORES = ["cv", "cs", "ct", "cg", "loc", "loq"] + ["d%d" % _i for _i in range(20)] \
    + [_n + str(_i) for _n in ("aq", "al", "am") for _i in range(ROUNDS)]


def rank_program(g, core, T, topo):
    rank = T.rank_of(core)
    if rank is None:
        return
    Q = {"v": g.vector, "s": g.scalar, "t": g.tensor, "g": g, "y": g.sync}
    own = {"v": "cv", "s": "cs", "t": "ct", "g": "cg"}
    total = {}
    waited = {}
    known = {q: {} for q in Q}
    recs = {}
    ndma = [0]
    nj = [0]

    def sl(name, a=None, b=None, step=1):
        o, n = POOL[name] if name in POOL else (0, SCRATCH[name][1][1])
        a, b, step = slice(a, b, step).indices(n)
        if name in POOL:
            name = "pool"
        if name == "ps":
            m = ((1 << 512) - 1) << (512 * (a // 512))
        else:
            m = 0
            for c in range(o + a, o + b, step):
                m |= 1 << c
        return (T[name][:, o + a:(o + b if o + b >= 0 else None):step], name, m)

    def back(name, a, b):
        v = sl(name, a, b)
        return (T[name][:, b - 1:(a - 1 if a else None):-1],) + v[1:]

    def nd(name, *idx):
        shape = SCRATCH[name][1][1:]
        m = 0
        for c in np.arange(int(np.prod(shape))).reshape(shape)[idx].reshape(-1).tolist():
            m |= 1 << c
        return (T[name][(slice(None),) + idx], name, m)

    vw = sl
    al = slice(None)
    rv = slice(None, None, -1)

    def col(name, a):
        return sl(name, a, a + 1)

    def ind(win, off, cast=None):
        ap_ = win[0] if cast is None else win[0].bitcast(cast)
        return (ap_.indirect(off[0]), win[1], win[2], off)

    def need(q, reads, writes):
        deps = {}
        for kind, views in (("r", reads), ("w", writes)):
            for v in views:
                for (m, k, tok, eng) in recs.get(v[1], []):
                    if not (m & v[2]):
                        continue
                    if kind == "r" and k == "r" and (v[1] != "ps" or eng == q):
                        continue
                    if eng == q and q == "t":
                        continue
                    if tok[0] not in deps or deps[tok[0]][1] < tok[1]:
                        deps[tok[0]] = tok
        for tok in sorted(deps.values(), key=lambda tk: -len(tk[2])):
            if known[q].get(tok[0], 0) >= tok[1]:
                continue
            Q[q].wait_ge(T.sem[tok[0]], tok[1])
            waited[tok[0]] = max(waited.get(tok[0], 0), tok[1])
            known[q][tok[0]] = tok[1]
            for s, n in tok[2].items():
                if known[q].get(s, 0) < n:
                    known[q][s] = n

    def note(eng, tok, reads, writes):
        for v in writes:
            old = recs.get(v[1], [])
            recs[v[1]] = [r for r in old if r[0] & ~v[2]] + [(v[2], "w", tok, eng)]
        for v in reads:
            recs.setdefault(v[1], []).append((v[2], "r", tok, eng))

    def op(q, fn, writes, reads):
        rd = []
        for v in reads:
            if isinstance(v, tuple):
                rd.append(v)
                if len(v) == 4:
                    rd.append(v[3])
        need(q, rd, writes)
        s = own[q]
        total[s] = total.get(s, 0) + 1
        fn().then_inc(T.sem[s], 1)
        note(q, (s, total[s], dict(known[q])), rd, writes)

    def dma(q, out, in_, writes, reads):
        need(q, reads, writes)
        s = "d%d" % ndma[0]
        ndma[0] += 1
        total[s] = 16
        Q[q].dma_start(out, in_).then_inc(T.sem[s], 16)
        note("dma", (s, 16, dict(known[q])), reads, writes)

    def ap(v):
        return v[0] if isinstance(v, tuple) else v

    def tt(out, a, b, o):
        op("v", lambda: g.vector.tensor_tensor(out[0], a[0], b[0], o), [out], [a, b])

    def ts(out, a, s1, o0, s2=None, o1=None):
        if s2 is None:
            op("v", lambda: g.vector.tensor_scalar(out[0], a[0], ap(s1), None, o0), [out], [a, s1])
        else:
            op("v", lambda: g.vector.tensor_scalar(out[0], a[0], ap(s1), ap(s2), o0, o1), [out], [a, s1, s2])

    def cp(out, a):
        op("v", lambda: g.vector.tensor_copy(out[0], a[0]), [out], [a])

    def scan(out, d0, d1, init, o0, o1):
        op("v", lambda: g.vector.tensor_tensor_scan(out[0], d0[0], d1[0], ap(init), o0, o1), [out], [d0, d1, init])

    def red(out, a, o):
        op("v", lambda: g.vector.tensor_reduce(out[0], a[0], AxisListType.X, o), [out], [a])

    def tr(out, a):
        op("v", lambda: g.vector.transpose(out[0], a[0]), [out], [a])

    def ms(out, c):
        op("v", lambda: g.vector.memset(out[0], c), [out], [])

    def quant(q, s, a):
        op("v", lambda: g.vector.quantize_mx(q[0], s[0], a[0]), [q, s], [a])

    def act(out, a, f, bias=None, scale=None, accum=None):
        kw = {}
        if scale is not None:
            kw["scale"] = scale
        if bias is not None:
            kw["bias"] = ap(bias)
        if accum is not None:
            kw["accum_out"] = accum[0]
        op("s", lambda: g.scalar.activation(out[0], a[0], f, **kw), [out] + ([accum] if accum else []), [a, bias])

    def pick(q, o, i):
        if q == "s":
            act(o, i, F.Copy)
        else:
            cp(o, i)

    def mm(bank, n, lq, ls, rq, rs):
        out = sl("ps", 512 * bank, 512 * bank + n)
        op("t", lambda: g.tensor.matmul_mx(out[0], lq[0], ls[0], rq[0], rs[0], True, True), [out], [lq, ls, rq, rs])

    def iota(out, pattern, base, mult=0):
        op("g", lambda: g.iota(out[0], pattern, base, mult, allow_small_or_imprecise_dtypes=True), [out], [])

    def remote(dst, out_ap, src, src_ap, sem, left="loc"):
        need("g", [src], [])
        rid, pid, _ = topo.addr(dst)
        g.remote_dma(out_ap, src_ap, T.sem[sem], T.sem[left], pid, rid, topo.mask(core, dst))
        total[left] = total.get(left, 0) + len(topo.engines(core, dst))

    def junk(n):
        nj[0] = (nj[0] + 1) % 4
        return sl("junk", 512 * nj[0], 512 * nj[0] + n)

    def ps(bank, a, b):
        return sl("ps", 512 * bank + a, 512 * bank + b)

    def some(todo, n=1):
        for _ in range(n):
            if todo:
                todo.pop(0)()

    mates = [T.cores[rank ^ PARTNER[t]] for t in range(ROUNDS)]
    for t in range(ROUNDS):
        n = len(topo.engines(mates[t], core))
        note("far", ("aq%d" % t, 2 * n, {}), [], [vw("lq%d" % t), vw("ls%d" % t)])
        note("far", ("al%d" % t, n, {}), [], [sl("la%d" % t, 0, 8)])
        note("far", ("am%d" % t, n, {}), [], [sl("la%d" % t, 8, 16)])
        total["aq%d" % t] = 2 * n
        total["al%d" % t] = n
        total["am%d" % t] = n

    dma("s", T.ub[:], T.u[:], [vw("ub")], [])
    for h in (0, 512):
        dma("y", T.tt0[:, h:h + 512], T.x[:, h:h + 512], [sl("tt0", h, h + 512)], [])

    ms(vw("ones"), 1.0)
    ms(vw("eb"), 0.0)
    op("g", lambda: g.affine_select(T.eb[:, 3:515:4], T.ones[:, 0:128], [[-1, 128]], A.is_equal, 0.0, 0, 1),
       [sl("eb", 3, 515, 4)], [vw("ones")])
    early = [lambda b=b: quant(sl("qe", 128 * b, 128 * b + 128), sl("se", 128 * b, 128 * b + 128),
                               sl("eb", 3 - b, 515 - b)) for b in range(4)]
    for d in range(2):
        iota(nd("tab2", 0, d, al), [[-1, 4], [17, 2], [-8, 2]], 9)
    for i, a, b, step, pat, base in [
            (1, 1, 16, 4, [[2, 4]], 66), (1, 3, 16, 4, [[57, 2], [17, 2]], 0), (2, 0, 4, 1, [[32, 4]], 24),
            (2, 4, 8, 1, [[1, 4]], D4 + 24), (2, 8, 12, 1, [[32, 4]], 22), (2, 12, 16, 1, [[1, 4]], D4 + 28)]:
        iota(nd("tab2", i, al, slice(a, b, step)), [[0, 2]] + pat, base)
    for a in (64, 80):
        scan(sl("tab", a, a + 16), sl("ones", 0, 16), sl("ones", 0, 16), -1.0, A.mult, A.add)
    for name, a, b, v in [("tab", 96, 112, 0.0), ("tab", 112, 128, 1.0), ("tmul", 0, 96, -1.0), ("kk", 0, 48, -1.0)]:
        ms(sl(name, a, b), v)
    for a, v in ((0, 0.0), (16, 16.0), (32, 1.0), (48, 17.0)):
        ts(sl("tab", a, a + 16), sl("tab", 64, 80), 32.0, A.mult, v, A.add)
    for e in range(2):
        ts(sl("pku", 8 * e, 8 * e + 8), sl("tab", 64, 72), 16.0, A.mult, float(e), A.add)
    ms(vw("tri"), 0.0)
    tr(vw("tabt"), vw("tab"))
    for name, a, b, step, v in [("tmul", 0, 96, 6, 0.0), ("tmul", 1, 96, 6, 1.0)]:
        ms(sl(name, a, b, step), v)
    some(early, 1)
    cp(sl("offs", 0, 4, 2), sl("tabt", 0, 64, 32))
    some(early, 2)

    rest = []
    for name, a, b, step, v in [
            ("d2", 128, 160, 1, -HUGE), ("kk", 49, 50, 1, B2), ("w3", 0, 128, 1, BIG), ("w3", 128, D4, 1, -HUGE),
            ("w2", 32, 56, 1, BIG), ("w2", WL + 32, WL + 56, 1, BIG), ("w2", 56, 64, 1, -HUGE),
            ("w2", WL + 56, WL + 64, 1, -HUGE), ("s4", 0, 16, 1, BIG), ("horn", 0, 8, 1, 1), ("side", 0, 7, 1, 0),
            ("nmul", 96, 97, 1, -B1), ("nmul", 0, 96, 1, 1), ("prt", 96, 97, 1, 0), ("d2", 138, 160, 16, 0),
            ("kk", 0, 49, 48, -B2), ("kk", 16, 33, 16, B2), ("kk", 35, 40, 1, 1), ("kk", 41, 45, 1, 1),
            ("kk", 25, 28, 2, 1), ("horn", 2, 7, 4, -2), ("horn", 4, 5, 1, 2), ("side", 2, 6, 1, 1),
            ("clt", 527, 528, 1, C), (1, 2, 9, 6, 56), (1, 0, 1, 1, 4), (1, 6, 7, 1, 21), (1, 4, 5, 1, 76),
            (1, 10, 11, 1, 78), (1, 12, 13, 1, 52), (1, 14, 15, 1, 50), (0, 12, 13, 1, 12), (0, 14, 15, 1, 29)]:
        n = len(range(a, b, step))
        if isinstance(name, str):
            out = sl(name, a, b, step)
        else:
            out, n = nd("tab2", name, al, slice(a, b, step)), 2 * n
        rest.append(lambda out=out, n=n, v=v: act(out, sl("ones", 0, n), F.Copy, scale=float(v)))
    some(rest, 20)
    quant(vw("qu"), vw("su"), vw("ub"))
    icol = col("tabt", 64)
    hcol = col("tabt", 96)
    half = sl("tab", 96, 128)
    o_s, o_z, o_1, o_2, o_3 = [col("offs", 2 * i) for i in range(5)]
    masks = [lambda: ts(vw("mbig"), half, hcol, A.not_equal, BIG, A.mult),
             lambda: ts(vw("mown"), half, hcol, A.is_equal, BIG, A.mult),
             lambda: ts(vw("madd"), half, hcol, A.not_equal, -1024.0, A.mult),
             lambda: ts(vw("mb1"), half, hcol, A.is_equal, -1.0, A.mult),
             lambda: tt(vw("mpm"), vw("mown"), vw("mbig"), A.subtract)]
    late = [lambda: tr(vw("tabu"), nd("tab2", al, al, al)),
            lambda: cp(sl("offs", 4, 10, 2), sl("tabu", 0, 96, 32)),
            lambda: ts(vw("cs"), vw("c16"), icol, A.add),
            lambda: ts(vw("chalf"), vw("c16"), icol, A.add, 0.5, A.add),
            lambda: ts(vw("lat"), icol, 1.0, A.add, 1024.0, A.mult), lambda: ts(vw("i256"), icol, 256.0, A.add)]

    def unpack(banks, src_q, src_s):
        for b in (0, 2, 1, 3):
            mm(banks[b], C, sl("qe", 128 * b, 128 * b + 128), sl("se", 128 * b, 128 * b + 128), src_q, src_s)

    def fetch(dst, banks, b, up=None):
        act(sl(dst, C * b, C * b + C), ps(banks[b], 0, C), F.Copy, scale=up if b > 1 else None)

    for t in range(ROUNDS):
        last = t == ROUNDS - 1
        qt, st, au, la = "qt%d" % t, "st%d" % t, "au%d" % t, "la%d" % t
        dd, ds, zz, zs, rw, fw = [n + str(t) for n in ("dd", "ds", "zz", "zs", "rw", "fw")]

        def turn(h):
            for c, n in (((0, 64),), ((64, 192), (C, C)))[h]:
                tr(sl("mtr", c, c + n), sl("mw", c, c + n) if c < C else back("mw", 0, C))

        def z(h):
            mm(1 + 5 * h, 128, vw("quz"), vw("suz"), sl(qt, 128 * h, 128 * h + 128), sl(st, 128 * h, 128 * h + 128))

        def s_(h):
            mm(2 + 3 * h, 128, vw("qus"), vw("sus"), sl(qt, 128 * h, 128 * h + 128), sl(st, 128 * h, 128 * h + 128))

        for h in range(2):
            quant(sl(qt, 128 * h, 128 * h + 128), sl(st, 128 * h, 128 * h + 128), sl("tt%d" % t, 512 * h, 512 * h + 512))
            mm(7 * h, 128, vw("qu"), vw("su"), sl(qt, 128 * h, 128 * h + 128), sl(st, 128 * h, 128 * h + 128))
            if t > 0:
                turn(h)
        if t == 0:
            act(vw("suz"), ind(vw("su"), sl("pku", 8, 16)), F.Copy)
            act(vw("sus"), ind(vw("su"), sl("pku", 0, 8)), F.Copy)
            some(rest, 4)
            cp((T.quz[:].bitcast(dt.uint32),) + vw("quz")[1:], ind(vw("qu"), sl("pku", 8, 16), dt.uint32))
        left = "loc" if t else "loq"
        remote(mates[t], T["lq%d" % t][:].bitcast(dt.uint8), vw(qt), T[qt][:].bitcast(dt.uint8), "aq%d" % t, left)
        remote(mates[t], T["ls%d" % t][:], vw(st), T[st][:], "aq%d" % t, left)
        if t == 0:
            g.sync.wait_ge(T.sem.loq, total["loq"])
            waited["loq"] = total["loq"]
            dma("y", T.qw[:].bitcast(dt.uint8), T.wc[:], [vw("qw")], [])
            dma("y", T.sw[:], T.ws[:], [vw("sw")], [])
            dma("y", T.vb[:], T.v[:], [vw("vb")], [])
            for name, pat, base in [("c16", [[16, 16]], 0), ("r16", [[0, C // 16], [1024, 16]], 0),
                                    ("c16w", [[16, C // 16], [0, 16]], 0), ("odd", [[2, C]], 1 - C),
                                    ("i512", [[1, 512]], 0)]:
                iota(vw(name), pat, base)

        fill, forks = [], []
        for h in (0, 128):
            for a in (h, h + 64):
                if t > 0:
                    fill.append(lambda a=a: tt(sl("bh", a, a + 64), sl("nz", a, a + 64), sl("mw", a, a + 64), A.add))
            for a in (h, h + 64):
                fill.append(lambda a=a: tt(sl("bh", C + a, C + a + 64), sl("bh", a, a + 64), sl("ab", a, a + 64), A.add))
        for j, a, e in ((0, 0, 64), (1, 0, 96), (0, 64, 160), (0, 160, C), (1, 96, C)):
            forks.append(lambda j=j, a=a, e=e: tt(sl("xc", 2 * a + j, 2 * e, 2), sl("bh", a, e), sl("r%d" % j, a, e), A.add))

        def size(h):
            act(sl("ab", 128 * h, 128 * h + 128), ps(2 + 3 * h, 0, 128), F.Abs)

        def relus(h):
            act(sl("r0", 128 * h, 128 * h + 128), ps(2 + 3 * h, 0, 128), F.Relu, scale=-1.0)
            act(sl("r1", 128 * h, 128 * h + 128), ps(2 + 3 * h, 0, 128), F.Relu)

        def nz(h):
            act(sl("nz" if t else "bh", 128 * h, 128 * h + 128), ps(1 + 5 * h, 0, 128), F.Relu, scale=-1.0)

        if t == 0:
            z(0)
            z(1)
        else:
            z(0)
            s_(0)
            z(1)
            s_(1)
        tr(sl("ptr", 0, 128), ps(0, 0, 128))
        tr(sl("ptr", C + 128, 2 * C), back("ps", 0, 128))
        tr(sl("ptr", 128, C), ps(7, 0, 128))
        tr(sl("ptr", C, C + 128), back("ps", 512 * 7, 512 * 7 + 128))
        nz(0)
        if t > 0:
            size(0)
            cp(sl("tri", 0, 96, 6), ind(vw("mtr"), o_s))
        else:
            cp((T.qus[:].bitcast(dt.uint32),) + vw("qus")[1:], ind(vw("qu"), sl("pku", 0, 8), dt.uint32))
            s_(0)
            s_(1)
            nz(1)
        ts(sl("tri", 1, 96, 6), ind(vw("ptr"), o_z), -1.0, A.mult, 0.0, A.max)
        act(sl("tri", 3, 96, 6), ind(vw("ptr"), o_s), F.Abs)
        if t > 0:
            nz(1)
            size(1)
            some(fill, 2)
        else:
            some(rest, 6)
            size(0)
            size(1)
            some(masks, 3)
        scan(vw("x6"), vw("tmul"), vw("tri"), 0.0, A.mult, A.add)
        relus(0)
        relus(1)
        if t == 0:
            some(rest, 9)
            some(masks, 1)
            some(early, 1)
        unpack(OWN, vw(qt), vw(st))

        def step(lo, hi, a, b):
            tt(lo, a, b, A.min)
            tt(hi, a, b, A.max)

        def count(i, pv, scale):
            act(junk(512), vw("bh"), F.Sign, bias=pv, scale=scale, accum=col("acc", i))

        some(fill, 2 if t else 0)
        step(nd("y1", al, slice(0, 4, 2)), nd("y1", al, slice(1, 4, 2)), sl("x6", 1, 96, 3), sl("x6", 95, 1, -3))
        some(fill, 2)
        step(nd("y2", al, al, slice(0, 4, 2)), nd("y2", al, al, slice(1, 4, 2)), nd("y1", slice(0, 8), al),
             nd("y1", slice(15, 7, -1), al))
        some(fill, 2)
        step(nd("y3", al, 0, al), nd("y3", al, 1, al), nd("y2", slice(0, 4), al, al), nd("y2", slice(4, 8), al, rv))
        red(col("w3", 88), nd("y2", slice(0, 8, 2), 0, 3), A.max)
        fetch(dd, OWN, 0)
        count(6, col("w3", 88), -1.0)
        some(forks, 1)
        step(nd("y4", al, 0, al), nd("y4", al, 1, al), nd("y3", al, al, slice(0, 2)), nd("y3", al, al, slice(2, 4)))
        some(forks, 1)
        step(nd("y5", al, slice(0, 8, 2)), nd("y5", al, slice(1, 8, 2)), nd("y4", al, al, 0), nd("y4", al, al, 1))
        some(forks, 1)

        def kth(out, l, s, k, init):
            scan(out, nd("y5", 4 + 2 * l + s, slice(k - 1, None, -1)), nd("y5", 2 * l + s, slice(0, k)), init,
                 A.max, A.min)

        for l in range(2):
            kth(sl("med", 8 * l, 8 * l + 8), l, 0, 8, 0.0)
            count(l, col("med", 8 * l + 7), -1.0)
        tt(col("w3", 120), nd("y5", 2, slice(7, 8)), nd("y5", 6, slice(7, 8)), A.max)
        step(nd("y6", al, 0, al), nd("y6", al, 1, al), nd("y5", slice(0, 4), al), nd("y5", slice(4, 8), rv))
        for l in range(2):
            kth(sl("d2", 40 + 16 * l, 160, 32), l, 0, 4, 0.0)
            kth(sl("d2", 9 + 16 * l, 160, 32), l, 1, 5, -BIG)
        step(nd("y7", al, 0, al), nd("y7", al, 1, al), nd("y6", al, al, slice(0, 4)), nd("y6", al, al, slice(4, 8)))
        ts(sl("w3", 86, 128, 32), sl("w3", 88, 128, 32), -1.0, A.mult)
        some(late, 1)
        step(nd("y8", al, 0, al), nd("y8", al, 1, al), nd("y7", al, al, slice(0, 2)), nd("y7", al, al, slice(2, 4)))

        def level2(l):
            o = WL * l + 32
            scan(sl("w2", o, o + 22, 2), sl("kk", 0, 11), sl("d2", 128 + 16 * l, 139 + 16 * l), col("acc", l),
                 A.mult, A.max)
            count(2 + l, col("w2", o + 18), 1.0)

        def sort_end(l):
            o = WL * l
            step(sl("w2", o, o + 32, 2), sl("w2", o + 1, o + 32, 2), nd("y8", slice(8 * l, 8 * l + 8), al, 0),
                 nd("y8", slice(8 * l, 8 * l + 8), al, 1))

        def clamp1(l):
            o = WL * l
            tt(sl("w2", o + 64, o + 80), ind(sl("w2", o, o + 32), o_1), sl("w2", o + 32, o + 48), A.min)

        def level3(l):
            o = WL * l
            scan(sl("w3", 32 * l, 32 * l + 26, 2), sl("kk", 16, 29), sl("w2", o + 56, o + 69), col("acc", 2 + l),
                 A.mult, A.max)
            count(4 + l, col("w3", 32 * l + 22), 1.0)

        def clamp2(l):
            o = WL * l
            tt(sl("w3", D4 + l, D4 + 32, 2), ind(sl("w2", o, o + WL), o_2), sl("w3", 32 * l, 32 * l + 16), A.min)

        def level4(l):
            scan(sl("s4", l, 112, 8), sl("kk", 32, 46), sl("w3", D4 - 4 + l, D4 + 24, 2), col("acc", 4 + l),
                 A.mult, A.max)
            count(8 + l, col("s4", 96 + l), 1.0)

        def alone(l):
            ts(sl("s4", 2 + l, 16, 8), sl("kk", 48, 50), col("ysg", C - 1) if l else col("acc", 6), A.mult)

        def under(a):
            ts(sl("lt", a, a + C), sl("bh", a, a + C), col("w3", 120), A.is_lt)

        level2(0)
        some(late, 1)
        sort_end(0)
        sort_end(1)
        level2(1)
        clamp1(0)
        under(0)
        clamp1(1)
        level3(0)
        under(C)
        clamp2(0)
        some(masks, 1)
        level3(1)
        some(forks, 1)
        scan(sl("ysg", 0, C), sl("lt", 0, C), sl("lt", C, 2 * C), -255.5, A.add, A.add)
        clamp2(1)
        level4(0)
        some(forks, 1)
        alone(0)
        alone(1)
        level4(1)
        for b in (2, 1, 3):
            fetch(dd, OWN, b, 64.0)

        def bounds(l, hi, lo):
            ts(sl("prep", hi, hi + 32), vw("mbig"), col("s4", 104 + l), A.max, col("yy", l), A.max)
            ts(sl("prep", lo, lo + 32), vw("mown"), col("s4", 104 + l), A.min, col("yy", l), A.min)

        def verdict(l):
            ts(sl("prep", 32 + 32 * l, 64 + 32 * l), vw("madd"), col("acc", 8 + l), A.add, 0.0, A.is_gt)
            ts(col("yy", l), col("acc", 8 + l), B2, A.mult)

        ts(col("e4", 7), col("ysg", C - 1), 0.0, A.is_ge)
        tt(sl("e4", 0, 7), sl("acc", 0, 7), sl("side", 0, 7), A.is_ge)
        tt(vw("u3"), ind(vw("w3"), o_3), sl("s4", 0, 16), A.min)
        scan(vw("e3"), vw("horn"), vw("e4"), (18 - 255.5 / 16) / -8, A.mult, A.add)
        verdict(0)
        red(col("fin", 0), sl("u3", 0, 8), A.max)
        red(col("fin", 1), sl("u3", 8, 16), A.max)
        ts(sl("prep", 0, 32), vw("mb1"), col("e3", 7), A.mult)
        bounds(0, 160, 256)
        verdict(1)
        ts(sl("prep", 128, 160), vw("mpm"), col("fin", 1), A.min, -1.0, A.mult)
        ts(sl("prep", 288, 320), vw("mown"), col("fin", 0), A.min)
        tr(sl("prt", 0, 96), sl("prep", 0, 96))
        bounds(1, 192, 224)
        tr(sl("prt", 128, 192), sl("prep", 128, 192))
        tr(sl("prt", 256, 320), sl("prep", 256, 320))
        scan(vw("nsum"), vw("nmul"), sl("prt", 0, 97), 0.0, A.mult, A.add)
        tr(sl("prt", 192, 256), sl("prep", 192, 256))
        scan(vw("cut"), sl("prt", 224, 320), sl("prt", 128, 224), col("nsum", 96), A.max, A.min)
        cut = col("cut", 95)
        unpack(FAR, vw("lq%d" % t), vw("ls%d" % t))

        for a, e in ((0, 400), (400, 2 * C)):
            act(sl("ysg", a, e), sl("xc", a, e), F.Sign, bias=cut, scale=-1.0)
        for b in (0, 2, 1, 3):
            fetch(ds, FAR, b)
        for h in (C, 0):
            ts(sl("lt", h, h + C), sl("xc", h, h + C), cut, A.is_lt)
        scan(back("clt", 15 + C, 15 + 2 * C), sl("ones", 0, C), back("lt", C, 2 * C), 256.0, A.mult, A.subtract)
        ts(sl("le", 16, 416), sl("ysg", 0, 400), 0.0, A.is_ge)
        scan(back("clt", 15, 15 + C), sl("ones", 0, C), back("lt", 0, C), col("clt", 15 + C), A.mult, A.subtract)
        ts(sl("le", 416, 528), sl("ysg", 400, 2 * C), 0.0, A.is_ge)
        some(late, 2)
        scan(sl("sb", 16, 416), sl("le", 16, 416), sl("clt", 16, 416), 0.0, A.add, A.min)
        some(late, 2)

        def kept(a, b):
            return sl("sb", 17 + 2 * a, 16 + 2 * b, 2)

        def signs(first):
            for m, (a, b) in SM.items():
                if (m < 8) == first:
                    act(junk(b - a), kept(a, b), F.Sign, bias=col("chalf", m), scale=-1.0, accum=col("isc", 68 * m + 67))

        nv = len(VM)

        def below(i):
            ts(sl("ifl", 136 * i, 136 * i + 136), kept(8 * VM[i], 8 * VM[i] + 136), col("cs", VM[i]), A.is_le,
               2.0, A.mult)

        def tally(j):
            m = VM[j]
            scan(sl("isc", 68 * m, 68 * m + 68), sl("ifl", 136 * j, 136 * j + 68),
                 sl("ifl", 136 * j + 68, 136 * j + 136), 16.0 * m - 2 * MID[m // 8], A.add, A.add)

        def send(h):
            ts(sl(au, 8 * h, 8 * h + 8), sl("isc", 544 * h + 67, 544 * h + 544, 68), 0.5, A.mult, MID[h], A.add)
            remote(mates[t], T[la][:, 8 * h:8 * h + 8], sl(au, 8 * h, 8 * h + 8), T[au][:, 8 * h:8 * h + 8],
                   ("al%d", "am%d")[h] % t)

        def mine(h):
            for b in range(2):
                act(sl(zz, C * b + 128 * h, C * b + 128 * h + 128), ind(sl(dd, C * b, C * b + C), sl(au, 8 * h, 8 * h + 8)),
                    F.Copy)

        if t == 1:
            quant(vw("qv"), vw("sv"), vw("vb"))
        signs(True)
        for i in range(2):
            below(i)
        scan(sl("sb", 416, 528), sl("le", 416, 528), sl("clt", 416, 528), col("sb", 415), A.add, A.min)
        signs(False)
        if t == 0:
            act(vw("latch"), vw("r16"), F.Relu, bias=vw("lat"), scale=-1.0)
        for i in range(2, 5):
            below(i)
        for i in range(5):
            tally(i)
        for i in range(5, nv):
            below(i)
        send(0)
        mine(0)
        for i in range(5, nv):
            tally(i)
        scan(vw("gw"), vw("odd"), sl("sb", 16, 528, 2), -256.0, A.max, A.subtract)
        send(1)
        mine(1)

        klist = vw("ku")

        def mosaic(h, b):
            pick("vs"[b % 2], sl(zs, 512 * h + b, 512 * h + 512, 4),
                 ind(sl(ds, C * b, C * b + C), sl(la, 8 * h, 8 * h + 8)))

        def product(h):
            q, s = sl("qz%d" % t, 128 * h, 128 * h + 128), sl("sz%d" % t, 128 * h, 128 * h + 128)
            quant(q, s, sl(zs, 512 * h, 512 * h + 512))
            for b in (0, 2, 1, 3):
                mm((OWN, FAR)[h][b], 128, sl("qw", 128 * b, 128 * b + 128), sl("sw", 128 * b, 128 * b + 128), q, s)

        def signed(b, h):
            for j in range(2):
                act(sl(rw, 512 * b + 256 * h + j, 512 * b + 256 * h + 256, 2), ps((OWN, FAR)[h][b], 0, 128),
                    F.Copy, scale=(0.015625, -0.015625)[j])

        def both(b, h):
            for j in range(2):
                tt(sl(fw, 512 * (b - 2) + 256 * h + j, 512 * (b - 2) + 256 * h + 256, 2),
                   sl(dd, C * b + 128 * h, C * b + 128 * h + 128), ps((OWN, FAR)[h][b], 0, 128), (A.add, A.subtract)[j])

        for h in (0, 128):
            tt(sl("hw", h, h + 128), ind(vw("gw"), sl(au, h // 16, h // 16 + 8)), sl("c16w", h, h + 128), A.add)
        for h in (0, 128):
            scan(sl("hl", h, h + 128), sl("latch", h, h + 128), sl("hw", h, h + 128), 0.0, A.add, A.min)

        mosaic(0, 0)
        ts(klist, sl("hl", 15, C, 16), vw("i256"), A.add)
        for b in range(1, 4):
            mosaic(0, b)
        mosaic(1, 0)
        mosaic(1, 1)
        product(0)
        mosaic(1, 2)
        mosaic(1, 3)
        product(1)
        pick("s", vw("mw"), ind(vw("xc"), klist))
        if last:
            dma("y", T.ml[:], T.mw[0:128:16, 0:C], [], [vw("mw")])
        for h in range(2):
            for b in range(2):
                signed(b, h)
                both(b + 2, h)
        nxt = "tt%d" % (t + 1)

        def state(a, e, which):
            kl_ = sl("ku", a // 16, e // 16)
            for b in which:
                tt(sl(nxt, 4 * a + b, 4 * e, 4), ind(sl(rw, 512 * b, 512 * b + 512), kl_),
                   sl(zz, C * b + a, C * b + e), A.add)
                act(sl(nxt, 4 * a + b + 2, 4 * e, 4), ind(sl(fw, 512 * b, 512 * b + 512), kl_), F.Copy, scale=0.015625)

        state(0, C, (0,))
        state(0, 128, (1,))
        state(128, C, (1,))

    qt, st = "qt%d" % ROUNDS, "st%d" % ROUNDS
    for h in range(2):
        a, e = 128 * h, 128 * h + 128
        quant(sl(qt, a, e), sl(st, a, e), sl("tt%d" % ROUNDS, 4 * a, 4 * e))
        mm(3 + h, 128, vw("qv"), vw("sv"), sl(qt, a, e), sl(st, a, e))
        dma("y", T.oc[:, 4 * a:4 * e], T[qt][:, a:e].bitcast(dt.uint8), [], [sl(qt, a, e)])
    act(vw("kw"), ind(sl("i512", 0, 512), vw("ku")), F.Copy)
    cp(sl("yo", 0, 128), ps(3, 0, 128))
    cp(sl("yo", 128, C), ps(4, 0, 128))
    dma("s", T.kl[:], T.kw[0:128:16, 0:C], [], [vw("kw")])
    dma("s", T.y[:, 0:128], T.yo[:, 0:128], [], [sl("yo", 0, 128)])
    for k in range(4):
        dma("y", T.osc[4 * k:4 * k + 4, :], T[st][32 * k:32 * k + 4, :], [], [vw(st)])
    dma("s", T.y[:, 128:C], T.yo[:, 128:C], [], [sl("yo", 128, C)])
    for s, n in total.items():
        if waited.get(s, 0) < n:
            g.wait_ge(T.sem[s], n)
